import numpy as np
import ml_dtypes


def mxq(x, axis, fmt="e4m3"):
    dtype, down = {"e4m3": (ml_dtypes.float8_e4m3fn, 7), "e5m2": (ml_dtypes.float8_e5m2, 14)}[fmt]
    v = np.moveaxis(np.asarray(x, np.float32).astype(ml_dtypes.bfloat16).astype(np.float64), axis, -1)
    blocks = v.reshape(v.shape[:-1] + (-1, 32))
    amax = np.abs(blocks).max(-1, keepdims=True)
    byte = np.maximum(np.where(amax > 0, np.frexp(amax)[1] - 1 + 127, 0) - down, 1)
    scale = np.exp2(byte - 127.0)
    codes = (blocks / scale).astype(np.float32).astype(dtype).astype(np.float64)
    return np.moveaxis((codes * scale).reshape(v.shape), -1, axis)


WIDE = False


def mx_kscale(k):
    if not WIDE:
        return np.ones(k)
    levels = np.array([10, -10, 5, -5, 0])
    if k % 512:
        return np.exp2(np.random.permutation(np.resize(levels, k // 32))).repeat(32)
    a = np.empty((k // 512, 16))
    for p in range(k // 512):
        a[p, :8] = np.random.permutation(np.resize(levels, 8))
        for g in range(8):
            far = levels[np.abs(levels - a[p, g]) >= 10]
            a[p, g + 8] = far[np.random.randint(len(far))]
    return np.exp2(a.ravel()).repeat(32)


BF16 = ml_dtypes.bfloat16


def bf(x):
    return np.asarray(x, np.float32).astype(BF16)


def f64(x):
    return np.asarray(x).astype(np.float64)


E2M1 = np.array([0.0, 0.5, 1.0, 1.5, 2.0, 3.0, 4.0, 6.0, -0.0, -0.5, -1.0, -1.5, -2.0, -3.0, -4.0, -6.0])


def pack_weight(w, fmt):
    k, n = w.shape
    w = f64(bf(w)).reshape(k // 32, 32, n)
    amax = np.abs(w).max(1)
    if fmt == "e4m3":
        byte = np.frexp(amax)[1] - 1 + 127 - 7
    else:
        mant, ex = np.frexp(amax / 6.0)
        byte = np.where(mant > 0.5, ex, ex - 1) + 127
    byte = np.clip(np.where(amax > 0, byte, 1), 1, 254)
    scaled = (w * np.exp2(127.0 - byte)[:, None, :]).reshape(k, n).astype(np.float32)
    by_word = np.ascontiguousarray(scaled.reshape(k // 512, 128, 4, n).transpose(0, 1, 3, 2))
    if fmt == "e4m3":
        words = by_word.astype(ml_dtypes.float8_e4m3fn).view(np.uint8)
    else:
        c = by_word.astype(ml_dtypes.float4_e2m1fn).view(np.uint8) & 0xF
        words = c[..., 0::2] | (c[..., 1::2] << 4)
    return np.ascontiguousarray(words), np.ascontiguousarray(byte.astype(np.uint8).reshape(k // 512, 16, n))


def unpack_weight(words, scales, fmt):
    g, p, n, _ = words.shape
    if fmt == "e4m3":
        vals = np.ascontiguousarray(words).view(ml_dtypes.float8_e4m3fn).astype(np.float64)
    else:
        nib = np.empty((g, p, n, 4), np.uint8)
        nib[..., 0::2] = words & 0xF
        nib[..., 1::2] = words >> 4
        vals = E2M1[nib]
    vals = vals * np.repeat(np.exp2(scales.astype(np.float64) - 127.0), 8, axis=1)[..., None]
    return vals.transpose(0, 1, 3, 2).reshape(g * 512, n)
def pack4(w):
    words, scales = pack_weight(w, "e2m1")
    return words.reshape(words.shape[0], 128, -1), scales


def unpack4(words, scales):
    return unpack_weight(words.reshape(words.shape[0], 128, -1, 2), scales, "e2m1")


N, X, P, M, E, C, H = 1024, 3, 3, 512, 2, 512, 512
WIDTH2 = 0.0018


def plane_coords(pts):
    u = np.stack([pts[:, 0], pts[:, 0], pts[:, 1]], axis=0)
    v = np.stack([pts[:, 1], pts[:, 2], pts[:, 2]], axis=0)
    return u, v


def softmax_last(s):
    e = np.exp(s - np.max(s, axis=-1, keepdims=True))
    return e / np.sum(e, axis=-1, keepdims=True)


def softplus(t):
    return np.maximum(t, 0.0) + np.log(1.0 + np.exp(-np.abs(t)))


def draw0():
    sm, sc = mx_kscale(M), mx_kscale(C)
    pts = bf(np.random.uniform(0.0, 1.0, (N, X)))
    cen = bf(np.random.uniform(0.0, 1.0, (P, M, E)))
    ga = bf(np.random.standard_normal((P, M)) * sm)
    feat = bf(np.random.standard_normal((P, M, C)) * 0.106 * np.sqrt(M) / sm[None, :, None])
    gc = bf((1.0 + 0.1 * np.random.standard_normal(C)) * sc)
    w1_words, w1_scales = pack4(np.random.standard_normal((C, H)) * 2.0 / np.sqrt(C) / sc[:, None])
    b1 = bf(np.random.standard_normal(H) * 0.4)
    return {
        "pts": pts,
        "cen": cen,
        "ga": ga,
        "feat": feat,
        "gc": gc,
        "w1_words": w1_words,
        "w1_scales": w1_scales,
        "b1": b1,
    }


def core(pts, cen, ga, feat, gc, w1_words, w1_scales, b1):
    pts, cen, ga, feat, gc, b1 = f64(pts), f64(cen), f64(ga), f64(feat), f64(gc), f64(b1)
    u, v = plane_coords(pts)
    du = u[:, :, None] - cen[:, None, :, 0]
    dv = v[:, :, None] - cen[:, None, :, 1]
    d2 = du * du + dv * dv
    k = softmax_last(-d2 / WIDTH2)
    a = k * ga[:, None, :]
    f = mxq(a, 2, "e4m3") @ mxq(feat, 1, "e4m3")
    z = f[0] * f[1] * f[2] * gc[None, :]
    t = (mxq(z, 1, "e4m3") @ unpack4(w1_words, w1_scales)) + b1[None, :]
    return softplus(t)


def e4m3fn_bytes(y):
    return np.clip(np.asarray(y, np.float64), -448.0, 448.0).astype(np.float32).astype(ml_dtypes.float8_e4m3fn).view(np.uint8)


def e4m3fn_values(b):
    return np.asarray(b, np.uint8).view(ml_dtypes.float8_e4m3fn).astype(np.float64)


def setup_inputs():
    d = draw0()
    x0 = np.asarray(d['feat']).astype(np.float64)
    s = (np.max(np.abs(x0), axis=(0, 2), keepdims=True) / 448.0).astype(np.float32)
    out = {}
    for k, v in d.items():
        if k == 'feat':
            out['feat_bytes'] = e4m3fn_bytes(x0 / s.astype(np.float64))
            out['feat_scale'] = s
        else:
            out[k] = v
    return out


def reference(pts, cen, ga, feat_bytes, feat_scale, gc, w1_words, w1_scales, b1):
    return core(pts, cen, ga, e4m3fn_values(feat_bytes) * feat_scale.astype(np.float64), gc, w1_words, w1_scales, b1)

@@ -1,0 +1,361 @@
+from contextlib import ExitStack
+
+import concourse.mybir as mybir
+from concourse.masks import make_identity
+
+F32 = mybir.dt.float32
+BF16 = mybir.dt.bfloat16
+U32 = mybir.dt.uint32
+I32 = mybir.dt.int32
+U8 = mybir.dt.uint8
+FP8 = mybir.dt.float8_e4m3fn
+FP8X4 = mybir.dt.float8_e4m3fn_x4
+FP4X4 = mybir.dt.float4_e2m1fn_x4
+ACT = mybir.ActivationFunctionType
+ALU = mybir.AluOpType
+
+N, P, M, C, H = 1024, 3, 512, 512, 512
+WIDTH2 = 0.0018
+T_CLAMP = 40.0
+FLOPS = 2 * N * M * C * P + 2 * N * C * H
+COORDS = ((0, 1), (0, 2), (1, 2))
+NT = N // 128
+CH = 4
+
+
+def tile_kplanesgaussiananchordecoder_w4_kernel(
+    tc, pts, cen, ga, feat_bytes, feat_scale, gc, w1_words, w1_scales, b1, out
+):
+    nc = tc.nc
+    with ExitStack() as ctx:
+        keep = ctx.enter_context(tc.tile_pool(name="keep", bufs=1))
+        work = ctx.enter_context(tc.tile_pool(name="work", bufs=2))
+        ps_d2 = ctx.enter_context(tc.psum_pool(name="ps_d2", bufs=3))
+        ps_xt = ctx.enter_context(tc.psum_pool(name="ps_xt", bufs=2))
+        ps_f = ctx.enter_context(tc.psum_pool(name="ps_f", bufs=2))
+        ps_o = ctx.enter_context(tc.psum_pool(name="ps_o", bufs=1))
+
+        warm = keep.tile([128, 1], F32, name="warm")
+        nc.vector.memset(warm[:], 0.0)
+        warm2 = keep.tile([128, 1], F32, name="warm2")
+        nc.scalar.activation(out=warm2[:], in_=warm[:], func=ACT.Exp)
+
+        cenb = keep.tile([128, P, 8], BF16, name="cenb")
+        nc.sync.dma_start(out=cenb[:], in_=cen.rearrange("x (p t) e -> p x (t e)", t=4))
+        half = N // 2
+        ptb = []
+        for h in range(2):
+            tile_h = keep.tile([128, half * 3], BF16, name="ptb%d" % h)
+            nc.sync.dma_start(
+                out=tile_h[:],
+                in_=pts[h * half : (h + 1) * half, :].rearrange("n x -> (n x)").partition_broadcast(128),
+            )
+            ptb.append(tile_h)
+        fb = keep.tile([128, P, 4, C], U8, name="fb")
+        fs = keep.tile([128, 4], F32, name="fs")
+        nc.sync.dma_start(out=fs[:], in_=feat_scale.rearrange("o (p t) x -> p (o t x)", t=4))
+        for pl in range(P):
+            nc.sync.dma_start(out=fb[:, pl, :, :], in_=feat_bytes[pl].rearrange("(p t) c -> p t c", t=4))
+        ident = keep.tile([128, 128], F32, name="ident")
+        make_identity(nc, ident[:])
+        gab = keep.tile([128, P * M], BF16, name="gab")
+        nc.gpsimd.dma_start(out=gab[:], in_=ga.rearrange("x m -> (x m)").partition_broadcast(128))
+        gcb = keep.tile([128, 4], BF16, name="gcb")
+        nc.gpsimd.dma_start(out=gcb[:], in_=gc.rearrange("(p t) -> p t", t=4))
+        gcf = keep.tile([128, 4], F32, name="gcf")
+        nc.gpsimd.tensor_copy(out=gcf[:], in_=gcb[:])
+        bb = keep.tile([128, H], BF16, name="bb")
+        nc.gpsimd.dma_start(out=bb[:], in_=b1.partition_broadcast(128))
+        ww = keep.tile([128, 2 * H], U8, name="ww", align_bytes=64)
+        ws = keep.tile([128, H], U8, name="ws", align_bytes=64)
+        nc.vector.memset(ws[:].bitcast(I32), 0)
+        for qd in range(4):
+            nc.sync.dma_start(
+                out=ws[32 * qd : 32 * qd + 4, :].bitcast(I32), in_=w1_scales[0, 4 * qd : 4 * qd + 4, :].bitcast(I32)
+            )
+        nc.sync.dma_start(out=ww[:], in_=w1_words[0])
+
+        fw = [keep.tile([128, C], U32, name="fw%d" % pl, align_bytes=64) for pl in range(P)]
+        fsc = [keep.tile([128, C], U8, name="fsc%d" % pl, align_bytes=64) for pl in range(P)]
+
+        def feat_parts(pl):
+            wide = work.tile([128, 4, C], BF16, name="wide", bufs=1)
+            grp = work.tile([128, 4 * C], BF16, name="fgrp", bufs=1, align_bytes=64)
+
+            def widen(t):
+                nc.vector.tensor_scalar(
+                    out=wide[:, t, :], in0=fb[:, pl, t, :].bitcast(FP8), scalar1=fs[:, t : t + 1], scalar2=None, op0=ALU.mult
+                )
+
+            def inter(tc2):
+                nc.vector.tensor_copy(
+                    out=grp[:].rearrange("p (t m j) -> p t m j", t=4, j=4)[:, 2 * tc2 : 2 * tc2 + 2],
+                    in_=wide[:].rearrange("p j (m t) -> p t m j", t=4)[:, 2 * tc2 : 2 * tc2 + 2],
+                )
+
+            def quant():
+                nc.vector.quantize_mx(out=fw[pl][:].bitcast(FP8X4), scales=fsc[pl][:], in_=grp[:])
+
+            return [lambda t=t: widen(t) for t in range(4)] + [lambda: inter(0), lambda: inter(1), quant]
+
+        steps = [(c, pl) for c in range(NT // CH) for pl in range(P)]
+        jobs = [(c, pl, i) for (c, pl) in steps for i in range(CH)]
+        sq = {}
+
+        def squares(s, n0, n1, t, e):
+            c, pl = steps[s]
+            if s not in sq:
+                sq[s] = work.tile([128, 2, 4, CH * 128], F32, name="sq")
+            x = COORDS[pl][e]
+            nc.scalar.activation(
+                out=sq[s][:, e, t, n0:n1],
+                in_=ptb[c][:].rearrange("p (n x) -> p n x", x=3)[:, n0:n1, x],
+                func=ACT.Square,
+                scale=-1.0,
+                bias=cenb[:, pl, 2 * t + e : 2 * t + e + 1],
+            )
+
+        st = {}
+        sums = {}
+
+        def d2_min(k):
+            c, pl, i = jobs[k]
+            s = k // CH
+            d2 = ps_d2.tile([128, 4, 128], F32, name="d2")
+            for t in range(4):
+                for e in range(2):
+                    nc.tensor.matmul(
+                        out=d2[:, t, :],
+                        lhsT=sq[s][:, e, t, 128 * i : 128 * i + 128],
+                        rhs=ident[:],
+                        start=(e == 0),
+                        stop=(e == 1),
+                        is_transpose=True,
+                    )
+            xs = work.tile([128, M], F32, name="xs", bufs=3)
+            mn = work.tile([128, 1], F32, name="mn", bufs=4)
+            nc.vector.tensor_scalar(
+                out=xs[:].rearrange("n (p t) -> n p t", t=4),
+                in0=d2[:].rearrange("n t p -> n p t"),
+                scalar1=1.0 / WIDTH2,
+                scalar2=None,
+                op0=ALU.mult,
+                op1=ALU.min,
+                accum_out=mn[:],
+            )
+            st[k] = [xs, mn]
+
+        def expo(k):
+            xs, mn = st[k]
+            e = work.tile([128, M], F32, name="e", bufs=4)
+            if k % 2 == 0:
+                sums[k // 2] = work.tile([128, 2], F32, name="sm", bufs=3)
+            sm = sums[k // 2]
+            nc.scalar.activation(
+                out=e[:], in_=xs[:], func=ACT.Exp, scale=-1.0, bias=mn[:], accum_out=sm[:, k % 2 : k % 2 + 1]
+            )
+            st[k] = e
+
+        def norm(r):
+            pl = jobs[2 * r][1]
+            ri = work.tile([128, 2], F32, name="ri", bufs=3)
+            nc.vector.reciprocal(out=ri[:], in_=sums[r][:])
+            for j in range(2):
+                a = work.tile([128, M], BF16, name="a", bufs=4)
+                nc.vector.scalar_tensor_tensor(
+                    out=a[:],
+                    in0=st[2 * r + j][:],
+                    scalar=ri[:, j : j + 1],
+                    in1=gab[:, pl * M : (pl + 1) * M],
+                    op0=ALU.mult,
+                    op1=ALU.mult,
+                )
+                st[2 * r + j] = a
+
+        pst = {}
+
+        def xpose(r):
+            xt = ps_xt.tile([128, 2, 2, 128], F32, name="xt")
+            for j in range(2):
+                words = st[2 * r + j][:].bitcast(F32)
+                for u in range(2):
+                    nc.tensor.transpose(xt[:, j, u, :], words[:, u : M // 2 : 2], ident[:])
+            g = work.tile([128, 256 * 4], BF16, name="g", align_bytes=64)
+            copy = nc.vector.tensor_copy if r % 2 == 0 else nc.scalar.copy
+            copy(
+                out=g[:].bitcast(F32).rearrange("p (j n u) -> p j n u", j=2, u=2),
+                in_=xt[:].rearrange("p j u n -> p j n u"),
+            )
+            pst[r] = g
+
+        def quant(r):
+            g = pst[r]
+            aw = work.tile([128, 256], U32, name="aw", align_bytes=64)
+            asc = work.tile([128, 256], U8, name="asc", align_bytes=64)
+            nc.vector.quantize_mx(out=aw[:].bitcast(FP8X4), scales=asc[:], in_=g[:])
+            pst[r] = (aw, asc)
+
+        fps = {}
+
+        def mx(r, j):
+            aw, asc = pst[r]
+            k = 2 * r + j
+            pl = jobs[k][1]
+            if pl == 0:
+                f = ps_f.tile([128, 2, 256], F32, name="f")
+                for h in range(2):
+                    t = 2 * j + h
+                    nc.tensor.matmul_mx(
+                        out=f[:, h, :],
+                        lhsT=fw[pl][:, 128 * t : 128 * t + 128].bitcast(FP8X4),
+                        lhsT_scale=fsc[pl][:, 128 * t : 128 * t + 128],
+                        rhs=aw[:].bitcast(FP8X4),
+                        rhs_scale=asc[:],
+                        start=True,
+                        stop=True,
+                    )
+                fps[k] = f
+                return
+            f = ps_f.tile([128, 4, 128], F32, name="f")
+            for t in range(4):
+                nc.tensor.matmul_mx(
+                    out=f[:, t, :],
+                    lhsT=fw[pl][:, 128 * t : 128 * t + 128].bitcast(FP8X4),
+                    lhsT_scale=fsc[pl][:, 128 * t : 128 * t + 128],
+                    rhs=aw[:, 128 * j : 128 * j + 128].bitcast(FP8X4),
+                    rhs_scale=asc[:, 128 * j : 128 * j + 128],
+                    start=True,
+                    stop=True,
+                )
+            fps[k] = f
+
+        zt = {}
+        z1t = {}
+        zg = {}
+
+        def zmul(k):
+            c, pl, i = jobs[k]
+            f = fps[k]
+            n = c * CH + i
+            if pl == 0:
+                if k % 2 == 0:
+                    zt[n // 2] = work.tile([128, 4, 256], F32, name="z0", bufs=3)
+                for h in range(2):
+                    t = 2 * (k % 2) + h
+                    nc.scalar.activation(
+                        out=zt[n // 2][:, t, :], in_=f[:, h, :], func=ACT.Copy, scale=gcf[:, t : t + 1]
+                    )
+            elif pl == 1:
+                z1 = work.tile([128, 4, 128], F32, name="z1", bufs=5)
+                nc.vector.tensor_tensor(out=z1[:], in0=f[:], in1=zt[n // 2][:, :, 128 * (n % 2) : 128 * (n % 2) + 128], op=ALU.mult)
+                z1t[n] = z1
+            else:
+                if n % 2 == 0:
+                    zg[n // 2] = work.tile([128, 2, 128, 4], BF16, name="zg", align_bytes=64)
+                nc.vector.tensor_tensor(
+                    out=zg[n // 2][:, n % 2],
+                    in0=f[:].rearrange("p t n -> p n t"),
+                    in1=z1t[n][:].rearrange("p t n -> p n t"),
+                    op=ALU.mult,
+                )
+
+        zq = {}
+        tt = {}
+        ee = {}
+
+        def zquant(r2):
+            zw = work.tile([128, 256], U32, name="zw", align_bytes=64)
+            zsc = work.tile([128, 256], U8, name="zsc", align_bytes=64)
+            nc.vector.quantize_mx(
+                out=zw[:].bitcast(FP8X4), scales=zsc[:], in_=zg[r2][:].rearrange("p j n t -> p (j n t)")
+            )
+            zq[r2] = (zw, zsc)
+
+        ops = {}
+
+        def omm(n):
+            zw, zsc = zq[n // 2]
+            j = n % 2
+            o = ps_o.tile([128, H], F32, name="o")
+            nc.tensor.matmul_mx(
+                out=o[:],
+                lhsT=zw[:, 128 * j : 128 * j + 128].bitcast(FP8X4),
+                lhsT_scale=zsc[:, 128 * j : 128 * j + 128],
+                rhs=ww[:].bitcast(FP4X4),
+                rhs_scale=ws[:],
+                start=True,
+                stop=True,
+            )
+            ops[n] = o
+
+        def bias(n):
+            tn = keep.tile([128, H], F32, name="t%d" % n)
+            nc.vector.tensor_tensor(out=tn[:], in0=ops[n][:], in1=bb[:], op=ALU.add)
+            tcl = work.tile([128, H], F32, name="tcl")
+            nc.vector.tensor_scalar_min(out=tcl[:], in0=tn[:], scalar1=T_CLAMP)
+            tt[n] = (tn, tcl)
+
+        def eexp(n):
+            tn, tcl = tt[n]
+            en = keep.tile([128, H], F32, name="en%d" % n)
+            nc.scalar.activation(out=en[:], in_=tcl[:], func=ACT.Exp)
+            ee[n] = en
+
+        def final(n):
+            ln = work.tile([128, H], F32, name="ln", bufs=3)
+            nc.scalar.activation(out=ln[:], in_=ee[n][:], func=ACT.Ln, bias=1.0)
+            res = work.tile([128, H], F32, name="res", bufs=3)
+            nc.vector.tensor_tensor(out=res[:], in0=ln[:], in1=tt[n][0][:], op=ALU.max)
+            nc.sync.dma_start(out=out[128 * n : 128 * n + 128, :], in_=res[:])
+
+        vq = []
+        for f in feat_parts(0):
+            f()
+        for hh in range(2):
+            for t in range(4):
+                for e in range(2):
+                    squares(0, 256 * hh, 256 * hh + 256, t, e)
+        J = len(jobs)
+        pend = []
+        late = {}
+
+        def at(it, fn):
+            late.setdefault(it, []).append(fn)
+
+        for it in range(J + 12):
+            if it < J:
+                s = it // CH
+                d2_min(it)
+                if s + 1 < len(steps):
+                    for x in range(2):
+                        q = 2 * (it % CH) + x
+                        squares(s + 1, 0, CH * 128, q // 2, q % 2)
+            if it >= 1 and it - 1 < J:
+                expo(it - 1)
+            if it >= 3 and it % 2 == 1 and (it - 3) // 2 < J // 2:
+                norm((it - 3) // 2)
+            for fn in late.pop(it, []):
+                fn()
+            if it >= 4 and it % 2 == 0 and (it - 4) // 2 < J // 2:
+                r = (it - 4) // 2
+                xpose(r)
+                at(it + 1, lambda r=r: (quant(r), mx(r, 0)))
+                at(it + 2, lambda r=r: (mx(r, 1), zmul(2 * r)))
+                at(it + 3, lambda r=r: zmul(2 * r + 1))
+                c, pl, i = jobs[2 * r]
+                if pl == 2:
+                    n = c * CH + i
+                    at(it + 4, lambda n=n: (zquant(n // 2), omm(n)))
+                    at(it + 5, lambda n=n: (bias(n), omm(n + 1)))
+                    at(it + 6, lambda n=n: (eexp(n), bias(n + 1)))
+                    at(it + 7, lambda n=n: eexp(n + 1))
+            if it in (0, 4):
+                pend = feat_parts(1 + it // 4)
+            for x in range(2):
+                if pend:
+                    pend.pop(0)()
+        for it in sorted(late):
+            for fn in late[it]:
+                fn()
+        for n in range(NT):
+            final(n)

@@ -14,13 +14,21 @@ FP4X4 = mybir.dt.float4_e2m1fn_x4
 ACT = mybir.ActivationFunctionType
 ALU = mybir.AluOpType
 
-N, P, M, C, H = 1024, 3, 512, 512, 512
+N, PLANES, M, C, H = 1024, 3, 512, 512, 512
 WIDTH2 = 0.0018
-T_CLAMP = 40.0
-FLOPS = 2 * N * M * C * P + 2 * N * C * H
+FLOPS = 2 * N * M * C * PLANES + 2 * N * C * H
 COORDS = ((0, 1), (0, 2), (1, 2))
-NT = N // 128
-CH = 4
+TILES = N // 128
+CHUNK = 4
+JOBS = TILES * PLANES
+LAG = 4
+FILL = 3
+LEAD = 4
+HURRY = 5
+ES = 1
+SPARE = 11
+EB = 11
+TINY = 2.0**-60
 
 
 def tile_kplanesgaussiananchordecoder_w4_kernel(
@@ -31,66 +39,80 @@ def tile_kplanesgaussiananchordecoder_w4_kernel(
         keep = ctx.enter_context(tc.tile_pool(name="keep", bufs=1))
         work = ctx.enter_context(tc.tile_pool(name="work", bufs=2))
         ps_d2 = ctx.enter_context(tc.psum_pool(name="ps_d2", bufs=3))
-        ps_xt = ctx.enter_context(tc.psum_pool(name="ps_xt", bufs=2))
+        ps_xt = ctx.enter_context(tc.psum_pool(name="ps_xt", bufs=1))
         ps_f = ctx.enter_context(tc.psum_pool(name="ps_f", bufs=2))
-        ps_o = ctx.enter_context(tc.psum_pool(name="ps_o", bufs=1))
+        ps_o = ctx.enter_context(tc.psum_pool(name="ps_o", bufs=2))
+        ctx.enter_context(tc.manual_schedule())
 
-        warm = keep.tile([128, 1], F32, name="warm")
-        nc.vector.memset(warm[:], 0.0)
-        warm2 = keep.tile([128, 1], F32, name="warm2")
-        nc.scalar.activation(out=warm2[:], in_=warm[:], func=ACT.Exp)
-
-        cenb = keep.tile([128, P, 8], BF16, name="cenb")
+        pt = keep.tile([128, TILES, 3], BF16, name="pt")
+        nc.sync.dma_start(out=pt[:], in_=pts.rearrange("(p j) x -> p j x", j=TILES))
+        cenb = keep.tile([128, PLANES, 8], BF16, name="cenb")
         nc.sync.dma_start(out=cenb[:], in_=cen.rearrange("x (p t) e -> p x (t e)", t=4))
-        half = N // 2
-        ptb = []
-        for h in range(2):
-            tile_h = keep.tile([128, half * 3], BF16, name="ptb%d" % h)
-            nc.sync.dma_start(
-                out=tile_h[:],
-                in_=pts[h * half : (h + 1) * half, :].rearrange("n x -> (n x)").partition_broadcast(128),
-            )
-            ptb.append(tile_h)
-        fb = keep.tile([128, P, 4, C], U8, name="fb")
+        gat = keep.tile([128, PLANES, 4], BF16, name="gat")
+        nc.sync.dma_start(out=gat[:], in_=ga.rearrange("x (p t) -> p x t", t=4))
         fs = keep.tile([128, 4], F32, name="fs")
         nc.sync.dma_start(out=fs[:], in_=feat_scale.rearrange("o (p t) x -> p (o t x)", t=4))
-        for pl in range(P):
-            nc.sync.dma_start(out=fb[:, pl, :, :], in_=feat_bytes[pl].rearrange("(p t) c -> p t c", t=4))
-        ident = keep.tile([128, 128], F32, name="ident")
-        make_identity(nc, ident[:])
-        gab = keep.tile([128, P * M], BF16, name="gab")
-        nc.gpsimd.dma_start(out=gab[:], in_=ga.rearrange("x m -> (x m)").partition_broadcast(128))
+        fb = []
+        for pl in range(PLANES):
+            bytes_pl = keep.tile([128, 4, C], U8, name="fb%d" % pl)
+            nc.sync.dma_start(out=bytes_pl[:], in_=feat_bytes[pl].rearrange("(p t) c -> p t c", t=4))
+            fb.append(bytes_pl)
         gcb = keep.tile([128, 4], BF16, name="gcb")
-        nc.gpsimd.dma_start(out=gcb[:], in_=gc.rearrange("(p t) -> p t", t=4))
-        gcf = keep.tile([128, 4], F32, name="gcf")
-        nc.gpsimd.tensor_copy(out=gcf[:], in_=gcb[:])
-        bb = keep.tile([128, H], BF16, name="bb")
-        nc.gpsimd.dma_start(out=bb[:], in_=b1.partition_broadcast(128))
+        nc.sync.dma_start(out=gcb[:], in_=gc.rearrange("(p t) -> p t", t=4))
         ww = keep.tile([128, 2 * H], U8, name="ww", align_bytes=64)
+        nc.sync.dma_start(out=ww[:], in_=w1_words[0])
         ws = keep.tile([128, H], U8, name="ws", align_bytes=64)
         nc.vector.memset(ws[:].bitcast(I32), 0)
         for qd in range(4):
             nc.sync.dma_start(
                 out=ws[32 * qd : 32 * qd + 4, :].bitcast(I32), in_=w1_scales[0, 4 * qd : 4 * qd + 4, :].bitcast(I32)
             )
-        nc.sync.dma_start(out=ww[:], in_=w1_words[0])
+        bb = keep.tile([128, H], BF16, name="bb")
+        nc.sync.dma_start(out=bb[:], in_=b1.partition_broadcast(128))
 
-        fw = [keep.tile([128, C], U32, name="fw%d" % pl, align_bytes=64) for pl in range(P)]
-        fsc = [keep.tile([128, C], U8, name="fsc%d" % pl, align_bytes=64) for pl in range(P)]
+        identb = keep.tile([128, 128], BF16, name="identb")
+        make_identity(nc, identb[:])
+        ident = keep.tile([128, 128], F32, name="ident")
+        make_identity(nc, ident[:])
+
+        spread = {}
+
+        def spread_points(c, x, copy):
+            bank = ps_d2.tile([128, CHUNK, 128], BF16, name="bank", tag="d2")
+            for i in range(CHUNK):
+                nc.tensor.transpose(bank[:, i, :], pt[:, CHUNK * c + i, x : x + 1].to_broadcast([128, 128]), identb[:])
+            coord = keep.tile([128, CHUNK * 128], BF16, name="coord%d%d" % (c, x))
+            copy(out=coord[:], in_=bank[:].rearrange("p i n -> p (i n)"))
+            spread[c, x] = coord
+
+        gab = keep.tile([128, PLANES, M], BF16, name="gab")
+
+        def spread_gains(planes):
+            bank = ps_f.tile([128, len(planes), 2, 128], F32, name="bank", tag="f")
+            for j, pl in enumerate(planes):
+                words = gat[:, pl, :].bitcast(F32)
+                for u in range(2):
+                    nc.tensor.transpose(bank[:, j, u, :], words[:, u : u + 1].to_broadcast([128, 128]), ident[:])
+            nc.vector.tensor_copy(
+                out=gab[:, planes[0] : planes[-1] + 1, :].bitcast(F32), in_=bank[:].rearrange("p j u m -> p j (u m)")
+            )
+
+        fw = [keep.tile([128, C], U32, name="fw%d" % pl, align_bytes=64) for pl in range(PLANES)]
+        fsc = [keep.tile([128, C], U8, name="fsc%d" % pl, align_bytes=64) for pl in range(PLANES)]
 
         def feat_parts(pl):
-            wide = work.tile([128, 4, C], BF16, name="wide", bufs=1)
-            grp = work.tile([128, 4 * C], BF16, name="fgrp", bufs=1, align_bytes=64)
+            wide = work.tile([128, 4, C], BF16, name="wide")
+            grp = work.tile([128, 4 * C], BF16, name="fgrp", align_bytes=64)
 
             def widen(t):
                 nc.vector.tensor_scalar(
-                    out=wide[:, t, :], in0=fb[:, pl, t, :].bitcast(FP8), scalar1=fs[:, t : t + 1], scalar2=None, op0=ALU.mult
+                    out=wide[:, t, :], in0=fb[pl][:, t, :].bitcast(FP8), scalar1=fs[:, t : t + 1], scalar2=None, op0=ALU.mult
                 )
 
-            def inter(tc2):
+            def inter(h):
                 nc.vector.tensor_copy(
-                    out=grp[:].rearrange("p (t m j) -> p t m j", t=4, j=4)[:, 2 * tc2 : 2 * tc2 + 2],
-                    in_=wide[:].rearrange("p j (m t) -> p t m j", t=4)[:, 2 * tc2 : 2 * tc2 + 2],
+                    out=grp[:].rearrange("p (t m j) -> p t m j", t=4, j=4)[:, 2 * h : 2 * h + 2],
+                    in_=wide[:].rearrange("p j (m t) -> p t m j", t=4)[:, 2 * h : 2 * h + 2],
                 )
 
             def quant():
@@ -98,189 +120,156 @@ def tile_kplanesgaussiananchordecoder_w4_kernel(
 
             return [lambda t=t: widen(t) for t in range(4)] + [lambda: inter(0), lambda: inter(1), quant]
 
-        steps = [(c, pl) for c in range(NT // CH) for pl in range(P)]
-        jobs = [(c, pl, i) for (c, pl) in steps for i in range(CH)]
+        def job(k):
+            step, i = divmod(k, CHUNK)
+            c, pl = divmod(step, PLANES)
+            return step, pl, CHUNK * c + i
+
         sq = {}
 
-        def squares(s, n0, n1, t, e):
-            c, pl = steps[s]
-            if s not in sq:
-                sq[s] = work.tile([128, 2, 4, CH * 128], F32, name="sq")
-            x = COORDS[pl][e]
+        def square(q):
+            step, r = divmod(q, 8)
+            e, t = divmod(r, 4)
+            c, pl = divmod(step, PLANES)
+            if r == 0:
+                sq[step] = work.tile([128, 2, 4, CHUNK * 128], F32, name="sq", bufs=3)
             nc.scalar.activation(
-                out=sq[s][:, e, t, n0:n1],
-                in_=ptb[c][:].rearrange("p (n x) -> p n x", x=3)[:, n0:n1, x],
+                out=sq[step][:, e, t, :],
+                in_=spread[c, COORDS[pl][e]][:],
                 func=ACT.Square,
                 scale=-1.0,
                 bias=cenb[:, pl, 2 * t + e : 2 * t + e + 1],
             )
 
-        st = {}
-        sums = {}
+        d2s, xss, es, sums, recips, normed, grouped, quantised, fps, zs, zgs, zqs, ops, ts, sgs = ({} for i in range(15))
 
-        def d2_min(k):
-            c, pl, i = jobs[k]
-            s = k // CH
-            d2 = ps_d2.tile([128, 4, 128], F32, name="d2")
+        def distances(k):
+            step, i = divmod(k, CHUNK)
+            d2 = ps_d2.tile([128, 4, 128], F32, name="d2", tag="d2")
             for t in range(4):
                 for e in range(2):
                     nc.tensor.matmul(
                         out=d2[:, t, :],
-                        lhsT=sq[s][:, e, t, 128 * i : 128 * i + 128],
+                        lhsT=sq[step][:, e, t, 128 * i : 128 * i + 128],
                         rhs=ident[:],
                         start=(e == 0),
                         stop=(e == 1),
                         is_transpose=True,
                     )
+            d2s[k] = d2
+
+        def minimum(k):
             xs = work.tile([128, M], F32, name="xs", bufs=3)
-            mn = work.tile([128, 1], F32, name="mn", bufs=4)
+            mn = work.tile([128, 1], F32, name="mn", bufs=3)
             nc.vector.tensor_scalar(
-                out=xs[:].rearrange("n (p t) -> n p t", t=4),
-                in0=d2[:].rearrange("n t p -> n p t"),
+                out=xs[:].rearrange("n (u p e) -> n u p e", u=2, e=2),
+                in0=d2s[k][:].rearrange("n (u e) p -> n u p e", u=2),
                 scalar1=1.0 / WIDTH2,
                 scalar2=None,
                 op0=ALU.mult,
                 op1=ALU.min,
                 accum_out=mn[:],
             )
-            st[k] = [xs, mn]
+            xss[k] = (xs, mn)
 
-        def expo(k):
-            xs, mn = st[k]
-            e = work.tile([128, M], F32, name="e", bufs=4)
+        def exponential(k):
+            xs, mn = xss[k]
+            e = work.tile([128, M], F32, name="e", bufs=EB)
             if k % 2 == 0:
-                sums[k // 2] = work.tile([128, 2], F32, name="sm", bufs=3)
-            sm = sums[k // 2]
+                sums[k // 2] = work.tile([128, 2], F32, name="sm", bufs=6)
             nc.scalar.activation(
-                out=e[:], in_=xs[:], func=ACT.Exp, scale=-1.0, bias=mn[:], accum_out=sm[:, k % 2 : k % 2 + 1]
+                out=e[:], in_=xs[:], func=ACT.Exp, scale=-1.0, bias=mn[:], accum_out=sums[k // 2][:, k % 2 : k % 2 + 1]
             )
-            st[k] = e
+            es[k] = e
 
-        def norm(r):
-            pl = jobs[2 * r][1]
-            ri = work.tile([128, 2], F32, name="ri", bufs=3)
-            nc.vector.reciprocal(out=ri[:], in_=sums[r][:])
-            for j in range(2):
-                a = work.tile([128, M], BF16, name="a", bufs=4)
-                nc.vector.scalar_tensor_tensor(
-                    out=a[:],
-                    in0=st[2 * r + j][:],
-                    scalar=ri[:, j : j + 1],
-                    in1=gab[:, pl * M : (pl + 1) * M],
-                    op0=ALU.mult,
-                    op1=ALU.mult,
-                )
-                st[2 * r + j] = a
+        def reciprocal(r):
+            recips[r] = work.tile([128, 2], F32, name="ri")
+            nc.vector.reciprocal(out=recips[r][:], in_=sums[r][:])
 
-        pst = {}
+        def normalise(k):
+            pl = job(k)[1]
+            a = work.tile([128, M], BF16, name="a", bufs=4)
+            nc.vector.scalar_tensor_tensor(
+                out=a[:],
+                in0=es[k][:],
+                scalar=recips[k // 2][:, k % 2 : k % 2 + 1],
+                in1=gab[:, pl, :],
+                op0=ALU.mult,
+                op1=ALU.mult,
+            )
+            normed[k] = a
 
-        def xpose(r):
+        def turn(r):
             xt = ps_xt.tile([128, 2, 2, 128], F32, name="xt")
             for j in range(2):
-                words = st[2 * r + j][:].bitcast(F32)
+                words = normed[2 * r + j][:].bitcast(F32)
                 for u in range(2):
-                    nc.tensor.transpose(xt[:, j, u, :], words[:, u : M // 2 : 2], ident[:])
-            g = work.tile([128, 256 * 4], BF16, name="g", align_bytes=64)
-            copy = nc.vector.tensor_copy if r % 2 == 0 else nc.scalar.copy
-            copy(
-                out=g[:].bitcast(F32).rearrange("p (j n u) -> p j n u", j=2, u=2),
-                in_=xt[:].rearrange("p j u n -> p j n u"),
-            )
-            pst[r] = g
+                    nc.tensor.transpose(xt[:, j, u, :], words[:, 128 * u : 128 * u + 128], ident[:])
+            grouped[r] = xt
 
-        def quant(r):
-            g = pst[r]
+        def copy_out(r):
+            g = work.tile([128, 256 * 4], BF16, name="g", align_bytes=64)
+            nc.scalar.copy(
+                out=g[:].bitcast(F32).rearrange("p (j n u) -> p j n u", j=2, u=2),
+                in_=grouped[r][:].rearrange("p j u n -> p j n u"),
+            )
+            grouped[r] = g
+
+        def quantise_a(r):
             aw = work.tile([128, 256], U32, name="aw", align_bytes=64)
             asc = work.tile([128, 256], U8, name="asc", align_bytes=64)
-            nc.vector.quantize_mx(out=aw[:].bitcast(FP8X4), scales=asc[:], in_=g[:])
-            pst[r] = (aw, asc)
+            nc.vector.quantize_mx(out=aw[:].bitcast(FP8X4), scales=asc[:], in_=grouped[r][:])
+            quantised[r] = (aw, asc)
 
-        fps = {}
-
-        def mx(r, j):
-            aw, asc = pst[r]
-            k = 2 * r + j
-            pl = jobs[k][1]
-            if pl == 0:
-                f = ps_f.tile([128, 2, 256], F32, name="f")
-                for h in range(2):
-                    t = 2 * j + h
-                    nc.tensor.matmul_mx(
-                        out=f[:, h, :],
-                        lhsT=fw[pl][:, 128 * t : 128 * t + 128].bitcast(FP8X4),
-                        lhsT_scale=fsc[pl][:, 128 * t : 128 * t + 128],
-                        rhs=aw[:].bitcast(FP8X4),
-                        rhs_scale=asc[:],
-                        start=True,
-                        stop=True,
-                    )
-                fps[k] = f
-                return
-            f = ps_f.tile([128, 4, 128], F32, name="f")
+        def plane_product(k):
+            aw, asc = quantised[k // 2]
+            pl = job(k)[1]
+            cols = slice(128 * (k % 2), 128 * (k % 2) + 128)
+            f = ps_f.tile([128, 4, 128], F32, name="f", tag="f")
             for t in range(4):
                 nc.tensor.matmul_mx(
                     out=f[:, t, :],
                     lhsT=fw[pl][:, 128 * t : 128 * t + 128].bitcast(FP8X4),
                     lhsT_scale=fsc[pl][:, 128 * t : 128 * t + 128],
-                    rhs=aw[:, 128 * j : 128 * j + 128].bitcast(FP8X4),
-                    rhs_scale=asc[:, 128 * j : 128 * j + 128],
+                    rhs=aw[:, cols].bitcast(FP8X4),
+                    rhs_scale=asc[:, cols],
                     start=True,
                     stop=True,
                 )
             fps[k] = f
 
-        zt = {}
-        z1t = {}
-        zg = {}
-
-        def zmul(k):
-            c, pl, i = jobs[k]
-            f = fps[k]
-            n = c * CH + i
+        def multiply(k):
+            step, pl, n = job(k)
+            f = fps[k][:].rearrange("p t n -> p n t")
             if pl == 0:
-                if k % 2 == 0:
-                    zt[n // 2] = work.tile([128, 4, 256], F32, name="z0", bufs=3)
-                for h in range(2):
-                    t = 2 * (k % 2) + h
-                    nc.scalar.activation(
-                        out=zt[n // 2][:, t, :], in_=f[:, h, :], func=ACT.Copy, scale=gcf[:, t : t + 1]
-                    )
-            elif pl == 1:
-                z1 = work.tile([128, 4, 128], F32, name="z1", bufs=5)
-                nc.vector.tensor_tensor(out=z1[:], in0=f[:], in1=zt[n // 2][:, :, 128 * (n % 2) : 128 * (n % 2) + 128], op=ALU.mult)
-                z1t[n] = z1
+                other = gcb[:].unsqueeze(1).to_broadcast([128, 128, 4])
+            else:
+                other = zs[n][:]
+            if pl < PLANES - 1:
+                zs[n] = work.tile([128, 128, 4], F32, name="z", bufs=CHUNK + 1)
+                dst = zs[n][:]
             else:
                 if n % 2 == 0:
-                    zg[n // 2] = work.tile([128, 2, 128, 4], BF16, name="zg", align_bytes=64)
-                nc.vector.tensor_tensor(
-                    out=zg[n // 2][:, n % 2],
-                    in0=f[:].rearrange("p t n -> p n t"),
-                    in1=z1t[n][:].rearrange("p t n -> p n t"),
-                    op=ALU.mult,
-                )
+                    zgs[n // 2] = work.tile([128, 2, 128, 4], BF16, name="zg", align_bytes=64)
+                dst = zgs[n // 2][:, n % 2]
+            nc.vector.tensor_tensor(out=dst, in0=f, in1=other, op=ALU.mult)
 
-        zq = {}
-        tt = {}
-        ee = {}
-
-        def zquant(r2):
+        def quantise_z(r):
             zw = work.tile([128, 256], U32, name="zw", align_bytes=64)
             zsc = work.tile([128, 256], U8, name="zsc", align_bytes=64)
             nc.vector.quantize_mx(
-                out=zw[:].bitcast(FP8X4), scales=zsc[:], in_=zg[r2][:].rearrange("p j n t -> p (j n t)")
+                out=zw[:].bitcast(FP8X4), scales=zsc[:], in_=zgs[r][:].rearrange("p j n t -> p (j n t)")
             )
-            zq[r2] = (zw, zsc)
+            zqs[r] = (zw, zsc)
 
-        ops = {}
-
-        def omm(n):
-            zw, zsc = zq[n // 2]
-            j = n % 2
+        def linear(n):
+            zw, zsc = zqs[n // 2]
+            cols = slice(128 * (n % 2), 128 * (n % 2) + 128)
             o = ps_o.tile([128, H], F32, name="o")
             nc.tensor.matmul_mx(
                 out=o[:],
-                lhsT=zw[:, 128 * j : 128 * j + 128].bitcast(FP8X4),
-                lhsT_scale=zsc[:, 128 * j : 128 * j + 128],
+                lhsT=zw[:, cols].bitcast(FP8X4),
+                lhsT_scale=zsc[:, cols],
                 rhs=ww[:].bitcast(FP4X4),
                 rhs_scale=ws[:],
                 start=True,
@@ -289,73 +278,126 @@ def tile_kplanesgaussiananchordecoder_w4_kernel(
             ops[n] = o
 
         def bias(n):
-            tn = keep.tile([128, H], F32, name="t%d" % n)
-            nc.vector.tensor_tensor(out=tn[:], in0=ops[n][:], in1=bb[:], op=ALU.add)
-            tcl = work.tile([128, H], F32, name="tcl")
-            nc.vector.tensor_scalar_min(out=tcl[:], in0=tn[:], scalar1=T_CLAMP)
-            tt[n] = (tn, tcl)
+            ts[n] = keep.tile([128, H], F32, name="t%d" % n)
+            nc.vector.tensor_tensor(out=ts[n][:], in0=ops[n][:], in1=bb[:], op=ALU.add)
 
-        def eexp(n):
-            tn, tcl = tt[n]
-            en = keep.tile([128, H], F32, name="en%d" % n)
-            nc.scalar.activation(out=en[:], in_=tcl[:], func=ACT.Exp)
-            ee[n] = en
+        def sigmoid(n):
+            sgs[n] = keep.tile([128, H], F32, name="sg%d" % n)
+            nc.scalar.activation(out=sgs[n][:], in_=ts[n][:], func=ACT.Sigmoid, scale=-1.0)
 
-        def final(n):
-            ln = work.tile([128, H], F32, name="ln", bufs=3)
-            nc.scalar.activation(out=ln[:], in_=ee[n][:], func=ACT.Ln, bias=1.0)
-            res = work.tile([128, H], F32, name="res", bufs=3)
-            nc.vector.tensor_tensor(out=res[:], in0=ln[:], in1=tt[n][0][:], op=ALU.max)
-            nc.sync.dma_start(out=out[128 * n : 128 * n + 128, :], in_=res[:])
+        out_tiles = out.rearrange("(p j) h -> j p h", j=TILES)
+        lns = {}
 
-        vq = []
-        for f in feat_parts(0):
-            f()
-        for hh in range(2):
-            for t in range(4):
-                for e in range(2):
-                    squares(0, 256 * hh, 256 * hh + 256, t, e)
-        J = len(jobs)
-        pend = []
-        late = {}
+        def logarithm(n):
+            lns[n] = work.tile([128, H], F32, name="ln", bufs=4)
+            nc.scalar.activation(out=lns[n][:], in_=sgs[n][:], func=ACT.Ln, bias=TINY)
 
-        def at(it, fn):
-            late.setdefault(it, []).append(fn)
+        def finish(n):
+            res = work.tile([128, H], F32, name="res", bufs=8)
+            nc.vector.scalar_tensor_tensor(
+                out=res[:], in0=lns[n][:], scalar=-1.0, in1=ts[n][:], op0=ALU.mult, op1=ALU.max
+            )
+            nc.sync.dma_start(out=out_tiles[n], in_=res[:])
 
-        for it in range(J + 12):
-            if it < J:
-                s = it // CH
-                d2_min(it)
-                if s + 1 < len(steps):
-                    for x in range(2):
-                        q = 2 * (it % CH) + x
-                        squares(s + 1, 0, CH * 128, q // 2, q % 2)
-            if it >= 1 and it - 1 < J:
-                expo(it - 1)
-            if it >= 3 and it % 2 == 1 and (it - 3) // 2 < J // 2:
-                norm((it - 3) // 2)
-            for fn in late.pop(it, []):
-                fn()
-            if it >= 4 and it % 2 == 0 and (it - 4) // 2 < J // 2:
-                r = (it - 4) // 2
-                xpose(r)
-                at(it + 1, lambda r=r: (quant(r), mx(r, 0)))
-                at(it + 2, lambda r=r: (mx(r, 1), zmul(2 * r)))
-                at(it + 3, lambda r=r: zmul(2 * r + 1))
-                c, pl, i = jobs[2 * r]
-                if pl == 2:
-                    n = c * CH + i
-                    at(it + 4, lambda n=n: (zquant(n // 2), omm(n)))
-                    at(it + 5, lambda n=n: (bias(n), omm(n + 1)))
-                    at(it + 6, lambda n=n: (eexp(n), bias(n + 1)))
-                    at(it + 7, lambda n=n: eexp(n + 1))
-            if it in (0, 4):
-                pend = feat_parts(1 + it // 4)
-            for x in range(2):
-                if pend:
-                    pend.pop(0)()
-        for it in sorted(late):
-            for fn in late[it]:
-                fn()
-        for n in range(NT):
-            final(n)
+        spread_points(0, 0, nc.scalar.copy)
+        spread_points(0, 1, nc.scalar.copy)
+        for part in feat_parts(0):
+            part()
+        for q in range(8):
+            square(q)
+        spread_points(0, 2, nc.vector.tensor_copy)
+        spread_gains([0, 1])
+        spread_gains([2])
+        filler = feat_parts(1) + feat_parts(2)
+        squares = list(range(8, 8 * JOBS // CHUNK))
+        front = list(range(JOBS))
+
+        def next_squares(count):
+            for x in range(min(count, len(squares))):
+                square(squares.pop(0))
+
+        def next_front():
+            if front:
+                i = front.pop(0)
+                if i + 2 < JOBS:
+                    distances(i + 2)
+                minimum(i)
+                next_squares(1)
+                exponential(i)
+
+        def fill(count):
+            for x in range(min(count, len(filler))):
+                filler.pop(0)()
+
+        def last_plane(k):
+            return 0 <= k < JOBS and job(k)[1] == PLANES - 1
+
+        distances(0)
+        distances(1)
+        next_squares(LEAD)
+        for i in range(LAG):
+            next_front()
+            fill(FILL)
+            next_squares(1)
+        pairs = JOBS // 2
+        early = [lambda n=n: sigmoid(n) for n in range(CHUNK)] + [lambda n=n: logarithm(n) for n in range(CHUNK)]
+        spare = list(range(CHUNK))
+
+        def early_softplus(count):
+            if not front:
+                for x in range(min(count, len(early))):
+                    early.pop(0)()
+
+        def spare_finish():
+            if spare and spare[0] in lns and r >= SPARE:
+                finish(spare.pop(0))
+
+        for r in range(pairs + 2):
+            k = 2 * r
+            next_front()
+            if r < pairs:
+                reciprocal(r)
+            if 2 <= r:
+                multiply(k - 3)
+            if last_plane(k - 3):
+                n = job(k - 3)[2]
+            if 1 <= r <= pairs:
+                quantise_a(r - 1)
+                plane_product(k - 2)
+                plane_product(k - 1)
+            next_squares(1)
+            early_softplus(ES)
+            if r < pairs:
+                normalise(k)
+                normalise(k + 1)
+                turn(r)
+            if last_plane(k - 3):
+                quantise_z(n // 2)
+                linear(n - 1)
+                linear(n)
+                next_squares(1)
+            if r >= HURRY:
+                next_front()
+            next_front()
+            spare_finish()
+            if r < pairs:
+                copy_out(r)
+            early_softplus(ES)
+            if 1 <= r <= pairs:
+                multiply(k - 2)
+            spare_finish()
+            if last_plane(k - 3):
+                bias(n - 1)
+                bias(n)
+                next_squares(1)
+            fill(FILL)
+            if r < 3:
+                spread_points(1, r, nc.scalar.copy)
+            next_squares(1)
+        for n in range(CHUNK, TILES):
+            sigmoid(n)
+        for n in spare:
+            finish(n)
+        for n in range(CHUNK, TILES):
+            logarithm(n)
+            finish(n)

@@ -19,15 +19,22 @@ WIDTH2 = 0.0018
 FLOPS = 2 * N * M * C * PLANES + 2 * N * C * H
 COORDS = ((0, 1), (0, 2), (1, 2))
 TILES = N // 128
-CHUNK = 4
+FIRST = 6
+CHUNKS = ((0, FIRST), (FIRST, TILES - FIRST))
 JOBS = TILES * PLANES
-LAG = 4
-FILL = 3
-LEAD = 4
-HURRY = 5
-ES = 1
-SPARE = 11
-EB = 11
+FILL = 2
+HEADF = 1
+LEAD = 12
+HURRY = 20
+RATE = 17
+EB = 10
+SQB = 2
+W2 = 0
+I2 = 0
+VCO = 1
+PLAIN = ()
+AHEAD = 2
+VCO0 = 1
 TINY = 2.0**-60
 
 
@@ -77,13 +84,16 @@ def tile_kplanesgaussiananchordecoder_w4_kernel(
 
         spread = {}
 
-        def spread_points(c, x, copy):
-            bank = ps_d2.tile([128, CHUNK, 128], BF16, name="bank", tag="d2")
-            for i in range(CHUNK):
-                nc.tensor.transpose(bank[:, i, :], pt[:, CHUNK * c + i, x : x + 1].to_broadcast([128, 128]), identb[:])
-            coord = keep.tile([128, CHUNK * 128], BF16, name="coord%d%d" % (c, x))
-            copy(out=coord[:], in_=bank[:].rearrange("p i n -> p (i n)"))
-            spread[c, x] = coord
+        def spread_points(x, pool, tag):
+            bank = pool.tile([128, TILES, 128], BF16, name="bank", tag=tag)
+            for j in range(TILES):
+                nc.tensor.transpose(bank[:, j, :], pt[:, j, x : x + 1].to_broadcast([128, 128]), identb[:])
+            spread[x] = bank[:].rearrange("p j n -> p (j n)")
+
+        def keep_points(x):
+            coord = keep.tile([128, N], BF16, name="coord%d" % x)
+            nc.vector.tensor_copy(out=coord[:], in_=spread[x])
+            spread[x] = coord[:]
 
         gab = keep.tile([128, PLANES, M], BF16, name="gab")
 
@@ -93,24 +103,30 @@ def tile_kplanesgaussiananchordecoder_w4_kernel(
                 words = gat[:, pl, :].bitcast(F32)
                 for u in range(2):
                     nc.tensor.transpose(bank[:, j, u, :], words[:, u : u + 1].to_broadcast([128, 128]), ident[:])
-            nc.vector.tensor_copy(
+            return lambda: nc.vector.tensor_copy(
                 out=gab[:, planes[0] : planes[-1] + 1, :].bitcast(F32), in_=bank[:].rearrange("p j u m -> p j (u m)")
             )
 
         fw = [keep.tile([128, C], U32, name="fw%d" % pl, align_bytes=64) for pl in range(PLANES)]
         fsc = [keep.tile([128, C], U8, name="fsc%d" % pl, align_bytes=64) for pl in range(PLANES)]
 
-        def feat_parts(pl):
+        def feat_parts(pl, widen_on_scalar, inter_on_scalar):
             wide = work.tile([128, 4, C], BF16, name="wide")
             grp = work.tile([128, 4 * C], BF16, name="fgrp", align_bytes=64)
 
             def widen(t):
+                if t < widen_on_scalar:
+                    nc.scalar.activation(
+                        out=wide[:, t, :], in_=fb[pl][:, t, :].bitcast(FP8), func=ACT.Copy, scale=fs[:, t : t + 1]
+                    )
+                    return
                 nc.vector.tensor_scalar(
                     out=wide[:, t, :], in0=fb[pl][:, t, :].bitcast(FP8), scalar1=fs[:, t : t + 1], scalar2=None, op0=ALU.mult
                 )
 
             def inter(h):
-                nc.vector.tensor_copy(
+                copy = nc.scalar.copy if h < inter_on_scalar else nc.vector.tensor_copy
+                copy(
                     out=grp[:].rearrange("p (t m j) -> p t m j", t=4, j=4)[:, 2 * h : 2 * h + 2],
                     in_=wide[:].rearrange("p j (m t) -> p t m j", t=4)[:, 2 * h : 2 * h + 2],
                 )
@@ -120,22 +136,24 @@ def tile_kplanesgaussiananchordecoder_w4_kernel(
 
             return [lambda t=t: widen(t) for t in range(4)] + [lambda: inter(0), lambda: inter(1), quant]
 
+        steps = [(first, count, pl) for first, count in CHUNKS for pl in range(PLANES)]
+        jobs = [(s, pl, first + i) for s, (first, count, pl) in enumerate(steps) for i in range(count)]
+
         def job(k):
-            step, i = divmod(k, CHUNK)
-            c, pl = divmod(step, PLANES)
-            return step, pl, CHUNK * c + i
+            return jobs[k]
 
         sq = {}
 
-        def square(q):
+        def square(q, lo=0, hi=None):
             step, r = divmod(q, 8)
             e, t = divmod(r, 4)
-            c, pl = divmod(step, PLANES)
-            if r == 0:
-                sq[step] = work.tile([128, 2, 4, CHUNK * 128], F32, name="sq", bufs=3)
+            first, count, pl = steps[step]
+            hi = count if hi is None else hi
+            if r == 0 and lo == 0:
+                sq[step] = work.tile([128, 2, 4, count * 128], F32, name="sq", tag="sq%d" % count, bufs=SQB if count == FIRST else PLANES)
             nc.scalar.activation(
-                out=sq[step][:, e, t, :],
-                in_=spread[c, COORDS[pl][e]][:],
+                out=sq[step][:, e, t, 128 * lo : 128 * hi],
+                in_=spread[COORDS[pl][e]][:, 128 * (first + lo) : 128 * (first + hi)],
                 func=ACT.Square,
                 scale=-1.0,
                 bias=cenb[:, pl, 2 * t + e : 2 * t + e + 1],
@@ -144,7 +162,8 @@ def tile_kplanesgaussiananchordecoder_w4_kernel(
         d2s, xss, es, sums, recips, normed, grouped, quantised, fps, zs, zgs, zqs, ops, ts, sgs = ({} for i in range(15))
 
         def distances(k):
-            step, i = divmod(k, CHUNK)
+            step, pl, n = jobs[k]
+            i = n - steps[step][0]
             d2 = ps_d2.tile([128, 4, 128], F32, name="d2", tag="d2")
             for t in range(4):
                 for e in range(2):
@@ -154,7 +173,7 @@ def tile_kplanesgaussiananchordecoder_w4_kernel(
                         rhs=ident[:],
                         start=(e == 0),
                         stop=(e == 1),
-                        is_transpose=True,
+                        is_transpose=not (e == 0 and t in PLAIN),
                     )
             d2s[k] = d2
 
@@ -200,16 +219,16 @@ def tile_kplanesgaussiananchordecoder_w4_kernel(
             normed[k] = a
 
         def turn(r):
-            xt = ps_xt.tile([128, 2, 2, 128], F32, name="xt")
+            xt = ps_xt.tile([128, 2, 2, 128], F32, name="xt", tag="xt")
             for j in range(2):
                 words = normed[2 * r + j][:].bitcast(F32)
                 for u in range(2):
                     nc.tensor.transpose(xt[:, j, u, :], words[:, 128 * u : 128 * u + 128], ident[:])
             grouped[r] = xt
 
-        def copy_out(r):
+        def copy_out(r, copy):
             g = work.tile([128, 256 * 4], BF16, name="g", align_bytes=64)
-            nc.scalar.copy(
+            copy(
                 out=g[:].bitcast(F32).rearrange("p (j n u) -> p j n u", j=2, u=2),
                 in_=grouped[r][:].rearrange("p j u n -> p j n u"),
             )
@@ -246,7 +265,7 @@ def tile_kplanesgaussiananchordecoder_w4_kernel(
             else:
                 other = zs[n][:]
             if pl < PLANES - 1:
-                zs[n] = work.tile([128, 128, 4], F32, name="z", bufs=CHUNK + 1)
+                zs[n] = work.tile([128, 128, 4], F32, name="z", bufs=FIRST + 1)
                 dst = zs[n][:]
             else:
                 if n % 2 == 0:
@@ -265,7 +284,7 @@ def tile_kplanesgaussiananchordecoder_w4_kernel(
         def linear(n):
             zw, zsc = zqs[n // 2]
             cols = slice(128 * (n % 2), 128 * (n % 2) + 128)
-            o = ps_o.tile([128, H], F32, name="o")
+            o = ps_o.tile([128, H], F32, name="o", tag="o")
             nc.tensor.matmul_mx(
                 out=o[:],
                 lhsT=zw[:, cols].bitcast(FP8X4),
@@ -277,52 +296,63 @@ def tile_kplanesgaussiananchordecoder_w4_kernel(
             )
             ops[n] = o
 
+        tall = keep.tile([128, TILES, H], F32, name="tall")
+        lall = keep.tile([128, TILES, H], F32, name="lall")
+
         def bias(n):
-            ts[n] = keep.tile([128, H], F32, name="t%d" % n)
-            nc.vector.tensor_tensor(out=ts[n][:], in0=ops[n][:], in1=bb[:], op=ALU.add)
+            nc.vector.tensor_tensor(out=tall[:, n, :], in0=ops[n][:], in1=bb[:], op=ALU.add)
 
-        def sigmoid(n):
-            sgs[n] = keep.tile([128, H], F32, name="sg%d" % n)
-            nc.scalar.activation(out=sgs[n][:], in_=ts[n][:], func=ACT.Sigmoid, scale=-1.0)
+        def sigmoid(n, count):
+            nc.scalar.activation(out=lall[:, n : n + count, :], in_=tall[:, n : n + count, :], func=ACT.Sigmoid, scale=-1.0)
 
-        out_tiles = out.rearrange("(p j) h -> j p h", j=TILES)
-        lns = {}
+        out_tiles = out.rearrange("(p j) h -> p j h", j=TILES)
 
-        def logarithm(n):
-            lns[n] = work.tile([128, H], F32, name="ln", bufs=4)
-            nc.scalar.activation(out=lns[n][:], in_=sgs[n][:], func=ACT.Ln, bias=TINY)
+        def logarithm(n, count):
+            nc.scalar.activation(out=lall[:, n : n + count, :], in_=lall[:, n : n + count, :], func=ACT.Ln, bias=TINY)
 
-        def finish(n):
-            res = work.tile([128, H], F32, name="res", bufs=8)
+        def finish(n, count):
             nc.vector.scalar_tensor_tensor(
-                out=res[:], in0=lns[n][:], scalar=-1.0, in1=ts[n][:], op0=ALU.mult, op1=ALU.max
+                out=tall[:, n : n + count, :], in0=lall[:, n : n + count, :], scalar=-1.0, in1=tall[:, n : n + count, :], op0=ALU.mult, op1=ALU.max
             )
-            nc.sync.dma_start(out=out_tiles[n], in_=res[:])
+            nc.sync.dma_start(out=out_tiles[:, n : n + count, :], in_=tall[:, n : n + count, :])
 
-        spread_points(0, 0, nc.scalar.copy)
-        spread_points(0, 1, nc.scalar.copy)
-        for part in feat_parts(0):
+        spread_points(0, ps_o, "o")
+        spread_points(1, ps_o, "o")
+        spread_points(2, ps_xt, "xt")
+        keep_gains = [spread_gains([0, 1]), spread_gains([2])]
+        first, second, third = feat_parts(0, 0, 0), feat_parts(1, 0, 0), feat_parts(2, W2, I2)
+        for part in first[:4] + second[:4] + first[4:6]:
             part()
         for q in range(8):
             square(q)
-        spread_points(0, 2, nc.vector.tensor_copy)
-        spread_gains([0, 1])
-        spread_gains([2])
-        filler = feat_parts(1) + feat_parts(2)
-        squares = list(range(8, 8 * JOBS // CHUNK))
+        keep_points(2)
+        first[6]()
+        keep_points(0)
+        for part in second[4:6] + keep_gains[:1]:
+            part()
+        filler = second[6:] + [lambda: keep_points(1)] + third[:4] + keep_gains[1:] + third[4:]
+        for x in range(HEADF):
+            filler.pop(0)()
+        squares = list(range(8, 8 * len(steps)))
         front = list(range(JOBS))
+        waiting = []
+        budget = [0.0]
 
-        def next_squares(count):
-            for x in range(min(count, len(squares))):
-                square(squares.pop(0))
+        def next_squares(columns):
+            budget[0] = budget[0] + columns
+            while squares and budget[0] > 0:
+                q = squares.pop(0)
+                budget[0] = budget[0] - steps[q // 8][1] - 0.5
+                square(q)
 
-        def next_front():
+        def next_minimum():
             if front:
                 i = front.pop(0)
-                if i + 2 < JOBS:
-                    distances(i + 2)
+                if i + AHEAD < JOBS:
+                    while squares and squares[0] // 8 <= job(i + AHEAD)[0]:
+                        next_squares(1)
+                    distances(i + AHEAD)
                 minimum(i)
-                next_squares(1)
                 exponential(i)
 
         def fill(count):
@@ -332,72 +362,91 @@ def tile_kplanesgaussiananchordecoder_w4_kernel(
         def last_plane(k):
             return 0 <= k < JOBS and job(k)[1] == PLANES - 1
 
-        distances(0)
-        distances(1)
+        for i in range(AHEAD):
+            distances(i)
         next_squares(LEAD)
-        for i in range(LAG):
-            next_front()
+        wide = PLANES * FIRST // 2
+        for r in range(wide + 3):
+            next_minimum()
+            if 1 <= r <= wide:
+                reciprocal(r - 1)
+            if 2 <= r <= wide + 1:
+                copy_out(r - 2, nc.scalar.copy if r - 2 >= VCO0 else nc.vector.tensor_copy)
+            if 3 <= r:
+                multiply(2 * r - 6)
+            if last_plane(2 * r - 8):
+                bias(job(2 * r - 8)[2])
             fill(FILL)
-            next_squares(1)
-        pairs = JOBS // 2
-        early = [lambda n=n: sigmoid(n) for n in range(CHUNK)] + [lambda n=n: logarithm(n) for n in range(CHUNK)]
-        spare = list(range(CHUNK))
-
-        def early_softplus(count):
-            if not front:
-                for x in range(min(count, len(early))):
-                    early.pop(0)()
-
-        def spare_finish():
-            if spare and spare[0] in lns and r >= SPARE:
-                finish(spare.pop(0))
-
-        for r in range(pairs + 2):
-            k = 2 * r
-            next_front()
-            if r < pairs:
-                reciprocal(r)
-            if 2 <= r:
-                multiply(k - 3)
-            if last_plane(k - 3):
-                n = job(k - 3)[2]
-            if 1 <= r <= pairs:
-                quantise_a(r - 1)
-                plane_product(k - 2)
-                plane_product(k - 1)
-            next_squares(1)
-            early_softplus(ES)
-            if r < pairs:
-                normalise(k)
-                normalise(k + 1)
-                turn(r)
-            if last_plane(k - 3):
+            next_minimum()
+            if 3 <= r:
+                multiply(2 * r - 5)
+            if last_plane(2 * r - 7):
+                bias(job(2 * r - 7)[2])
+            fill(FILL)
+            if 2 <= r <= wide + 1:
+                quantise_a(r - 2)
+                plane_product(2 * r - 4)
+                plane_product(2 * r - 3)
+            if r >= HURRY:
+                next_minimum()
+            if last_plane(2 * r - 5):
+                n = job(2 * r - 5)[2]
                 quantise_z(n // 2)
                 linear(n - 1)
                 linear(n)
-                next_squares(1)
-            if r >= HURRY:
-                next_front()
-            next_front()
-            spare_finish()
-            if r < pairs:
-                copy_out(r)
-            early_softplus(ES)
-            if 1 <= r <= pairs:
-                multiply(k - 2)
-            spare_finish()
-            if last_plane(k - 3):
-                bias(n - 1)
-                bias(n)
-                next_squares(1)
-            fill(FILL)
-            if r < 3:
-                spread_points(1, r, nc.scalar.copy)
-            next_squares(1)
-        for n in range(CHUNK, TILES):
-            sigmoid(n)
-        for n in spare:
-            finish(n)
-        for n in range(CHUNK, TILES):
-            logarithm(n)
-            finish(n)
+            if 1 <= r <= wide:
+                normalise(2 * r - 2)
+                normalise(2 * r - 1)
+                turn(r - 1)
+            next_squares(RATE)
+
+        def weights(r):
+            normalise(2 * r)
+            normalise(2 * r + 1)
+            turn(r)
+
+        def products(r):
+            quantise_a(r)
+            plane_product(2 * r)
+            plane_product(2 * r + 1)
+
+        def multiplies(r):
+            multiply(2 * r)
+            multiply(2 * r + 1)
+
+        reciprocal(wide)
+        reciprocal(wide + 1)
+        sigmoid(0, 2)
+        weights(wide)
+        bias(FIRST - 2)
+        bias(FIRST - 1)
+        copy_out(wide, nc.scalar.copy)
+        sigmoid(2, 2)
+        reciprocal(wide + 2)
+        weights(wide + 1)
+        products(wide)
+        copy_out(wide + 1, nc.scalar.copy)
+        sigmoid(4, 2)
+        weights(wide + 2)
+        multiplies(wide)
+        products(wide + 1)
+        logarithm(0, 2)
+        copy_out(wide + 2, nc.vector.tensor_copy if VCO else nc.scalar.copy)
+        logarithm(2, 2)
+        multiplies(wide + 1)
+        logarithm(4, 2)
+        products(wide + 2)
+        finish(0, 2)
+        multiplies(wide + 2)
+        finish(2, 1)
+        quantise_z(FIRST // 2)
+        linear(FIRST)
+        linear(FIRST + 1)
+        finish(3, 1)
+        for n in range(FIRST, TILES):
+            bias(n)
+            sigmoid(n, 1)
+        finish(4, 2)
+        for n in range(FIRST, TILES):
+            logarithm(n, 1)
+            finish(n, 1)

@@ -32,7 +32,7 @@ SQB = 2
 W2 = 0
 I2 = 0
 VCO = 1
-PLAIN = ()
+PLAIN = (0, 3)
 AHEAD = 2
 VCO0 = 1
 TINY = 2.0**-60

@@ -20,22 +20,27 @@ FLOPS = 2 * N * M * C * PLANES + 2 * N * C * H
 COORDS = ((0, 1), (0, 2), (1, 2))
 TILES = N // 128
 FIRST = 6
-CHUNKS = ((0, FIRST), (FIRST, TILES - FIRST))
 JOBS = TILES * PLANES
 FILL = 2
-HEADF = 1
-LEAD = 12
+HEADF = 3
+LEAD = 10
 HURRY = 20
-RATE = 17
+RATE = 18
 EB = 10
-SQB = 2
+SQB = 3
 W2 = 0
 I2 = 0
 VCO = 1
 PLAIN = (0, 3)
 AHEAD = 2
-VCO0 = 1
+VCO0 = 0
+LATE = 0
+SIZES = (4, 2, 2)
+W1 = 0
+I1 = 0
+KEEP = "vv"
 TINY = 2.0**-60
+CHUNKS = [(sum(SIZES[:c]), SIZES[c]) for c in range(len(SIZES))]
 
 
 def tile_kplanesgaussiananchordecoder_w4_kernel(
@@ -51,19 +56,34 @@ def tile_kplanesgaussiananchordecoder_w4_kernel(
         ps_o = ctx.enter_context(tc.psum_pool(name="ps_o", bufs=2))
         ctx.enter_context(tc.manual_schedule())
 
-        pt = keep.tile([128, TILES, 3], BF16, name="pt")
-        nc.sync.dma_start(out=pt[:], in_=pts.rearrange("(p j) x -> p j x", j=TILES))
+        head = SIZES[0]
+        pt = keep.tile([128, head, 4], BF16, name="pt")
+        nc.sync.dma_start(out=pt[:, :, 0:3], in_=pts[0 : 128 * head, :].rearrange("(j p) x -> p j x", p=128))
+        fs = keep.tile([128, 4], F32, name="fs")
+        nc.scalar.dma_start(out=fs[:], in_=feat_scale.rearrange("o (p t) x -> p (o t x)", t=4))
+        fb = [keep.tile([128, 4, C], U8, name="fb%d" % pl) for pl in range(PLANES)]
+
+        def load_feat(pl):
+            nc.sync.dma_start(out=fb[pl][:], in_=feat_bytes[pl].rearrange("(p t) c -> p t c", t=4))
+
         cenb = keep.tile([128, PLANES, 8], BF16, name="cenb")
-        nc.sync.dma_start(out=cenb[:], in_=cen.rearrange("x (p t) e -> p x (t e)", t=4))
+        nc.scalar.dma_start(out=cenb[:], in_=cen.rearrange("x (p t) e -> p x (t e)", t=4))
+        load_feat(0)
         gat = keep.tile([128, PLANES, 4], BF16, name="gat")
         nc.sync.dma_start(out=gat[:], in_=ga.rearrange("x (p t) -> p x t", t=4))
-        fs = keep.tile([128, 4], F32, name="fs")
-        nc.sync.dma_start(out=fs[:], in_=feat_scale.rearrange("o (p t) x -> p (o t x)", t=4))
-        fb = []
-        for pl in range(PLANES):
-            bytes_pl = keep.tile([128, 4, C], U8, name="fb%d" % pl)
-            nc.sync.dma_start(out=bytes_pl[:], in_=feat_bytes[pl].rearrange("(p t) c -> p t c", t=4))
-            fb.append(bytes_pl)
+        load_feat(1)
+        half = N // 2
+        points = [keep.tile([128, half, 3], BF16, name="points%d" % h) for h in range(2)]
+
+        def load_points(h):
+            nc.sync.dma_start(
+                out=points[h][:].rearrange("p n x -> p (n x)"),
+                in_=pts[h * half : (h + 1) * half, :].rearrange("n x -> (n x)").partition_broadcast(128),
+            )
+
+        load_points(0)
+        load_feat(2)
+        load_points(1)
         gcb = keep.tile([128, 4], BF16, name="gcb")
         nc.sync.dma_start(out=gcb[:], in_=gc.rearrange("(p t) -> p t", t=4))
         ww = keep.tile([128, 2 * H], U8, name="ww", align_bytes=64)
@@ -80,30 +100,32 @@ def tile_kplanesgaussiananchordecoder_w4_kernel(
         identb = keep.tile([128, 128], BF16, name="identb")
         make_identity(nc, identb[:])
         ident = keep.tile([128, 128], F32, name="ident")
-        make_identity(nc, ident[:])
+        nc.scalar.activation(out=ident[:], in_=identb[:], func=ACT.Copy)
 
         spread = {}
 
-        def spread_points(x, pool, tag):
-            bank = pool.tile([128, TILES, 128], BF16, name="bank", tag=tag)
-            for j in range(TILES):
+        def spread_points(x):
+            bank = ps_o.tile([128, head, 128], BF16, name="bank", tag="o")
+            for j in range(head):
                 nc.tensor.transpose(bank[:, j, :], pt[:, j, x : x + 1].to_broadcast([128, 128]), identb[:])
             spread[x] = bank[:].rearrange("p j n -> p (j n)")
 
-        def keep_points(x):
-            coord = keep.tile([128, N], BF16, name="coord%d" % x)
-            nc.vector.tensor_copy(out=coord[:], in_=spread[x])
-            spread[x] = coord[:]
+        def coordinate(step, e):
+            first, count, pl = steps[step]
+            if step == 0:
+                return spread[e]
+            h, start = divmod(128 * first, half)
+            return points[h][:, start : start + 128 * count, COORDS[pl][e]]
 
         gab = keep.tile([128, PLANES, M], BF16, name="gab")
 
-        def spread_gains(planes):
+        def spread_gains(planes, copy):
             bank = ps_f.tile([128, len(planes), 2, 128], F32, name="bank", tag="f")
             for j, pl in enumerate(planes):
                 words = gat[:, pl, :].bitcast(F32)
                 for u in range(2):
                     nc.tensor.transpose(bank[:, j, u, :], words[:, u : u + 1].to_broadcast([128, 128]), ident[:])
-            return lambda: nc.vector.tensor_copy(
+            return lambda: copy(
                 out=gab[:, planes[0] : planes[-1] + 1, :].bitcast(F32), in_=bank[:].rearrange("p j u m -> p j (u m)")
             )
 
@@ -111,7 +133,7 @@ def tile_kplanesgaussiananchordecoder_w4_kernel(
         fsc = [keep.tile([128, C], U8, name="fsc%d" % pl, align_bytes=64) for pl in range(PLANES)]
 
         def feat_parts(pl, widen_on_scalar, inter_on_scalar):
-            wide = work.tile([128, 4, C], BF16, name="wide")
+            wide = work.tile([128, 4, C], BF16, name="wide", bufs=3)
             grp = work.tile([128, 4 * C], BF16, name="fgrp", align_bytes=64)
 
             def widen(t):
@@ -150,10 +172,10 @@ def tile_kplanesgaussiananchordecoder_w4_kernel(
             first, count, pl = steps[step]
             hi = count if hi is None else hi
             if r == 0 and lo == 0:
-                sq[step] = work.tile([128, 2, 4, count * 128], F32, name="sq", tag="sq%d" % count, bufs=SQB if count == FIRST else PLANES)
+                sq[step] = work.tile([128, 2, 4, count * 128], F32, name="sq", tag="sq%d" % count, bufs=SQB)
             nc.scalar.activation(
                 out=sq[step][:, e, t, 128 * lo : 128 * hi],
-                in_=spread[COORDS[pl][e]][:, 128 * (first + lo) : 128 * (first + hi)],
+                in_=coordinate(step, e),
                 func=ACT.Square,
                 scale=-1.0,
                 bias=cenb[:, pl, 2 * t + e : 2 * t + e + 1],
@@ -240,11 +262,11 @@ def tile_kplanesgaussiananchordecoder_w4_kernel(
             nc.vector.quantize_mx(out=aw[:].bitcast(FP8X4), scales=asc[:], in_=grouped[r][:])
             quantised[r] = (aw, asc)
 
-        def plane_product(k):
+        def plane_product(k, pool=ps_f, tag="f"):
             aw, asc = quantised[k // 2]
             pl = job(k)[1]
             cols = slice(128 * (k % 2), 128 * (k % 2) + 128)
-            f = ps_f.tile([128, 4, 128], F32, name="f", tag="f")
+            f = pool.tile([128, 4, 128], F32, name="f", tag=tag)
             for t in range(4):
                 nc.tensor.matmul_mx(
                     out=f[:, t, :],
@@ -305,7 +327,7 @@ def tile_kplanesgaussiananchordecoder_w4_kernel(
         def sigmoid(n, count):
             nc.scalar.activation(out=lall[:, n : n + count, :], in_=tall[:, n : n + count, :], func=ACT.Sigmoid, scale=-1.0)
 
-        out_tiles = out.rearrange("(p j) h -> p j h", j=TILES)
+        out_tiles = out.rearrange("(j p) h -> p j h", p=128)
 
         def logarithm(n, count):
             nc.scalar.activation(out=lall[:, n : n + count, :], in_=lall[:, n : n + count, :], func=ACT.Ln, bias=TINY)
@@ -316,21 +338,16 @@ def tile_kplanesgaussiananchordecoder_w4_kernel(
             )
             nc.sync.dma_start(out=out_tiles[:, n : n + count, :], in_=tall[:, n : n + count, :])
 
-        spread_points(0, ps_o, "o")
-        spread_points(1, ps_o, "o")
-        spread_points(2, ps_xt, "xt")
-        keep_gains = [spread_gains([0, 1]), spread_gains([2])]
-        first, second, third = feat_parts(0, 0, 0), feat_parts(1, 0, 0), feat_parts(2, W2, I2)
+        spread_points(0)
+        spread_points(1)
+        eng = [nc.scalar.copy if x == "s" else nc.vector.tensor_copy for x in KEEP]
+        spare = [spread_gains([0, 1], eng[0]), spread_gains([2], eng[1])]
+        first, second, third = feat_parts(0, 0, 0), feat_parts(1, W1, I1), feat_parts(2, W2, I2)
         for part in first[:4] + second[:4] + first[4:6]:
             part()
         for q in range(8):
             square(q)
-        keep_points(2)
-        first[6]()
-        keep_points(0)
-        for part in second[4:6] + keep_gains[:1]:
-            part()
-        filler = second[6:] + [lambda: keep_points(1)] + third[:4] + keep_gains[1:] + third[4:]
+        filler = second[4:5] + first[6:] + second[5:6] + third[:4] + second[6:] + third[4:]
         for x in range(HEADF):
             filler.pop(0)()
         squares = list(range(8, 8 * len(steps)))
@@ -377,6 +394,8 @@ def tile_kplanesgaussiananchordecoder_w4_kernel(
             if last_plane(2 * r - 8):
                 bias(job(2 * r - 8)[2])
             fill(FILL)
+            if spare:
+                spare.pop(0)()
             next_minimum()
             if 3 <= r:
                 multiply(2 * r - 5)
@@ -405,14 +424,10 @@ def tile_kplanesgaussiananchordecoder_w4_kernel(
             normalise(2 * r + 1)
             turn(r)
 
-        def products(r):
+        def products(r, pool, tag):
             quantise_a(r)
-            plane_product(2 * r)
-            plane_product(2 * r + 1)
-
-        def multiplies(r):
-            multiply(2 * r)
-            multiply(2 * r + 1)
+            plane_product(2 * r, pool, tag)
+            plane_product(2 * r + 1, pool, tag)
 
         reciprocal(wide)
         reciprocal(wide + 1)
@@ -424,28 +439,31 @@ def tile_kplanesgaussiananchordecoder_w4_kernel(
         sigmoid(2, 2)
         reciprocal(wide + 2)
         weights(wide + 1)
-        products(wide)
+        products(wide, ps_f, "f")
         copy_out(wide + 1, nc.scalar.copy)
         sigmoid(4, 2)
         weights(wide + 2)
-        multiplies(wide)
-        products(wide + 1)
+        multiply(2 * wide)
+        products(wide + 1, ps_d2, "d2")
+        multiply(2 * wide + 1)
         logarithm(0, 2)
         copy_out(wide + 2, nc.vector.tensor_copy if VCO else nc.scalar.copy)
         logarithm(2, 2)
-        multiplies(wide + 1)
+        multiply(2 * wide + 2)
         logarithm(4, 2)
-        products(wide + 2)
-        finish(0, 2)
-        multiplies(wide + 2)
-        finish(2, 1)
+        products(wide + 2, ps_f, "f")
+        multiply(2 * wide + 3)
+        finish(0, 1)
+        multiply(2 * wide + 4)
+        multiply(2 * wide + 5)
         quantise_z(FIRST // 2)
         linear(FIRST)
         linear(FIRST + 1)
-        finish(3, 1)
+        finish(1, 1)
         for n in range(FIRST, TILES):
             bias(n)
             sigmoid(n, 1)
+        finish(2, 2)
         finish(4, 2)
         for n in range(FIRST, TILES):
             logarithm(n, 1)

@@ -26,7 +26,7 @@ HEADF = 3
 LEAD = 10
 HURRY = 20
 RATE = 18
-EB = 10
+EB = 14
 SQB = 3
 W2 = 0
 I2 = 0
@@ -34,11 +34,19 @@ VCO = 1
 PLAIN = (0, 3)
 AHEAD = 2
 VCO0 = 0
-LATE = 0
+LATE = 3
 SIZES = (4, 2, 2)
 W1 = 0
 I1 = 0
 KEEP = "vv"
+XB = 3
+RAMP = 4
+ON_SCALAR = ()
+POOL = range(2, 8)
+PBIAS = 2
+HALVES = 0
+PTAIL = 0
+GB = 2
 TINY = 2.0**-60
 CHUNKS = [(sum(SIZES[:c]), SIZES[c]) for c in range(len(SIZES))]
 
@@ -63,12 +71,13 @@ def tile_kplanesgaussiananchordecoder_w4_kernel(
         nc.scalar.dma_start(out=fs[:], in_=feat_scale.rearrange("o (p t) x -> p (o t x)", t=4))
         fb = [keep.tile([128, 4, C], U8, name="fb%d" % pl) for pl in range(PLANES)]
 
-        def load_feat(pl):
-            nc.sync.dma_start(out=fb[pl][:], in_=feat_bytes[pl].rearrange("(p t) c -> p t c", t=4))
+        def load_feat(pl, lo=0, hi=4):
+            nc.sync.dma_start(out=fb[pl][:, lo:hi, :], in_=feat_bytes[pl].rearrange("(p t) c -> p t c", t=4)[:, lo:hi, :])
 
         cenb = keep.tile([128, PLANES, 8], BF16, name="cenb")
         nc.scalar.dma_start(out=cenb[:], in_=cen.rearrange("x (p t) e -> p x (t e)", t=4))
-        load_feat(0)
+        load_feat(0, 0, 2)
+        load_feat(0, 2, 4)
         gat = keep.tile([128, PLANES, 4], BF16, name="gat")
         nc.sync.dma_start(out=gat[:], in_=ga.rearrange("x (p t) -> p x t", t=4))
         load_feat(1)
@@ -86,6 +95,7 @@ def tile_kplanesgaussiananchordecoder_w4_kernel(
         load_points(1)
         gcb = keep.tile([128, 4], BF16, name="gcb")
         nc.sync.dma_start(out=gcb[:], in_=gc.rearrange("(p t) -> p t", t=4))
+        gcf = keep.tile([128, 4], F32, name="gcf")
         ww = keep.tile([128, 2 * H], U8, name="ww", align_bytes=64)
         nc.sync.dma_start(out=ww[:], in_=w1_words[0])
         ws = keep.tile([128, H], U8, name="ws", align_bytes=64)
@@ -200,8 +210,8 @@ def tile_kplanesgaussiananchordecoder_w4_kernel(
             d2s[k] = d2
 
         def minimum(k):
-            xs = work.tile([128, M], F32, name="xs", bufs=3)
-            mn = work.tile([128, 1], F32, name="mn", bufs=3)
+            xs = work.tile([128, M], F32, name="xs", bufs=XB)
+            mn = work.tile([128, 1], F32, name="mn", bufs=XB)
             nc.vector.tensor_scalar(
                 out=xs[:].rearrange("n (u p e) -> n u p e", u=2, e=2),
                 in0=d2s[k][:].rearrange("n (u e) p -> n u p e", u=2),
@@ -216,7 +226,7 @@ def tile_kplanesgaussiananchordecoder_w4_kernel(
         def exponential(k):
             xs, mn = xss[k]
             e = work.tile([128, M], F32, name="e", bufs=EB)
-            if k % 2 == 0:
+            if k // 2 not in sums:
                 sums[k // 2] = work.tile([128, 2], F32, name="sm", bufs=6)
             nc.scalar.activation(
                 out=e[:], in_=xs[:], func=ACT.Exp, scale=-1.0, bias=mn[:], accum_out=sums[k // 2][:, k % 2 : k % 2 + 1]
@@ -227,9 +237,21 @@ def tile_kplanesgaussiananchordecoder_w4_kernel(
             recips[r] = work.tile([128, 2], F32, name="ri")
             nc.vector.reciprocal(out=recips[r][:], in_=sums[r][:])
 
+        weighted = {}
+
+        def gain_on_pool(k, spent):
+            nc.gpsimd.tensor_tensor(out=spent[:], in0=es[k][:], in1=gab[:, job(k)[1], :], op=ALU.mult)
+            weighted[k] = spent
+
         def normalise(k):
             pl = job(k)[1]
             a = work.tile([128, M], BF16, name="a", bufs=4)
+            normed[k] = a
+            if k in weighted:
+                nc.vector.tensor_scalar(
+                    out=a[:], in0=weighted[k][:], scalar1=recips[k // 2][:, k % 2 : k % 2 + 1], scalar2=None, op0=ALU.mult
+                )
+                return
             nc.vector.scalar_tensor_tensor(
                 out=a[:],
                 in0=es[k][:],
@@ -249,7 +271,7 @@ def tile_kplanesgaussiananchordecoder_w4_kernel(
             grouped[r] = xt
 
         def copy_out(r, copy):
-            g = work.tile([128, 256 * 4], BF16, name="g", align_bytes=64)
+            g = work.tile([128, 256 * 4], BF16, name="g", align_bytes=64, bufs=GB)
             copy(
                 out=g[:].bitcast(F32).rearrange("p (j n u) -> p j n u", j=2, u=2),
                 in_=grouped[r][:].rearrange("p j u n -> p j n u"),
@@ -266,6 +288,21 @@ def tile_kplanesgaussiananchordecoder_w4_kernel(
             aw, asc = quantised[k // 2]
             pl = job(k)[1]
             cols = slice(128 * (k % 2), 128 * (k % 2) + 128)
+            if k // 2 in ON_SCALAR:
+                f = pool.tile([128, 2, 256], F32, name="f", tag=tag)
+                for h in range(2):
+                    t = 2 * (k % 2) + h
+                    nc.tensor.matmul_mx(
+                        out=f[:, h, :],
+                        lhsT=fw[pl][:, 128 * t : 128 * t + 128].bitcast(FP8X4),
+                        lhsT_scale=fsc[pl][:, 128 * t : 128 * t + 128],
+                        rhs=aw[:].bitcast(FP8X4),
+                        rhs_scale=asc[:],
+                        start=True,
+                        stop=True,
+                    )
+                fps[k] = f
+                return
             f = pool.tile([128, 4, 128], F32, name="f", tag=tag)
             for t in range(4):
                 nc.tensor.matmul_mx(
@@ -279,18 +316,32 @@ def tile_kplanesgaussiananchordecoder_w4_kernel(
                 )
             fps[k] = f
 
+        gained = {}
+
         def multiply(k):
             step, pl, n = job(k)
+            if k // 2 in ON_SCALAR:
+                if n // 2 not in gained:
+                    gained[n // 2] = work.tile([128, 4, 256], F32, name="gained")
+                    for j in range(2):
+                        zs[n - n % 2 + j] = gained[n // 2][:, :, 128 * j : 128 * j + 128].rearrange("p t n -> p n t")
+                for h in range(2):
+                    t = 2 * (k % 2) + h
+                    nc.scalar.activation(
+                        out=gained[n // 2][:, t, :], in_=fps[k][:, h, :], func=ACT.Copy, scale=gcf[:, t : t + 1]
+                    )
+                return
             f = fps[k][:].rearrange("p t n -> p n t")
             if pl == 0:
                 other = gcb[:].unsqueeze(1).to_broadcast([128, 128, 4])
             else:
-                other = zs[n][:]
+                other = zs[n]
             if pl < PLANES - 1:
-                zs[n] = work.tile([128, 128, 4], F32, name="z", bufs=FIRST + 1)
-                dst = zs[n][:]
+                z = work.tile([128, 128, 4], F32, name="z", bufs=FIRST + 1)
+                zs[n] = z[:]
+                dst = zs[n]
             else:
-                if n % 2 == 0:
+                if n // 2 not in zgs:
                     zgs[n // 2] = work.tile([128, 2, 128, 4], BF16, name="zg", align_bytes=64)
                 dst = zgs[n // 2][:, n % 2]
             nc.vector.tensor_tensor(out=dst, in0=f, in1=other, op=ALU.mult)
@@ -318,25 +369,42 @@ def tile_kplanesgaussiananchordecoder_w4_kernel(
             )
             ops[n] = o
 
-        tall = keep.tile([128, TILES, H], F32, name="tall")
         lall = keep.tile([128, TILES, H], F32, name="lall")
 
         def bias(n):
-            nc.vector.tensor_tensor(out=tall[:, n, :], in0=ops[n][:], in1=bb[:], op=ALU.add)
+            ts[n] = keep.tile([128, H], F32, name="t%d" % n)
+            nc.vector.tensor_tensor(out=ts[n][:], in0=ops[n][:], in1=bb[:], op=ALU.add)
+
+        def unload(n):
+            nc.scalar.copy(out=lall[:, n, :], in_=ops[n][:])
+
+        def bias_on_pool(n, spent):
+            nc.gpsimd.tensor_tensor(out=spent[:], in0=lall[:, n, :], in1=bb[:], op=ALU.add)
+            ts[n] = spent
 
         def sigmoid(n, count):
-            nc.scalar.activation(out=lall[:, n : n + count, :], in_=tall[:, n : n + count, :], func=ACT.Sigmoid, scale=-1.0)
+            for j in range(n, n + count):
+                nc.scalar.activation(out=lall[:, j, :], in_=ts[j][:], func=ACT.Sigmoid, scale=-1.0)
 
         out_tiles = out.rearrange("(j p) h -> p j h", p=128)
 
         def logarithm(n, count):
             nc.scalar.activation(out=lall[:, n : n + count, :], in_=lall[:, n : n + count, :], func=ACT.Ln, bias=TINY)
 
-        def finish(n, count):
+        def last_logarithm(n, h):
+            cols = slice(h * H // 2, (h + 1) * H // 2)
+            nc.scalar.activation(out=lall[:, n, cols], in_=lall[:, n, cols], func=ACT.Ln, bias=TINY)
             nc.vector.scalar_tensor_tensor(
-                out=tall[:, n : n + count, :], in0=lall[:, n : n + count, :], scalar=-1.0, in1=tall[:, n : n + count, :], op0=ALU.mult, op1=ALU.max
+                out=lall[:, n, cols], in0=lall[:, n, cols], scalar=-1.0, in1=ts[n][:, cols], op0=ALU.mult, op1=ALU.max
             )
-            nc.sync.dma_start(out=out_tiles[:, n : n + count, :], in_=tall[:, n : n + count, :])
+            nc.sync.dma_start(out=out_tiles[:, n, cols], in_=lall[:, n, cols])
+
+        def finish(n, count):
+            for j in range(n, n + count):
+                nc.vector.scalar_tensor_tensor(
+                    out=lall[:, j, :], in0=lall[:, j, :], scalar=-1.0, in1=ts[j][:], op0=ALU.mult, op1=ALU.max
+                )
+            nc.sync.dma_start(out=out_tiles[:, n : n + count, :], in_=lall[:, n : n + count, :])
 
         spread_points(0)
         spread_points(1)
@@ -347,6 +415,8 @@ def tile_kplanesgaussiananchordecoder_w4_kernel(
             part()
         for q in range(8):
             square(q)
+        if ON_SCALAR:
+            nc.vector.tensor_copy(out=gcf[:], in_=gcb[:])
         filler = second[4:5] + first[6:] + second[5:6] + third[:4] + second[6:] + third[4:]
         for x in range(HEADF):
             filler.pop(0)()
@@ -382,6 +452,18 @@ def tile_kplanesgaussiananchordecoder_w4_kernel(
         for i in range(AHEAD):
             distances(i)
         next_squares(LEAD)
+        unloaded = []
+
+        def spent_g(r):
+            return grouped[r][:].bitcast(F32)
+
+        def leave_bank(n):
+            if n < PBIAS:
+                unload(n)
+                unloaded.append(n)
+            else:
+                bias(n)
+
         wide = PLANES * FIRST // 2
         for r in range(wide + 3):
             next_minimum()
@@ -392,7 +474,7 @@ def tile_kplanesgaussiananchordecoder_w4_kernel(
             if 3 <= r:
                 multiply(2 * r - 6)
             if last_plane(2 * r - 8):
-                bias(job(2 * r - 8)[2])
+                leave_bank(job(2 * r - 8)[2])
             fill(FILL)
             if spare:
                 spare.pop(0)()
@@ -400,10 +482,11 @@ def tile_kplanesgaussiananchordecoder_w4_kernel(
             if 3 <= r:
                 multiply(2 * r - 5)
             if last_plane(2 * r - 7):
-                bias(job(2 * r - 7)[2])
+                leave_bank(job(2 * r - 7)[2])
             fill(FILL)
             if 2 <= r <= wide + 1:
                 quantise_a(r - 2)
+                flat = [None, spent_g(r - 2), es.get(2 * wide - 4)]
                 plane_product(2 * r - 4)
                 plane_product(2 * r - 3)
             if r >= HURRY:
@@ -414,9 +497,18 @@ def tile_kplanesgaussiananchordecoder_w4_kernel(
                 linear(n - 1)
                 linear(n)
             if 1 <= r <= wide:
-                normalise(2 * r - 2)
                 normalise(2 * r - 1)
+                normalise(2 * r - 2)
                 turn(r - 1)
+                if unloaded:
+                    bias_on_pool(unloaded.pop(0), es[2 * r - 2])
+                elif r in POOL:
+                    gain_on_pool(2 * r + 1, es[2 * r - 2])
+            if r == wide and PTAIL >= 1:
+                gain_on_pool(2 * wide, es[2 * r - 2])
+            if r == wide + 1:
+                for j in range(1, PTAIL):
+                    gain_on_pool(2 * wide + j, flat[j])
             next_squares(RATE)
 
         def weights(r):
@@ -446,13 +538,16 @@ def tile_kplanesgaussiananchordecoder_w4_kernel(
         multiply(2 * wide)
         products(wide + 1, ps_d2, "d2")
         multiply(2 * wide + 1)
+        if not VCO:
+            copy_out(wide + 2, nc.scalar.copy)
         logarithm(0, 2)
-        copy_out(wide + 2, nc.vector.tensor_copy if VCO else nc.scalar.copy)
+        if VCO:
+            copy_out(wide + 2, nc.vector.tensor_copy)
         logarithm(2, 2)
         multiply(2 * wide + 2)
         logarithm(4, 2)
-        products(wide + 2, ps_f, "f")
         multiply(2 * wide + 3)
+        products(wide + 2, ps_f, "f")
         finish(0, 1)
         multiply(2 * wide + 4)
         multiply(2 * wide + 5)
@@ -465,6 +560,12 @@ def tile_kplanesgaussiananchordecoder_w4_kernel(
             sigmoid(n, 1)
         finish(2, 2)
         finish(4, 2)
-        for n in range(FIRST, TILES):
-            logarithm(n, 1)
-            finish(n, 1)
+        if HALVES:
+            logarithm(FIRST, 1)
+            finish(FIRST, 1)
+            for h in range(2):
+                last_logarithm(FIRST + 1, h)
+        else:
+            for n in range(FIRST, TILES):
+                logarithm(n, 1)
+                finish(n, 1)

@@ -15,40 +15,20 @@ ACT = mybir.ActivationFunctionType
 ALU = mybir.AluOpType
 
 N, PLANES, M, C, H = 1024, 3, 512, 512, 512
-WIDTH2 = 0.0018
 FLOPS = 2 * N * M * C * PLANES + 2 * N * C * H
+WIDTH2 = 0.0018
 COORDS = ((0, 1), (0, 2), (1, 2))
 TILES = N // 128
-FIRST = 6
 JOBS = TILES * PLANES
-FILL = 2
-HEADF = 3
-LEAD = 10
-HURRY = 20
-RATE = 18
-EB = 14
-SQB = 3
-W2 = 0
-I2 = 0
-VCO = 1
-PLAIN = (0, 3)
-AHEAD = 2
-VCO0 = 0
-LATE = 3
-SIZES = (4, 2, 2)
-W1 = 0
-I1 = 0
-KEEP = "vv"
-XB = 3
-RAMP = 4
-ON_SCALAR = ()
-POOL = range(2, 8)
-PBIAS = 2
-HALVES = 0
-PTAIL = 0
-GB = 2
 TINY = 2.0**-60
-CHUNKS = [(sum(SIZES[:c]), SIZES[c]) for c in range(len(SIZES))]
+
+CHUNKS = ((0, 4), (4, 2), (6, 2))
+EARLY_TILES = CHUNKS[-1][0]
+EARLY_PAIRS = PLANES * EARLY_TILES // 2
+MATMUL_BLOCKS = (0, 3)
+SQUARES_A_TURN, SQUARES_AHEAD, SQUARES_BETWEEN = 18, 10, 10
+FEAT_AHEAD, FEAT_A_MINIMUM = 3, 2
+POOL_BIAS_TILES = 2
 
 
 def tile_kplanesgaussiananchordecoder_w4_kernel(
@@ -64,23 +44,26 @@ def tile_kplanesgaussiananchordecoder_w4_kernel(
         ps_o = ctx.enter_context(tc.psum_pool(name="ps_o", bufs=2))
         ctx.enter_context(tc.manual_schedule())
 
-        head = SIZES[0]
-        pt = keep.tile([128, head, 4], BF16, name="pt")
-        nc.sync.dma_start(out=pt[:, :, 0:3], in_=pts[0 : 128 * head, :].rearrange("(j p) x -> p j x", p=128))
-        fs = keep.tile([128, 4], F32, name="fs")
-        nc.scalar.dma_start(out=fs[:], in_=feat_scale.rearrange("o (p t) x -> p (o t x)", t=4))
-        fb = [keep.tile([128, 4, C], U8, name="fb%d" % pl) for pl in range(PLANES)]
+        head_tiles = CHUNKS[0][1]
+        head_points = keep.tile([128, head_tiles, 4], BF16, name="head_points")
+        nc.sync.dma_start(
+            out=head_points[:, :, 0:3], in_=pts[0 : 128 * head_tiles, :].rearrange("(j p) x -> p j x", p=128)
+        )
+        scale_sb = keep.tile([128, 4], F32, name="scale_sb")
+        nc.scalar.dma_start(out=scale_sb[:], in_=feat_scale.rearrange("o (p t) x -> p (o t x)", t=4))
+        bytes_sb = [keep.tile([128, 4, C], U8, name="bytes_sb%d" % pl) for pl in range(PLANES)]
 
-        def load_feat(pl, lo=0, hi=4):
-            nc.sync.dma_start(out=fb[pl][:, lo:hi, :], in_=feat_bytes[pl].rearrange("(p t) c -> p t c", t=4)[:, lo:hi, :])
+        def load_feat(pl, lo, hi):
+            rows = feat_bytes[pl].rearrange("(p t) c -> p t c", t=4)
+            nc.sync.dma_start(out=bytes_sb[pl][:, lo:hi, :], in_=rows[:, lo:hi, :])
 
-        cenb = keep.tile([128, PLANES, 8], BF16, name="cenb")
-        nc.scalar.dma_start(out=cenb[:], in_=cen.rearrange("x (p t) e -> p x (t e)", t=4))
+        centres = keep.tile([128, PLANES, 8], BF16, name="centres")
+        nc.scalar.dma_start(out=centres[:], in_=cen.rearrange("x (p t) e -> p x (t e)", t=4))
         load_feat(0, 0, 2)
         load_feat(0, 2, 4)
-        gat = keep.tile([128, PLANES, 4], BF16, name="gat")
-        nc.sync.dma_start(out=gat[:], in_=ga.rearrange("x (p t) -> p x t", t=4))
-        load_feat(1)
+        gain_rows = keep.tile([128, PLANES, 4], BF16, name="gain_rows")
+        nc.sync.dma_start(out=gain_rows[:], in_=ga.rearrange("x (p t) -> p x t", t=4))
+        load_feat(1, 0, 4)
         half = N // 2
         points = [keep.tile([128, half, 3], BF16, name="points%d" % h) for h in range(2)]
 
@@ -91,481 +74,390 @@ def tile_kplanesgaussiananchordecoder_w4_kernel(
             )
 
         load_points(0)
-        load_feat(2)
+        load_feat(2, 0, 4)
         load_points(1)
-        gcb = keep.tile([128, 4], BF16, name="gcb")
-        nc.sync.dma_start(out=gcb[:], in_=gc.rearrange("(p t) -> p t", t=4))
-        gcf = keep.tile([128, 4], F32, name="gcf")
-        ww = keep.tile([128, 2 * H], U8, name="ww", align_bytes=64)
-        nc.sync.dma_start(out=ww[:], in_=w1_words[0])
-        ws = keep.tile([128, H], U8, name="ws", align_bytes=64)
-        nc.vector.memset(ws[:].bitcast(I32), 0)
-        for qd in range(4):
+        channel_gain = keep.tile([128, 4], BF16, name="channel_gain")
+        nc.sync.dma_start(out=channel_gain[:], in_=gc.rearrange("(p t) -> p t", t=4))
+        w_words = keep.tile([128, 2 * H], U8, name="w_words", align_bytes=64)
+        nc.sync.dma_start(out=w_words[:], in_=w1_words[0])
+        w_scales = keep.tile([128, H], U8, name="w_scales", align_bytes=64)
+        nc.vector.memset(w_scales[:].bitcast(I32), 0)
+        for q in range(4):
             nc.sync.dma_start(
-                out=ws[32 * qd : 32 * qd + 4, :].bitcast(I32), in_=w1_scales[0, 4 * qd : 4 * qd + 4, :].bitcast(I32)
+                out=w_scales[32 * q : 32 * q + 4, :].bitcast(I32), in_=w1_scales[0, 4 * q : 4 * q + 4, :].bitcast(I32)
             )
-        bb = keep.tile([128, H], BF16, name="bb")
-        nc.sync.dma_start(out=bb[:], in_=b1.partition_broadcast(128))
+        bias_row = keep.tile([128, H], BF16, name="bias_row")
+        nc.sync.dma_start(out=bias_row[:], in_=b1.partition_broadcast(128))
 
-        identb = keep.tile([128, 128], BF16, name="identb")
-        make_identity(nc, identb[:])
+        ident_bf = keep.tile([128, 128], BF16, name="ident_bf")
+        make_identity(nc, ident_bf[:])
         ident = keep.tile([128, 128], F32, name="ident")
-        nc.scalar.activation(out=ident[:], in_=identb[:], func=ACT.Copy)
-
-        spread = {}
-
-        def spread_points(x):
-            bank = ps_o.tile([128, head, 128], BF16, name="bank", tag="o")
-            for j in range(head):
-                nc.tensor.transpose(bank[:, j, :], pt[:, j, x : x + 1].to_broadcast([128, 128]), identb[:])
-            spread[x] = bank[:].rearrange("p j n -> p (j n)")
-
-        def coordinate(step, e):
-            first, count, pl = steps[step]
-            if step == 0:
-                return spread[e]
-            h, start = divmod(128 * first, half)
-            return points[h][:, start : start + 128 * count, COORDS[pl][e]]
-
-        gab = keep.tile([128, PLANES, M], BF16, name="gab")
-
-        def spread_gains(planes, copy):
-            bank = ps_f.tile([128, len(planes), 2, 128], F32, name="bank", tag="f")
-            for j, pl in enumerate(planes):
-                words = gat[:, pl, :].bitcast(F32)
-                for u in range(2):
-                    nc.tensor.transpose(bank[:, j, u, :], words[:, u : u + 1].to_broadcast([128, 128]), ident[:])
-            return lambda: copy(
-                out=gab[:, planes[0] : planes[-1] + 1, :].bitcast(F32), in_=bank[:].rearrange("p j u m -> p j (u m)")
-            )
-
-        fw = [keep.tile([128, C], U32, name="fw%d" % pl, align_bytes=64) for pl in range(PLANES)]
-        fsc = [keep.tile([128, C], U8, name="fsc%d" % pl, align_bytes=64) for pl in range(PLANES)]
-
-        def feat_parts(pl, widen_on_scalar, inter_on_scalar):
-            wide = work.tile([128, 4, C], BF16, name="wide", bufs=3)
-            grp = work.tile([128, 4 * C], BF16, name="fgrp", align_bytes=64)
-
-            def widen(t):
-                if t < widen_on_scalar:
-                    nc.scalar.activation(
-                        out=wide[:, t, :], in_=fb[pl][:, t, :].bitcast(FP8), func=ACT.Copy, scale=fs[:, t : t + 1]
-                    )
-                    return
-                nc.vector.tensor_scalar(
-                    out=wide[:, t, :], in0=fb[pl][:, t, :].bitcast(FP8), scalar1=fs[:, t : t + 1], scalar2=None, op0=ALU.mult
-                )
-
-            def inter(h):
-                copy = nc.scalar.copy if h < inter_on_scalar else nc.vector.tensor_copy
-                copy(
-                    out=grp[:].rearrange("p (t m j) -> p t m j", t=4, j=4)[:, 2 * h : 2 * h + 2],
-                    in_=wide[:].rearrange("p j (m t) -> p t m j", t=4)[:, 2 * h : 2 * h + 2],
-                )
-
-            def quant():
-                nc.vector.quantize_mx(out=fw[pl][:].bitcast(FP8X4), scales=fsc[pl][:], in_=grp[:])
-
-            return [lambda t=t: widen(t) for t in range(4)] + [lambda: inter(0), lambda: inter(1), quant]
+        nc.scalar.activation(out=ident[:], in_=ident_bf[:], func=ACT.Copy)
 
         steps = [(first, count, pl) for first, count in CHUNKS for pl in range(PLANES)]
         jobs = [(s, pl, first + i) for s, (first, count, pl) in enumerate(steps) for i in range(count)]
 
-        def job(k):
-            return jobs[k]
+        head_coords = []
 
-        sq = {}
+        def spread_points(x):
+            bank = ps_o.tile([128, head_tiles, 128], BF16, name="head_bank", tag="o")
+            for j in range(head_tiles):
+                nc.tensor.transpose(bank[:, j, :], head_points[:, j, x : x + 1].to_broadcast([128, 128]), ident_bf[:])
+            head_coords.append(bank[:].rearrange("p j n -> p (j n)"))
 
-        def square(q, lo=0, hi=None):
-            step, r = divmod(q, 8)
-            e, t = divmod(r, 4)
-            first, count, pl = steps[step]
-            hi = count if hi is None else hi
-            if r == 0 and lo == 0:
-                sq[step] = work.tile([128, 2, 4, count * 128], F32, name="sq", tag="sq%d" % count, bufs=SQB)
-            nc.scalar.activation(
-                out=sq[step][:, e, t, 128 * lo : 128 * hi],
-                in_=coordinate(step, e),
-                func=ACT.Square,
-                scale=-1.0,
-                bias=cenb[:, pl, 2 * t + e : 2 * t + e + 1],
+        gains = keep.tile([128, PLANES, M], BF16, name="gains")
+
+        def spread_gains(planes):
+            bank = ps_f.tile([128, len(planes), 2, 128], F32, name="gain_bank", tag="f")
+            for j, pl in enumerate(planes):
+                words = gain_rows[:, pl, :].bitcast(F32)
+                for u in range(2):
+                    nc.tensor.transpose(bank[:, j, u, :], words[:, u : u + 1].to_broadcast([128, 128]), ident[:])
+            return lambda: nc.vector.tensor_copy(
+                out=gains[:, planes[0] : planes[-1] + 1, :].bitcast(F32), in_=bank[:].rearrange("p j u m -> p j (u m)")
             )
 
-        d2s, xss, es, sums, recips, normed, grouped, quantised, fps, zs, zgs, zqs, ops, ts, sgs = ({} for i in range(15))
+        feat_words = [keep.tile([128, C], U32, name="feat_words%d" % pl, align_bytes=64) for pl in range(PLANES)]
+        feat_scales = [keep.tile([128, C], U8, name="feat_scales%d" % pl, align_bytes=64) for pl in range(PLANES)]
+
+        def feat_parts(pl):
+            widened = work.tile([128, 4, C], BF16, name="widened", bufs=PLANES)
+            side_by_side = work.tile([128, 4 * C], BF16, name="side_by_side", align_bytes=64)
+
+            def widen(j):
+                nc.vector.tensor_scalar(
+                    out=widened[:, j, :],
+                    in0=bytes_sb[pl][:, j, :].bitcast(FP8),
+                    scalar1=scale_sb[:, j : j + 1],
+                    scalar2=None,
+                    op0=ALU.mult,
+                )
+
+            def interleave(h):
+                nc.vector.tensor_copy(
+                    out=side_by_side[:].rearrange("p (t m j) -> p t m j", t=4, j=4)[:, 2 * h : 2 * h + 2],
+                    in_=widened[:].rearrange("p j (m t) -> p t m j", t=4)[:, 2 * h : 2 * h + 2],
+                )
+
+            def quantise():
+                nc.vector.quantize_mx(out=feat_words[pl][:].bitcast(FP8X4), scales=feat_scales[pl][:], in_=side_by_side[:])
+
+            return [lambda j=j: widen(j) for j in range(4)], [lambda h=h: interleave(h) for h in range(2)], [quantise]
+
+        squared, distance, scaled, expo, sums, recips, gained, weights = ({} for i in range(8))
+        turned, grouped, feature, partial, z_pair, linear_out, biased = ({} for i in range(7))
+
+        def square(q):
+            step, within = divmod(q, 8)
+            e, t = divmod(within, 4)
+            first, count, pl = steps[step]
+            if within == 0:
+                squared[step] = work.tile([128, 2, 4, count * 128], F32, name="squared", tag="squared%d" % count, bufs=3)
+            if step == 0:
+                coordinate = head_coords[e]
+            else:
+                h, start = divmod(128 * first, half)
+                coordinate = points[h][:, start : start + 128 * count, COORDS[pl][e]]
+            nc.scalar.activation(
+                out=squared[step][:, e, t, :],
+                in_=coordinate,
+                func=ACT.Square,
+                scale=-1.0,
+                bias=centres[:, pl, 2 * t + e : 2 * t + e + 1],
+            )
 
         def distances(k):
             step, pl, n = jobs[k]
             i = n - steps[step][0]
-            d2 = ps_d2.tile([128, 4, 128], F32, name="d2", tag="d2")
+            distance[k] = ps_d2.tile([128, 4, 128], F32, name="d2", tag="d2")
             for t in range(4):
                 for e in range(2):
                     nc.tensor.matmul(
-                        out=d2[:, t, :],
-                        lhsT=sq[step][:, e, t, 128 * i : 128 * i + 128],
+                        out=distance[k][:, t, :],
+                        lhsT=squared[step][:, e, t, 128 * i : 128 * i + 128],
                         rhs=ident[:],
                         start=(e == 0),
                         stop=(e == 1),
-                        is_transpose=not (e == 0 and t in PLAIN),
+                        is_transpose=not (e == 0 and t in MATMUL_BLOCKS),
                     )
-            d2s[k] = d2
 
         def minimum(k):
-            xs = work.tile([128, M], F32, name="xs", bufs=XB)
-            mn = work.tile([128, 1], F32, name="mn", bufs=XB)
+            values = work.tile([128, M], F32, name="values", bufs=3)
+            least = work.tile([128, 1], F32, name="least", bufs=3)
             nc.vector.tensor_scalar(
-                out=xs[:].rearrange("n (u p e) -> n u p e", u=2, e=2),
-                in0=d2s[k][:].rearrange("n (u e) p -> n u p e", u=2),
+                out=values[:].rearrange("n (u p e) -> n u p e", u=2, e=2),
+                in0=distance[k][:].rearrange("n (u e) p -> n u p e", u=2),
                 scalar1=1.0 / WIDTH2,
                 scalar2=None,
                 op0=ALU.mult,
                 op1=ALU.min,
-                accum_out=mn[:],
+                accum_out=least[:],
             )
-            xss[k] = (xs, mn)
+            scaled[k] = (values, least)
 
         def exponential(k):
-            xs, mn = xss[k]
-            e = work.tile([128, M], F32, name="e", bufs=EB)
-            if k // 2 not in sums:
-                sums[k // 2] = work.tile([128, 2], F32, name="sm", bufs=6)
+            values, least = scaled[k]
+            expo[k] = work.tile([128, M], F32, name="expo", bufs=12)
+            if k % 2 == 0:
+                sums[k // 2] = work.tile([128, 2], F32, name="sums", bufs=6)
             nc.scalar.activation(
-                out=e[:], in_=xs[:], func=ACT.Exp, scale=-1.0, bias=mn[:], accum_out=sums[k // 2][:, k % 2 : k % 2 + 1]
+                out=expo[k][:],
+                in_=values[:],
+                func=ACT.Exp,
+                scale=-1.0,
+                bias=least[:],
+                accum_out=sums[k // 2][:, k % 2 : k % 2 + 1],
             )
-            es[k] = e
 
         def reciprocal(r):
-            recips[r] = work.tile([128, 2], F32, name="ri")
+            recips[r] = work.tile([128, 2], F32, name="recips")
             nc.vector.reciprocal(out=recips[r][:], in_=sums[r][:])
 
-        weighted = {}
-
         def gain_on_pool(k, spent):
-            nc.gpsimd.tensor_tensor(out=spent[:], in0=es[k][:], in1=gab[:, job(k)[1], :], op=ALU.mult)
-            weighted[k] = spent
+            nc.gpsimd.tensor_tensor(out=spent, in0=expo[k][:], in1=gains[:, jobs[k][1], :], op=ALU.mult)
+            gained[k] = spent
 
         def normalise(k):
-            pl = job(k)[1]
-            a = work.tile([128, M], BF16, name="a", bufs=4)
-            normed[k] = a
-            if k in weighted:
-                nc.vector.tensor_scalar(
-                    out=a[:], in0=weighted[k][:], scalar1=recips[k // 2][:, k % 2 : k % 2 + 1], scalar2=None, op0=ALU.mult
+            weights[k] = work.tile([128, M], BF16, name="weights", bufs=4)
+            factor = recips[k // 2][:, k % 2 : k % 2 + 1]
+            if k in gained:
+                nc.vector.tensor_scalar(out=weights[k][:], in0=gained[k], scalar1=factor, scalar2=None, op0=ALU.mult)
+            else:
+                nc.vector.scalar_tensor_tensor(
+                    out=weights[k][:],
+                    in0=expo[k][:],
+                    scalar=factor,
+                    in1=gains[:, jobs[k][1], :],
+                    op0=ALU.mult,
+                    op1=ALU.mult,
                 )
-                return
-            nc.vector.scalar_tensor_tensor(
-                out=a[:],
-                in0=es[k][:],
-                scalar=recips[k // 2][:, k % 2 : k % 2 + 1],
-                in1=gab[:, pl, :],
-                op0=ALU.mult,
-                op1=ALU.mult,
-            )
-            normed[k] = a
 
         def turn(r):
-            xt = ps_xt.tile([128, 2, 2, 128], F32, name="xt", tag="xt")
+            turned[r] = ps_xt.tile([128, 2, 2, 128], F32, name="turned", tag="xt")
             for j in range(2):
-                words = normed[2 * r + j][:].bitcast(F32)
+                words = weights[2 * r + j][:].bitcast(F32)
                 for u in range(2):
-                    nc.tensor.transpose(xt[:, j, u, :], words[:, 128 * u : 128 * u + 128], ident[:])
-            grouped[r] = xt
+                    nc.tensor.transpose(turned[r][:, j, u, :], words[:, 128 * u : 128 * u + 128], ident[:])
 
         def copy_out(r, copy):
-            g = work.tile([128, 256 * 4], BF16, name="g", align_bytes=64, bufs=GB)
+            grouped[r] = work.tile([128, 256 * 4], BF16, name="grouped", align_bytes=64, bufs=3)
             copy(
-                out=g[:].bitcast(F32).rearrange("p (j n u) -> p j n u", j=2, u=2),
-                in_=grouped[r][:].rearrange("p j u n -> p j n u"),
+                out=grouped[r][:].bitcast(F32).rearrange("p (j n u) -> p j n u", j=2, u=2),
+                in_=turned[r][:].rearrange("p j u n -> p j n u"),
             )
-            grouped[r] = g
 
-        def quantise_a(r):
-            aw = work.tile([128, 256], U32, name="aw", align_bytes=64)
-            asc = work.tile([128, 256], U8, name="asc", align_bytes=64)
-            nc.vector.quantize_mx(out=aw[:].bitcast(FP8X4), scales=asc[:], in_=grouped[r][:])
-            quantised[r] = (aw, asc)
-
-        def plane_product(k, pool=ps_f, tag="f"):
-            aw, asc = quantised[k // 2]
-            pl = job(k)[1]
-            cols = slice(128 * (k % 2), 128 * (k % 2) + 128)
-            if k // 2 in ON_SCALAR:
-                f = pool.tile([128, 2, 256], F32, name="f", tag=tag)
-                for h in range(2):
-                    t = 2 * (k % 2) + h
+        def products(r, pool, tag):
+            words = work.tile([128, 256], U32, name="a_words", align_bytes=64)
+            scales = work.tile([128, 256], U8, name="a_scales", align_bytes=64)
+            nc.vector.quantize_mx(out=words[:].bitcast(FP8X4), scales=scales[:], in_=grouped[r][:])
+            for k in (2 * r, 2 * r + 1):
+                pl = jobs[k][1]
+                cols = slice(128 * (k % 2), 128 * (k % 2) + 128)
+                feature[k] = pool.tile([128, 4, 128], F32, name="feature", tag=tag)
+                for t in range(4):
                     nc.tensor.matmul_mx(
-                        out=f[:, h, :],
-                        lhsT=fw[pl][:, 128 * t : 128 * t + 128].bitcast(FP8X4),
-                        lhsT_scale=fsc[pl][:, 128 * t : 128 * t + 128],
-                        rhs=aw[:].bitcast(FP8X4),
-                        rhs_scale=asc[:],
+                        out=feature[k][:, t, :],
+                        lhsT=feat_words[pl][:, 128 * t : 128 * t + 128].bitcast(FP8X4),
+                        lhsT_scale=feat_scales[pl][:, 128 * t : 128 * t + 128],
+                        rhs=words[:, cols].bitcast(FP8X4),
+                        rhs_scale=scales[:, cols],
                         start=True,
                         stop=True,
                     )
-                fps[k] = f
-                return
-            f = pool.tile([128, 4, 128], F32, name="f", tag=tag)
-            for t in range(4):
+
+        def multiply(k):
+            step, pl, n = jobs[k]
+            other = channel_gain[:].unsqueeze(1).to_broadcast([128, 128, 4]) if pl == 0 else partial[n][:]
+            if pl < PLANES - 1:
+                partial[n] = work.tile([128, 128, 4], F32, name="partial", bufs=EARLY_TILES + 1)
+                result = partial[n][:]
+            else:
+                if n % 2 == 0:
+                    z_pair[n // 2] = work.tile([128, 2, 128, 4], BF16, name="z_pair", align_bytes=64)
+                result = z_pair[n // 2][:, n % 2]
+            nc.vector.tensor_tensor(out=result, in0=feature[k][:].rearrange("p t n -> p n t"), in1=other, op=ALU.mult)
+
+        def linear(n):
+            words = work.tile([128, 256], U32, name="z_words", align_bytes=64)
+            scales = work.tile([128, 256], U8, name="z_scales", align_bytes=64)
+            nc.vector.quantize_mx(
+                out=words[:].bitcast(FP8X4), scales=scales[:], in_=z_pair[n // 2][:].rearrange("p j n t -> p (j n t)")
+            )
+            for j in range(2):
+                linear_out[n - 1 + j] = ps_o.tile([128, H], F32, name="linear_out", tag="o")
                 nc.tensor.matmul_mx(
-                    out=f[:, t, :],
-                    lhsT=fw[pl][:, 128 * t : 128 * t + 128].bitcast(FP8X4),
-                    lhsT_scale=fsc[pl][:, 128 * t : 128 * t + 128],
-                    rhs=aw[:, cols].bitcast(FP8X4),
-                    rhs_scale=asc[:, cols],
+                    out=linear_out[n - 1 + j][:],
+                    lhsT=words[:, 128 * j : 128 * j + 128].bitcast(FP8X4),
+                    lhsT_scale=scales[:, 128 * j : 128 * j + 128],
+                    rhs=w_words[:].bitcast(FP4X4),
+                    rhs_scale=w_scales[:],
                     start=True,
                     stop=True,
                 )
-            fps[k] = f
 
-        gained = {}
-
-        def multiply(k):
-            step, pl, n = job(k)
-            if k // 2 in ON_SCALAR:
-                if n // 2 not in gained:
-                    gained[n // 2] = work.tile([128, 4, 256], F32, name="gained")
-                    for j in range(2):
-                        zs[n - n % 2 + j] = gained[n // 2][:, :, 128 * j : 128 * j + 128].rearrange("p t n -> p n t")
-                for h in range(2):
-                    t = 2 * (k % 2) + h
-                    nc.scalar.activation(
-                        out=gained[n // 2][:, t, :], in_=fps[k][:, h, :], func=ACT.Copy, scale=gcf[:, t : t + 1]
-                    )
-                return
-            f = fps[k][:].rearrange("p t n -> p n t")
-            if pl == 0:
-                other = gcb[:].unsqueeze(1).to_broadcast([128, 128, 4])
-            else:
-                other = zs[n]
-            if pl < PLANES - 1:
-                z = work.tile([128, 128, 4], F32, name="z", bufs=FIRST + 1)
-                zs[n] = z[:]
-                dst = zs[n]
-            else:
-                if n // 2 not in zgs:
-                    zgs[n // 2] = work.tile([128, 2, 128, 4], BF16, name="zg", align_bytes=64)
-                dst = zgs[n // 2][:, n % 2]
-            nc.vector.tensor_tensor(out=dst, in0=f, in1=other, op=ALU.mult)
-
-        def quantise_z(r):
-            zw = work.tile([128, 256], U32, name="zw", align_bytes=64)
-            zsc = work.tile([128, 256], U8, name="zsc", align_bytes=64)
-            nc.vector.quantize_mx(
-                out=zw[:].bitcast(FP8X4), scales=zsc[:], in_=zgs[r][:].rearrange("p j n t -> p (j n t)")
-            )
-            zqs[r] = (zw, zsc)
-
-        def linear(n):
-            zw, zsc = zqs[n // 2]
-            cols = slice(128 * (n % 2), 128 * (n % 2) + 128)
-            o = ps_o.tile([128, H], F32, name="o", tag="o")
-            nc.tensor.matmul_mx(
-                out=o[:],
-                lhsT=zw[:, cols].bitcast(FP8X4),
-                lhsT_scale=zsc[:, cols],
-                rhs=ww[:].bitcast(FP4X4),
-                rhs_scale=ws[:],
-                start=True,
-                stop=True,
-            )
-            ops[n] = o
-
-        lall = keep.tile([128, TILES, H], F32, name="lall")
+        sums_b = keep.tile([128, TILES, H], F32, name="sums_b")
+        result_sb = keep.tile([128, TILES, H], F32, name="result_sb")
+        out_tiles = out.rearrange("(j p) h -> p j h", p=128)
+        unloaded = []
 
         def bias(n):
-            ts[n] = keep.tile([128, H], F32, name="t%d" % n)
-            nc.vector.tensor_tensor(out=ts[n][:], in0=ops[n][:], in1=bb[:], op=ALU.add)
-
-        def unload(n):
-            nc.scalar.copy(out=lall[:, n, :], in_=ops[n][:])
+            if n < POOL_BIAS_TILES:
+                nc.scalar.copy(out=result_sb[:, n, :], in_=linear_out[n][:])
+                unloaded.append(n)
+            else:
+                nc.vector.tensor_tensor(out=sums_b[:, n, :], in0=linear_out[n][:], in1=bias_row[:], op=ALU.add)
 
         def bias_on_pool(n, spent):
-            nc.gpsimd.tensor_tensor(out=spent[:], in0=lall[:, n, :], in1=bb[:], op=ALU.add)
-            ts[n] = spent
+            nc.gpsimd.tensor_tensor(out=spent, in0=result_sb[:, n, :], in1=bias_row[:], op=ALU.add)
+            biased[n] = spent.unsqueeze(1)
+
+        def with_bias(n, count):
+            return biased[n] if n in biased else sums_b[:, n : n + count, :]
 
         def sigmoid(n, count):
-            for j in range(n, n + count):
-                nc.scalar.activation(out=lall[:, j, :], in_=ts[j][:], func=ACT.Sigmoid, scale=-1.0)
-
-        out_tiles = out.rearrange("(j p) h -> p j h", p=128)
+            nc.scalar.activation(out=result_sb[:, n : n + count, :], in_=with_bias(n, count), func=ACT.Sigmoid, scale=-1.0)
 
         def logarithm(n, count):
-            nc.scalar.activation(out=lall[:, n : n + count, :], in_=lall[:, n : n + count, :], func=ACT.Ln, bias=TINY)
-
-        def last_logarithm(n, h):
-            cols = slice(h * H // 2, (h + 1) * H // 2)
-            nc.scalar.activation(out=lall[:, n, cols], in_=lall[:, n, cols], func=ACT.Ln, bias=TINY)
-            nc.vector.scalar_tensor_tensor(
-                out=lall[:, n, cols], in0=lall[:, n, cols], scalar=-1.0, in1=ts[n][:, cols], op0=ALU.mult, op1=ALU.max
-            )
-            nc.sync.dma_start(out=out_tiles[:, n, cols], in_=lall[:, n, cols])
+            part = result_sb[:, n : n + count, :]
+            nc.scalar.activation(out=part, in_=part, func=ACT.Ln, bias=TINY)
 
         def finish(n, count):
-            for j in range(n, n + count):
-                nc.vector.scalar_tensor_tensor(
-                    out=lall[:, j, :], in0=lall[:, j, :], scalar=-1.0, in1=ts[j][:], op0=ALU.mult, op1=ALU.max
-                )
-            nc.sync.dma_start(out=out_tiles[:, n : n + count, :], in_=lall[:, n : n + count, :])
+            part = result_sb[:, n : n + count, :]
+            nc.vector.scalar_tensor_tensor(
+                out=part, in0=part, scalar=-1.0, in1=with_bias(n, count), op0=ALU.mult, op1=ALU.max
+            )
+            nc.sync.dma_start(out=out_tiles[:, n : n + count, :], in_=part)
 
         spread_points(0)
         spread_points(1)
-        eng = [nc.scalar.copy if x == "s" else nc.vector.tensor_copy for x in KEEP]
-        spare = [spread_gains([0, 1], eng[0]), spread_gains([2], eng[1])]
-        first, second, third = feat_parts(0, 0, 0), feat_parts(1, W1, I1), feat_parts(2, W2, I2)
-        for part in first[:4] + second[:4] + first[4:6]:
+        keep_gains = [spread_gains([0, 1]), spread_gains([2])]
+        (widen0, inter0, quant0), (widen1, inter1, quant1), (widen2, inter2, quant2) = map(feat_parts, range(PLANES))
+        for part in widen0 + widen1 + inter0:
             part()
         for q in range(8):
             square(q)
-        if ON_SCALAR:
-            nc.vector.tensor_copy(out=gcf[:], in_=gcb[:])
-        filler = second[4:5] + first[6:] + second[5:6] + third[:4] + second[6:] + third[4:]
-        for x in range(HEADF):
-            filler.pop(0)()
-        squares = list(range(8, 8 * len(steps)))
-        front = list(range(JOBS))
-        waiting = []
-        budget = [0.0]
+        feat_left = inter1[:1] + quant0 + inter1[1:] + widen2 + inter2 + quant1 + quant2
+        squares_left = list(range(8, 8 * len(steps)))
+        jobs_left = list(range(JOBS))
+        budget = []
 
-        def next_squares(columns):
-            budget[0] = budget[0] + columns
-            while squares and budget[0] > 0:
-                q = squares.pop(0)
-                budget[0] = budget[0] - steps[q // 8][1] - 0.5
+        def more_feat(count):
+            for part in feat_left[:count]:
+                part()
+                feat_left.remove(part)
+
+        def more_squares(widths):
+            budget.append(widths)
+            while squares_left and sum(budget) > 0:
+                q = squares_left.pop(0)
+                budget.append(-steps[q // 8][1] - 0.5)
                 square(q)
 
-        def next_minimum():
-            if front:
-                i = front.pop(0)
-                if i + AHEAD < JOBS:
-                    while squares and squares[0] // 8 <= job(i + AHEAD)[0]:
-                        next_squares(1)
-                    distances(i + AHEAD)
-                minimum(i)
-                exponential(i)
-
-        def fill(count):
-            for x in range(min(count, len(filler))):
-                filler.pop(0)()
+        def next_job():
+            if jobs_left:
+                k = jobs_left.pop(0)
+                if k + 2 < JOBS:
+                    while squares_left and squares_left[0] // 8 <= jobs[k + 2][0]:
+                        more_squares(1)
+                    distances(k + 2)
+                minimum(k)
+                exponential(k)
 
         def last_plane(k):
-            return 0 <= k < JOBS and job(k)[1] == PLANES - 1
+            return k >= 0 and jobs[k][1] == PLANES - 1
 
-        for i in range(AHEAD):
-            distances(i)
-        next_squares(LEAD)
-        unloaded = []
+        more_feat(FEAT_AHEAD)
+        distances(0)
+        distances(1)
+        more_squares(SQUARES_AHEAD)
 
-        def spent_g(r):
-            return grouped[r][:].bitcast(F32)
-
-        def leave_bank(n):
-            if n < PBIAS:
-                unload(n)
-                unloaded.append(n)
-            else:
-                bias(n)
-
-        wide = PLANES * FIRST // 2
-        for r in range(wide + 3):
-            next_minimum()
-            if 1 <= r <= wide:
+        last = EARLY_PAIRS + 2
+        for r in range(last + 1):
+            filling = r <= 2
+            next_job()
+            if r >= 1:
                 reciprocal(r - 1)
-            if 2 <= r <= wide + 1:
-                copy_out(r - 2, nc.scalar.copy if r - 2 >= VCO0 else nc.vector.tensor_copy)
-            if 3 <= r:
+            if 3 <= r < last:
+                copy_out(r - 2, nc.scalar.copy)
+            if not filling:
                 multiply(2 * r - 6)
             if last_plane(2 * r - 8):
-                leave_bank(job(2 * r - 8)[2])
-            fill(FILL)
-            if spare:
-                spare.pop(0)()
-            next_minimum()
-            if 3 <= r:
+                bias(jobs[2 * r - 8][2])
+            between = SQUARES_BETWEEN if filling else 0
+            more_squares(between)
+            more_feat(FEAT_A_MINIMUM)
+            if keep_gains:
+                keep_gains.pop(0)()
+            if r == 2:
+                copy_out(0, nc.vector.tensor_copy)
+            next_job()
+            if not filling:
                 multiply(2 * r - 5)
             if last_plane(2 * r - 7):
-                leave_bank(job(2 * r - 7)[2])
-            fill(FILL)
-            if 2 <= r <= wide + 1:
-                quantise_a(r - 2)
-                flat = [None, spent_g(r - 2), es.get(2 * wide - 4)]
-                plane_product(2 * r - 4)
-                plane_product(2 * r - 3)
-            if r >= HURRY:
-                next_minimum()
+                bias(jobs[2 * r - 7][2])
+            more_feat(FEAT_A_MINIMUM)
+            if 2 <= r < last:
+                products(r - 2, ps_f, "f")
+            if r == last - 1:
+                next_job()
+                gain_later = grouped[r - 2][:].bitcast(F32)
+            if r == last:
+                normalise(2 * EARLY_PAIRS)
+                normalise(2 * EARLY_PAIRS + 1)
             if last_plane(2 * r - 5):
-                n = job(2 * r - 5)[2]
-                quantise_z(n // 2)
-                linear(n - 1)
-                linear(n)
-            if 1 <= r <= wide:
+                linear(jobs[2 * r - 5][2])
+            if r == last:
+                turn(EARLY_PAIRS)
+            if 1 <= r <= EARLY_PAIRS:
                 normalise(2 * r - 1)
                 normalise(2 * r - 2)
                 turn(r - 1)
+                spent = [gained.get(k, expo[k][:]) for k in (2 * r - 2, 2 * r - 1)]
                 if unloaded:
-                    bias_on_pool(unloaded.pop(0), es[2 * r - 2])
-                elif r in POOL:
-                    gain_on_pool(2 * r + 1, es[2 * r - 2])
-            if r == wide and PTAIL >= 1:
-                gain_on_pool(2 * wide, es[2 * r - 2])
-            if r == wide + 1:
-                for j in range(1, PTAIL):
-                    gain_on_pool(2 * wide + j, flat[j])
-            next_squares(RATE)
+                    for buffer in spent:
+                        bias_on_pool(unloaded.pop(0), buffer)
+                elif r >= 2:
+                    gain_on_pool(2 * r + 1, spent[0])
+            if r == last - 1:
+                gain_on_pool(2 * r, gain_later)
+            more_squares(SQUARES_A_TURN - between)
 
-        def weights(r):
-            normalise(2 * r)
-            normalise(2 * r + 1)
-            turn(r)
-
-        def products(r, pool, tag):
-            quantise_a(r)
-            plane_product(2 * r, pool, tag)
-            plane_product(2 * r + 1, pool, tag)
-
-        reciprocal(wide)
-        reciprocal(wide + 1)
-        sigmoid(0, 2)
-        weights(wide)
-        bias(FIRST - 2)
-        bias(FIRST - 1)
-        copy_out(wide, nc.scalar.copy)
-        sigmoid(2, 2)
-        reciprocal(wide + 2)
-        weights(wide + 1)
-        products(wide, ps_f, "f")
-        copy_out(wide + 1, nc.scalar.copy)
-        sigmoid(4, 2)
-        weights(wide + 2)
-        multiply(2 * wide)
-        products(wide + 1, ps_d2, "d2")
-        multiply(2 * wide + 1)
-        if not VCO:
-            copy_out(wide + 2, nc.scalar.copy)
+        first_pair, second_pair, third_pair = range(EARLY_PAIRS, EARLY_PAIRS + PLANES)
+        for n in range(EARLY_TILES // 2):
+            sigmoid(n, 1)
+        reciprocal(third_pair)
+        normalise(2 * second_pair + 1)
+        bias(EARLY_TILES - 2)
+        bias(EARLY_TILES - 1)
+        copy_out(first_pair, nc.scalar.copy)
+        normalise(2 * second_pair)
+        turn(second_pair)
+        normalise(2 * third_pair)
+        products(first_pair, ps_f, "f")
+        sigmoid(EARLY_TILES // 2, EARLY_TILES // 2)
+        copy_out(second_pair, nc.scalar.copy)
+        normalise(2 * third_pair + 1)
+        turn(third_pair)
+        multiply(2 * first_pair)
+        products(second_pair, ps_d2, "d2")
+        multiply(2 * first_pair + 1)
         logarithm(0, 2)
-        if VCO:
-            copy_out(wide + 2, nc.vector.tensor_copy)
+        copy_out(third_pair, nc.vector.tensor_copy)
         logarithm(2, 2)
-        multiply(2 * wide + 2)
+        multiply(2 * second_pair)
         logarithm(4, 2)
-        multiply(2 * wide + 3)
-        products(wide + 2, ps_f, "f")
+        products(third_pair, ps_f, "f")
+        multiply(2 * second_pair + 1)
+        multiply(2 * third_pair)
+        multiply(2 * third_pair + 1)
         finish(0, 1)
-        multiply(2 * wide + 4)
-        multiply(2 * wide + 5)
-        quantise_z(FIRST // 2)
-        linear(FIRST)
-        linear(FIRST + 1)
+        linear(TILES - 1)
         finish(1, 1)
-        for n in range(FIRST, TILES):
+        for n in range(EARLY_TILES, TILES):
             bias(n)
             sigmoid(n, 1)
         finish(2, 2)
         finish(4, 2)
-        if HALVES:
-            logarithm(FIRST, 1)
-            finish(FIRST, 1)
-            for h in range(2):
-                last_logarithm(FIRST + 1, h)
-        else:
-            for n in range(FIRST, TILES):
-                logarithm(n, 1)
-                finish(n, 1)
+        for n in range(EARLY_TILES, TILES):
+            logarithm(n, 1)
+            finish(n, 1)

@@ -46,11 +46,11 @@ def tile_kplanesgaussiananchordecoder_w4_kernel(
 
         head_tiles = CHUNKS[0][1]
         head_points = keep.tile([128, head_tiles, 4], BF16, name="head_points")
-        nc.sync.dma_start(
+        nc.scalar.dma_start(
             out=head_points[:, :, 0:3], in_=pts[0 : 128 * head_tiles, :].rearrange("(j p) x -> p j x", p=128)
         )
         scale_sb = keep.tile([128, 4], F32, name="scale_sb")
-        nc.scalar.dma_start(out=scale_sb[:], in_=feat_scale.rearrange("o (p t) x -> p (o t x)", t=4))
+        nc.sync.dma_start(out=scale_sb[:], in_=feat_scale.rearrange("o (p t) x -> p (o t x)", t=4))
         bytes_sb = [keep.tile([128, 4, C], U8, name="bytes_sb%d" % pl) for pl in range(PLANES)]
 
         def load_feat(pl, lo, hi):
@@ -240,7 +240,7 @@ def tile_kplanesgaussiananchordecoder_w4_kernel(
                     nc.tensor.transpose(turned[r][:, j, u, :], words[:, 128 * u : 128 * u + 128], ident[:])
 
         def copy_out(r, copy):
-            grouped[r] = work.tile([128, 256 * 4], BF16, name="grouped", align_bytes=64, bufs=3)
+            grouped[r] = work.tile([128, 256 * 4], BF16, name="grouped", align_bytes=64)
             copy(
                 out=grouped[r][:].bitcast(F32).rearrange("p (j n u) -> p j n u", j=2, u=2),
                 in_=turned[r][:].rearrange("p j u n -> p j n u"),
@@ -377,6 +377,10 @@ def tile_kplanesgaussiananchordecoder_w4_kernel(
             next_job()
             if r >= 1:
                 reciprocal(r - 1)
+            if r == last:
+                normalise(2 * EARLY_PAIRS)
+                normalise(2 * EARLY_PAIRS + 1)
+                turn(EARLY_PAIRS)
             if 3 <= r < last:
                 copy_out(r - 2, nc.scalar.copy)
             if not filling:
@@ -400,14 +404,11 @@ def tile_kplanesgaussiananchordecoder_w4_kernel(
                 products(r - 2, ps_f, "f")
             if r == last - 1:
                 next_job()
-                gain_later = grouped[r - 2][:].bitcast(F32)
             if r == last:
-                normalise(2 * EARLY_PAIRS)
-                normalise(2 * EARLY_PAIRS + 1)
+                reciprocal(r)
+                normalise(2 * EARLY_PAIRS + 2)
             if last_plane(2 * r - 5):
                 linear(jobs[2 * r - 5][2])
-            if r == last:
-                turn(EARLY_PAIRS)
             if 1 <= r <= EARLY_PAIRS:
                 normalise(2 * r - 1)
                 normalise(2 * r - 2)
@@ -418,24 +419,21 @@ def tile_kplanesgaussiananchordecoder_w4_kernel(
                         bias_on_pool(unloaded.pop(0), buffer)
                 elif r >= 2:
                     gain_on_pool(2 * r + 1, spent[0])
-            if r == last - 1:
-                gain_on_pool(2 * r, gain_later)
             more_squares(SQUARES_A_TURN - between)
 
         first_pair, second_pair, third_pair = range(EARLY_PAIRS, EARLY_PAIRS + PLANES)
-        for n in range(EARLY_TILES // 2):
-            sigmoid(n, 1)
-        reciprocal(third_pair)
+        sigmoid(0, 1)
+        copy_out(first_pair, nc.scalar.copy)
+        sigmoid(1, 1)
+        sigmoid(2, 2)
         normalise(2 * second_pair + 1)
+        turn(second_pair)
+        products(first_pair, ps_f, "f")
         bias(EARLY_TILES - 2)
         bias(EARLY_TILES - 1)
-        copy_out(first_pair, nc.scalar.copy)
-        normalise(2 * second_pair)
-        turn(second_pair)
-        normalise(2 * third_pair)
-        products(first_pair, ps_f, "f")
-        sigmoid(EARLY_TILES // 2, EARLY_TILES // 2)
         copy_out(second_pair, nc.scalar.copy)
+        sigmoid(4, 2)
+        normalise(2 * third_pair)
         normalise(2 * third_pair + 1)
         turn(third_pair)
         multiply(2 * first_pair)

@@ -26,7 +26,7 @@ CHUNKS = ((0, 4), (4, 2), (6, 2))
 EARLY_TILES = CHUNKS[-1][0]
 EARLY_PAIRS = PLANES * EARLY_TILES // 2
 MATMUL_BLOCKS = (0, 3)
-SQUARES_A_TURN, SQUARES_AHEAD, SQUARES_BETWEEN = 18, 10, 10
+WIDE_SQUARES_AHEAD, WIDE_SQUARES_A_JOB, NARROW_SQUARES_A_TURN = 3, 2, 7
 FEAT_AHEAD, FEAT_A_MINIMUM = 3, 2
 POOL_BIAS_TILES = 2
 
@@ -58,7 +58,7 @@ def tile_kplanesgaussiananchordecoder_w4_kernel(
             nc.sync.dma_start(out=bytes_sb[pl][:, lo:hi, :], in_=rows[:, lo:hi, :])
 
         centres = keep.tile([128, PLANES, 8], BF16, name="centres")
-        nc.scalar.dma_start(out=centres[:], in_=cen.rearrange("x (p t) e -> p x (t e)", t=4))
+        nc.scalar.dma_start(out=centres[:], in_=cen.rearrange("x (p t) axis -> p x (t axis)", t=4))
         load_feat(0, 0, 2)
         load_feat(0, 2, 4)
         gain_rows = keep.tile([128, PLANES, 4], BF16, name="gain_rows")
@@ -82,10 +82,9 @@ def tile_kplanesgaussiananchordecoder_w4_kernel(
         nc.sync.dma_start(out=w_words[:], in_=w1_words[0])
         w_scales = keep.tile([128, H], U8, name="w_scales", align_bytes=64)
         nc.vector.memset(w_scales[:].bitcast(I32), 0)
-        for q in range(4):
-            nc.sync.dma_start(
-                out=w_scales[32 * q : 32 * q + 4, :].bitcast(I32), in_=w1_scales[0, 4 * q : 4 * q + 4, :].bitcast(I32)
-            )
+        for quad in range(4):
+            rows = w1_scales[0, 4 * quad : 4 * quad + 4, :]
+            nc.sync.dma_start(out=w_scales[32 * quad : 32 * quad + 4, :].bitcast(I32), in_=rows.bitcast(I32))
         bias_row = keep.tile([128, H], BF16, name="bias_row")
         nc.sync.dma_start(out=bias_row[:], in_=b1.partition_broadcast(128))
 
@@ -140,7 +139,8 @@ def tile_kplanesgaussiananchordecoder_w4_kernel(
                 )
 
             def quantise():
-                nc.vector.quantize_mx(out=feat_words[pl][:].bitcast(FP8X4), scales=feat_scales[pl][:], in_=side_by_side[:])
+                codes = feat_words[pl][:].bitcast(FP8X4)
+                nc.vector.quantize_mx(out=codes, scales=feat_scales[pl][:], in_=side_by_side[:])
 
             return [lambda j=j: widen(j) for j in range(4)], [lambda h=h: interleave(h) for h in range(2)], [quantise]
 
@@ -149,21 +149,21 @@ def tile_kplanesgaussiananchordecoder_w4_kernel(
 
         def square(q):
             step, within = divmod(q, 8)
-            e, t = divmod(within, 4)
+            axis, t = divmod(within, 4)
             first, count, pl = steps[step]
             if within == 0:
                 squared[step] = work.tile([128, 2, 4, count * 128], F32, name="squared", tag="squared%d" % count, bufs=3)
             if step == 0:
-                coordinate = head_coords[e]
+                coordinate = head_coords[axis]
             else:
                 h, start = divmod(128 * first, half)
-                coordinate = points[h][:, start : start + 128 * count, COORDS[pl][e]]
+                coordinate = points[h][:, start : start + 128 * count, COORDS[pl][axis]]
             nc.scalar.activation(
-                out=squared[step][:, e, t, :],
+                out=squared[step][:, axis, t, :],
                 in_=coordinate,
                 func=ACT.Square,
                 scale=-1.0,
-                bias=centres[:, pl, 2 * t + e : 2 * t + e + 1],
+                bias=centres[:, pl, 2 * t + axis : 2 * t + axis + 1],
             )
 
         def distances(k):
@@ -171,14 +171,14 @@ def tile_kplanesgaussiananchordecoder_w4_kernel(
             i = n - steps[step][0]
             distance[k] = ps_d2.tile([128, 4, 128], F32, name="d2", tag="d2")
             for t in range(4):
-                for e in range(2):
+                for axis in range(2):
                     nc.tensor.matmul(
                         out=distance[k][:, t, :],
-                        lhsT=squared[step][:, e, t, 128 * i : 128 * i + 128],
+                        lhsT=squared[step][:, axis, t, 128 * i : 128 * i + 128],
                         rhs=ident[:],
-                        start=(e == 0),
-                        stop=(e == 1),
-                        is_transpose=not (e == 0 and t in MATMUL_BLOCKS),
+                        start=(axis == 0),
+                        stop=(axis == 1),
+                        is_transpose=not (axis == 0 and t in MATMUL_BLOCKS),
                     )
 
         def minimum(k):
@@ -315,7 +315,8 @@ def tile_kplanesgaussiananchordecoder_w4_kernel(
             return biased[n] if n in biased else sums_b[:, n : n + count, :]
 
         def sigmoid(n, count):
-            nc.scalar.activation(out=result_sb[:, n : n + count, :], in_=with_bias(n, count), func=ACT.Sigmoid, scale=-1.0)
+            part = result_sb[:, n : n + count, :]
+            nc.scalar.activation(out=part, in_=with_bias(n, count), func=ACT.Sigmoid, scale=-1.0)
 
         def logarithm(n, count):
             part = result_sb[:, n : n + count, :]
@@ -339,19 +340,16 @@ def tile_kplanesgaussiananchordecoder_w4_kernel(
         feat_left = inter1[:1] + quant0 + inter1[1:] + widen2 + inter2 + quant1 + quant2
         squares_left = list(range(8, 8 * len(steps)))
         jobs_left = list(range(JOBS))
-        budget = []
 
         def more_feat(count):
             for part in feat_left[:count]:
                 part()
                 feat_left.remove(part)
 
-        def more_squares(widths):
-            budget.append(widths)
-            while squares_left and sum(budget) > 0:
-                q = squares_left.pop(0)
-                budget.append(-steps[q // 8][1] - 0.5)
+        def more_squares(count):
+            for q in squares_left[:count]:
                 square(q)
+                squares_left.remove(q)
 
         def next_job():
             if jobs_left:
@@ -369,7 +367,7 @@ def tile_kplanesgaussiananchordecoder_w4_kernel(
         more_feat(FEAT_AHEAD)
         distances(0)
         distances(1)
-        more_squares(SQUARES_AHEAD)
+        more_squares(WIDE_SQUARES_AHEAD)
 
         last = EARLY_PAIRS + 2
         for r in range(last + 1):
@@ -387,8 +385,8 @@ def tile_kplanesgaussiananchordecoder_w4_kernel(
                 multiply(2 * r - 6)
             if last_plane(2 * r - 8):
                 bias(jobs[2 * r - 8][2])
-            between = SQUARES_BETWEEN if filling else 0
-            more_squares(between)
+            if filling:
+                more_squares(WIDE_SQUARES_A_JOB)
             more_feat(FEAT_A_MINIMUM)
             if keep_gains:
                 keep_gains.pop(0)()
@@ -419,7 +417,7 @@ def tile_kplanesgaussiananchordecoder_w4_kernel(
                         bias_on_pool(unloaded.pop(0), buffer)
                 elif r >= 2:
                     gain_on_pool(2 * r + 1, spent[0])
-            more_squares(SQUARES_A_TURN - between)
+            more_squares(WIDE_SQUARES_A_JOB if filling else NARROW_SQUARES_A_TURN)
 
         first_pair, second_pair, third_pair = range(EARLY_PAIRS, EARLY_PAIRS + PLANES)
         sigmoid(0, 1)

@@ -23,12 +23,14 @@ JOBS = TILES * PLANES
 TINY = 2.0**-60
 
 CHUNKS = ((0, 4), (4, 2), (6, 2))
-EARLY_TILES = CHUNKS[-1][0]
-EARLY_PAIRS = PLANES * EARLY_TILES // 2
 MATMUL_BLOCKS = (0, 3)
-WIDE_SQUARES_AHEAD, WIDE_SQUARES_A_JOB, NARROW_SQUARES_A_TURN = 3, 2, 7
-FEAT_AHEAD, FEAT_A_MINIMUM = 3, 2
-POOL_BIAS_TILES = 2
+FEAT_AHEAD = 13
+FEAT_A_SLOT = 2
+SQUARES_AHEAD = 3
+MARGIN = 0
+MODES = "VVAAAWAWAWAWAWAWAWAWAWXX"
+POOL_BIAS = ()
+TAILV = 0
 
 
 def tile_kplanesgaussiananchordecoder_w4_kernel(
@@ -38,8 +40,8 @@ def tile_kplanesgaussiananchordecoder_w4_kernel(
     with ExitStack() as ctx:
         keep = ctx.enter_context(tc.tile_pool(name="keep", bufs=1))
         work = ctx.enter_context(tc.tile_pool(name="work", bufs=2))
-        ps_d2 = ctx.enter_context(tc.psum_pool(name="ps_d2", bufs=3))
-        ps_xt = ctx.enter_context(tc.psum_pool(name="ps_xt", bufs=1))
+        ps_d2 = ctx.enter_context(tc.psum_pool(name="ps_d2", bufs=2))
+        ps_xt = ctx.enter_context(tc.psum_pool(name="ps_xt", bufs=2))
         ps_f = ctx.enter_context(tc.psum_pool(name="ps_f", bufs=2))
         ps_o = ctx.enter_context(tc.psum_pool(name="ps_o", bufs=2))
         ctx.enter_context(tc.manual_schedule())
@@ -75,6 +77,10 @@ def tile_kplanesgaussiananchordecoder_w4_kernel(
 
         load_points(0)
         load_feat(2, 0, 4)
+        gain_all = keep.tile([128, PLANES, M], BF16, name="gain_all")
+        nc.sync.dma_start(
+            out=gain_all[:].rearrange("n x m -> n (x m)"), in_=ga.rearrange("x m -> (x m)").partition_broadcast(128)
+        )
         load_points(1)
         channel_gain = keep.tile([128, 4], BF16, name="channel_gain")
         nc.sync.dma_start(out=channel_gain[:], in_=gc.rearrange("(p t) -> p t", t=4))
@@ -103,18 +109,6 @@ def tile_kplanesgaussiananchordecoder_w4_kernel(
             for j in range(head_tiles):
                 nc.tensor.transpose(bank[:, j, :], head_points[:, j, x : x + 1].to_broadcast([128, 128]), ident_bf[:])
             head_coords.append(bank[:].rearrange("p j n -> p (j n)"))
-
-        gains = keep.tile([128, PLANES, M], BF16, name="gains")
-
-        def spread_gains(planes):
-            bank = ps_f.tile([128, len(planes), 2, 128], F32, name="gain_bank", tag="f")
-            for j, pl in enumerate(planes):
-                words = gain_rows[:, pl, :].bitcast(F32)
-                for u in range(2):
-                    nc.tensor.transpose(bank[:, j, u, :], words[:, u : u + 1].to_broadcast([128, 128]), ident[:])
-            return lambda: nc.vector.tensor_copy(
-                out=gains[:, planes[0] : planes[-1] + 1, :].bitcast(F32), in_=bank[:].rearrange("p j u m -> p j (u m)")
-            )
 
         feat_words = [keep.tile([128, C], U32, name="feat_words%d" % pl, align_bytes=64) for pl in range(PLANES)]
         feat_scales = [keep.tile([128, C], U8, name="feat_scales%d" % pl, align_bytes=64) for pl in range(PLANES)]
@@ -145,7 +139,12 @@ def tile_kplanesgaussiananchordecoder_w4_kernel(
             return [lambda j=j: widen(j) for j in range(4)], [lambda h=h: interleave(h) for h in range(2)], [quantise]
 
         squared, distance, scaled, expo, sums, recips, gained, weights = ({} for i in range(8))
-        turned, grouped, feature, partial, z_pair, linear_out, biased = ({} for i in range(7))
+        turned, grouped, codes, feature, partial, z_pair, z_codes, linear_out = ({} for i in range(8))
+        first_job = [[s for s, pl, n in jobs].index(s) for s in range(len(steps))]
+        pairs = JOBS // 2
+
+        def by_words(k):
+            return MODES[k] in "WX"
 
         def square(q):
             step, within = divmod(q, 8)
@@ -184,22 +183,20 @@ def tile_kplanesgaussiananchordecoder_w4_kernel(
         def minimum(k):
             values = work.tile([128, M], F32, name="values", bufs=3)
             least = work.tile([128, 1], F32, name="least", bufs=3)
+            target, source = values[:], distance[k][:].rearrange("n t p -> n (t p)")
+            if by_words(k):
+                target = values[:].rearrange("n (u p e) -> n u p e", u=2, e=2)
+                source = distance[k][:].rearrange("n (u e) p -> n u p e", u=2)
             nc.vector.tensor_scalar(
-                out=values[:].rearrange("n (u p e) -> n u p e", u=2, e=2),
-                in0=distance[k][:].rearrange("n (u e) p -> n u p e", u=2),
-                scalar1=1.0 / WIDTH2,
-                scalar2=None,
-                op0=ALU.mult,
-                op1=ALU.min,
-                accum_out=least[:],
+                out=target, in0=source, scalar1=1.0 / WIDTH2, scalar2=None, op0=ALU.mult, op1=ALU.min, accum_out=least[:]
             )
             scaled[k] = (values, least)
 
         def exponential(k):
             values, least = scaled[k]
-            expo[k] = work.tile([128, M], F32, name="expo", bufs=12)
+            expo[k] = work.tile([128, M], F32, name="expo", bufs=8)
             if k % 2 == 0:
-                sums[k // 2] = work.tile([128, 2], F32, name="sums", bufs=6)
+                sums[k // 2] = work.tile([128, 2], F32, name="sums", bufs=3)
             nc.scalar.activation(
                 out=expo[k][:],
                 in_=values[:],
@@ -210,66 +207,86 @@ def tile_kplanesgaussiananchordecoder_w4_kernel(
             )
 
         def reciprocal(r):
-            recips[r] = work.tile([128, 2], F32, name="recips")
+            recips[r] = work.tile([128, 2], F32, name="recips", bufs=3)
             nc.vector.reciprocal(out=recips[r][:], in_=sums[r][:])
 
-        def gain_on_pool(k, spent):
-            nc.gpsimd.tensor_tensor(out=spent, in0=expo[k][:], in1=gains[:, jobs[k][1], :], op=ALU.mult)
-            gained[k] = spent
+        def spent(k):
+            return k // 2 - 2 if MODES[k] == "W" else None
 
-        def normalise(k):
-            weights[k] = work.tile([128, M], BF16, name="weights", bufs=4)
-            factor = recips[k // 2][:, k % 2 : k % 2 + 1]
-            if k in gained:
-                nc.vector.tensor_scalar(out=weights[k][:], in0=gained[k], scalar1=factor, scalar2=None, op0=ALU.mult)
-            else:
-                nc.vector.scalar_tensor_tensor(
-                    out=weights[k][:],
-                    in0=expo[k][:],
-                    scalar=factor,
-                    in1=gains[:, jobs[k][1], :],
-                    op0=ALU.mult,
-                    op1=ALU.mult,
-                )
-
-        def turn(r):
-            turned[r] = ps_xt.tile([128, 2, 2, 128], F32, name="turned", tag="xt")
-            for j in range(2):
-                words = weights[2 * r + j][:].bitcast(F32)
-                for u in range(2):
-                    nc.tensor.transpose(turned[r][:, j, u, :], words[:, 128 * u : 128 * u + 128], ident[:])
-
-        def copy_out(r, copy):
-            grouped[r] = work.tile([128, 256 * 4], BF16, name="grouped", align_bytes=64)
-            copy(
-                out=grouped[r][:].bitcast(F32).rearrange("p (j n u) -> p j n u", j=2, u=2),
-                in_=turned[r][:].rearrange("p j u n -> p j n u"),
+        def pool_gain(k):
+            gained[k] = expo[k][:]
+            if spent(k) is not None:
+                gained[k] = grouped[spent(k)][:].rearrange("p j n t -> p (j n t)").bitcast(F32)
+            nc.gpsimd.tensor_tensor(
+                out=gained[k].rearrange("n (u p e) -> n u p e", u=2, e=2),
+                in0=expo[k][:].rearrange("n (u p e) -> n u p e", u=2, e=2),
+                in1=gain_all[:, jobs[k][1], :].rearrange("n (p u e) -> n u p e", u=2, e=2),
+                op=ALU.mult,
             )
 
-        def products(r, pool, tag):
-            words = work.tile([128, 256], U32, name="a_words", align_bytes=64)
-            scales = work.tile([128, 256], U8, name="a_scales", align_bytes=64)
-            nc.vector.quantize_mx(out=words[:].bitcast(FP8X4), scales=scales[:], in_=grouped[r][:])
-            for k in (2 * r, 2 * r + 1):
-                pl = jobs[k][1]
-                cols = slice(128 * (k % 2), 128 * (k % 2) + 128)
-                feature[k] = pool.tile([128, 4, 128], F32, name="feature", tag=tag)
-                for t in range(4):
-                    nc.tensor.matmul_mx(
-                        out=feature[k][:, t, :],
-                        lhsT=feat_words[pl][:, 128 * t : 128 * t + 128].bitcast(FP8X4),
-                        lhsT_scale=feat_scales[pl][:, 128 * t : 128 * t + 128],
-                        rhs=words[:, cols].bitcast(FP8X4),
-                        rhs_scale=scales[:, cols],
-                        start=True,
-                        stop=True,
-                    )
+        def normalise(k):
+            source = target = expo[k][:]
+            factor = recips[k // 2][:, k % 2 : k % 2 + 1]
+            if by_words(k):
+                weights[k] = work.tile([128, M], BF16, name="weights", bufs=4)
+                source, target = gained[k], weights[k][:]
+            if MODES[k] == "X":
+                nc.scalar.activation(out=target, in_=source, func=ACT.Copy, scale=factor)
+            elif MODES[k] == "V":
+                nc.vector.tensor_scalar(out=target, in0=source, scalar1=factor, scalar2=None, op0=ALU.mult)
+            else:
+                nc.gpsimd.tensor_scalar(out=target, in0=source, scalar1=factor, scalar2=1.0, op0=ALU.mult, op1=ALU.mult)
+
+        def turn(k):
+            blocks = 2 if by_words(k) else 4
+            source = weights[k][:].bitcast(F32) if by_words(k) else expo[k][:]
+            turned[k] = ps_xt.tile([128, blocks, 128], F32, name="turned", tag="xt")
+            for t in range(blocks):
+                nc.tensor.transpose(turned[k][:, t, :], source[:, 128 * t : 128 * t + 128], ident[:])
+
+        def group(k):
+            if k // 2 not in grouped:
+                grouped[k // 2] = work.tile([128, 2, 128, 4], BF16, name="grouped", align_bytes=64, bufs=4)
+            target = grouped[k // 2][:, k % 2]
+            if by_words(k):
+                nc.scalar.copy(out=target.bitcast(F32), in_=turned[k][:].rearrange("p u n -> p n u"))
+            else:
+                nc.vector.tensor_tensor(
+                    out=target,
+                    in0=turned[k][:].rearrange("p t n -> p n t"),
+                    in1=gain_rows[:, jobs[k][1], :].unsqueeze(1).to_broadcast([128, 128, 4]),
+                    op=ALU.mult,
+                )
+
+        def quantise(source, count, name):
+            words = work.tile([128, 128 * count], U32, name=name + "_words", tag=name + "_words", align_bytes=64)
+            scales = work.tile([128, 128 * count], U8, name=name + "_scales", tag=name + "_scales", align_bytes=64)
+            nc.vector.quantize_mx(out=words[:].bitcast(FP8X4), scales=scales[:], in_=source.rearrange("p j n t -> p (j n t)"))
+            return [(words[:, 128 * j : 128 * j + 128].bitcast(FP8X4), scales[:, 128 * j : 128 * j + 128]) for j in range(count)]
+
+        def quantise_weights(k, count):
+            for j, operand in enumerate(quantise(grouped[k // 2][:, k % 2 : k % 2 + count], count, "a")):
+                codes[k + j] = operand
+
+        def products(k):
+            pl = jobs[k][1]
+            feature[k] = ps_f.tile([128, 4, 128], F32, name="feature", tag="f")
+            for t in range(4):
+                nc.tensor.matmul_mx(
+                    out=feature[k][:, t, :],
+                    lhsT=feat_words[pl][:, 128 * t : 128 * t + 128].bitcast(FP8X4),
+                    lhsT_scale=feat_scales[pl][:, 128 * t : 128 * t + 128],
+                    rhs=codes[k][0],
+                    rhs_scale=codes[k][1],
+                    start=True,
+                    stop=True,
+                )
 
         def multiply(k):
             step, pl, n = jobs[k]
             other = channel_gain[:].unsqueeze(1).to_broadcast([128, 128, 4]) if pl == 0 else partial[n][:]
             if pl < PLANES - 1:
-                partial[n] = work.tile([128, 128, 4], F32, name="partial", bufs=EARLY_TILES + 1)
+                partial[n] = work.tile([128, 128, 4], F32, name="partial", bufs=7)
                 result = partial[n][:]
             else:
                 if n % 2 == 0:
@@ -277,183 +294,192 @@ def tile_kplanesgaussiananchordecoder_w4_kernel(
                 result = z_pair[n // 2][:, n % 2]
             nc.vector.tensor_tensor(out=result, in0=feature[k][:].rearrange("p t n -> p n t"), in1=other, op=ALU.mult)
 
+        def quantise_z(n, count):
+            for j, operand in enumerate(quantise(z_pair[n // 2][:, n % 2 : n % 2 + count], count, "z")):
+                z_codes[n + j] = operand
+
         def linear(n):
-            words = work.tile([128, 256], U32, name="z_words", align_bytes=64)
-            scales = work.tile([128, 256], U8, name="z_scales", align_bytes=64)
-            nc.vector.quantize_mx(
-                out=words[:].bitcast(FP8X4), scales=scales[:], in_=z_pair[n // 2][:].rearrange("p j n t -> p (j n t)")
+            linear_out[n] = ps_o.tile([128, H], F32, name="linear_out", tag="o")
+            nc.tensor.matmul_mx(
+                out=linear_out[n][:],
+                lhsT=z_codes[n][0],
+                lhsT_scale=z_codes[n][1],
+                rhs=w_words[:].bitcast(FP4X4),
+                rhs_scale=w_scales[:],
+                start=True,
+                stop=True,
             )
-            for j in range(2):
-                linear_out[n - 1 + j] = ps_o.tile([128, H], F32, name="linear_out", tag="o")
-                nc.tensor.matmul_mx(
-                    out=linear_out[n - 1 + j][:],
-                    lhsT=words[:, 128 * j : 128 * j + 128].bitcast(FP8X4),
-                    lhsT_scale=scales[:, 128 * j : 128 * j + 128],
-                    rhs=w_words[:].bitcast(FP4X4),
-                    rhs_scale=w_scales[:],
-                    start=True,
-                    stop=True,
-                )
 
         sums_b = keep.tile([128, TILES, H], F32, name="sums_b")
         result_sb = keep.tile([128, TILES, H], F32, name="result_sb")
         out_tiles = out.rearrange("(j p) h -> p j h", p=128)
-        unloaded = []
 
         def bias(n):
-            if n < POOL_BIAS_TILES:
+            if n in POOL_BIAS:
                 nc.scalar.copy(out=result_sb[:, n, :], in_=linear_out[n][:])
-                unloaded.append(n)
             else:
                 nc.vector.tensor_tensor(out=sums_b[:, n, :], in0=linear_out[n][:], in1=bias_row[:], op=ALU.add)
 
-        def bias_on_pool(n, spent):
-            nc.gpsimd.tensor_tensor(out=spent, in0=result_sb[:, n, :], in1=bias_row[:], op=ALU.add)
-            biased[n] = spent.unsqueeze(1)
-
-        def with_bias(n, count):
-            return biased[n] if n in biased else sums_b[:, n : n + count, :]
+        def pool_bias(n):
+            nc.gpsimd.tensor_tensor(out=sums_b[:, n, :], in0=result_sb[:, n, :], in1=bias_row[:], op=ALU.add)
 
         def sigmoid(n, count):
-            part = result_sb[:, n : n + count, :]
-            nc.scalar.activation(out=part, in_=with_bias(n, count), func=ACT.Sigmoid, scale=-1.0)
+            part = slice(n, n + count)
+            nc.scalar.activation(out=result_sb[:, part, :], in_=sums_b[:, part, :], func=ACT.Sigmoid, scale=-1.0)
 
-        def logarithm(n, count):
-            part = result_sb[:, n : n + count, :]
+        def logarithm(n, lo, hi):
+            part = result_sb[:, n, lo:hi]
             nc.scalar.activation(out=part, in_=part, func=ACT.Ln, bias=TINY)
 
-        def finish(n, count):
-            part = result_sb[:, n : n + count, :]
+        def finish(n, lo, hi):
+            part = result_sb[:, n, lo:hi]
             nc.vector.scalar_tensor_tensor(
-                out=part, in0=part, scalar=-1.0, in1=with_bias(n, count), op0=ALU.mult, op1=ALU.max
+                out=part, in0=part, scalar=-1.0, in1=sums_b[:, n, lo:hi], op0=ALU.mult, op1=ALU.max
             )
-            nc.sync.dma_start(out=out_tiles[:, n : n + count, :], in_=part)
+            nc.sync.dma_start(out=out_tiles[:, n, lo:hi], in_=part)
+
+        (widen0, inter0, quant0), (widen1, inter1, quant1), (widen2, inter2, quant2) = map(feat_parts, range(PLANES))
+        feat_order = widen0 + widen1 + inter0 + inter1[:1] + quant0 + inter1[1:] + widen2 + quant1 + inter2 + quant2
+        feat_ready = [feat_order.index(part[0]) for part in (quant0, quant1, quant2)]
+
+        def feat(i):
+            feat_order[i]()
+
+        def last_job(n):
+            return [k for k in range(JOBS) if jobs[k][1:] == (PLANES - 1, n)][0]
+
+        made = set()
+
+        def needs(stage, i, *rest):
+            if stage == distances:
+                return [(square, 8 * jobs[i][0] + 7), (minimum, i - 2)]
+            if stage == square:
+                same = [s for s in range(i // 8) if steps[s][1] == steps[i // 8][1]]
+                return [(distances, first_job[same[-3]] + steps[same[-3]][1] - 1)] if len(same) >= 3 else []
+            if stage == minimum:
+                return [(distances, i), (exponential, i - 3)]
+            if stage == exponential:
+                return [(minimum, i), (turn, i - 8)]
+            if stage == reciprocal:
+                return [(exponential, 2 * i + 1)]
+            if stage == pool_gain:
+                return [(exponential, i)] + ([(quantise_weights, 2 * spent(i))] if spent(i) is not None else [])
+            if stage == normalise:
+                return [(reciprocal, i // 2)] + ([(pool_gain, i)] if by_words(i) else [])
+            if stage == turn:
+                return [(normalise, i), (group, i - 2)]
+            if stage == group:
+                return [(turn, i)]
+            if stage == quantise_weights:
+                return [(group, i + j) for j in range(rest[0])]
+            if stage == products:
+                return [(quantise_weights, i), (multiply, i - 2), (feat, feat_ready[jobs[i][1]])]
+            if stage == multiply:
+                return [(products, i)]
+            if stage == quantise_z:
+                return [(multiply, last_job(i + j)) for j in range(rest[0])]
+            if stage == linear:
+                return [(quantise_z, i), (bias, i - 2)]
+            if stage == bias:
+                return [(linear, i)]
+            if stage == pool_bias:
+                return [(bias, i)]
+            if stage == sigmoid:
+                return [(pool_bias if i + j in POOL_BIAS else bias, i + j) for j in range(rest[0])]
+            if stage == logarithm:
+                return [(sigmoid, i)]
+            if stage == finish:
+                return [(logarithm, i, rest[0])]
+            return []
+
+        def issue(orders):
+            while any(orders):
+                moved = False
+                for order in orders:
+                    while order and all(need in made or need[1] < 0 for need in needs(*order[0])):
+                        stage, i, *rest = order.pop(0)
+                        stage(i, *rest)
+                        counted = stage in (quantise_weights, quantise_z, sigmoid)
+                        made.update((stage, i + j) for j in range(rest[0] if counted else 1))
+                        if stage == logarithm:
+                            made.add((stage, i, rest[0]))
+                        moved = True
+                assert moved
 
         spread_points(0)
         spread_points(1)
-        keep_gains = [spread_gains([0, 1]), spread_gains([2])]
-        (widen0, inter0, quant0), (widen1, inter1, quant1), (widen2, inter2, quant2) = map(feat_parts, range(PLANES))
-        for part in widen0 + widen1 + inter0:
-            part()
-        for q in range(8):
-            square(q)
-        feat_left = inter1[:1] + quant0 + inter1[1:] + widen2 + inter2 + quant1 + quant2
-        squares_left = list(range(8, 8 * len(steps)))
-        jobs_left = list(range(JOBS))
+        vector, scalar, pool, tensor = [], [], [], []
 
-        def more_feat(count):
-            for part in feat_left[:count]:
-                part()
-                feat_left.remove(part)
+        squares_left = list(range(8 * len(steps)))
 
         def more_squares(count):
-            for q in squares_left[:count]:
-                square(q)
-                squares_left.remove(q)
+            scalar.extend((square, squares_left.pop(0)) for i in range(min(count, len(squares_left))))
 
-        def next_job():
-            if jobs_left:
-                k = jobs_left.pop(0)
-                if k + 2 < JOBS:
-                    while squares_left and squares_left[0] // 8 <= jobs[k + 2][0]:
-                        more_squares(1)
-                    distances(k + 2)
-                minimum(k)
-                exponential(k)
+        more_squares(8 + SQUARES_AHEAD)
+        for k in range(JOBS):
+            scalar.append((exponential, k))
+            if k >= 3 and by_words(k - 3):
+                scalar.append((group, k - 3))
+            need = 0
+            for s in range(len(steps)):
+                left = len([q for q in squares_left if q // 8 <= s])
+                need = max(need, -(-left // max(first_job[s] - 1 - MARGIN - k, 1)))
+            more_squares(need)
+        last = JOBS - 1
+        scalar += [(group, last - 2), (normalise, last - 1), (normalise, last), (group, last - 1), (group, last)]
+        scalar += [(bias, n) for n in POOL_BIAS] + [(sigmoid, n, 2) for n in (0, 2, 4)] + [(sigmoid, 6, 1), (sigmoid, 7, 1)]
+        parts = [(0, 0, H // 2), (0, H // 2, H)] + [(n, 0, H) for n in range(1, TILES - 1)]
+        parts += [(TILES - 1, 0, H // 2), (TILES - 1, H // 2, H)]
+        scalar += [(logarithm, *part) for part in parts]
 
-        def last_plane(k):
-            return k >= 0 and jobs[k][1] == PLANES - 1
+        for r in range(pairs):
+            pool += [(pool_gain, k) for k in (2 * r, 2 * r + 1) if by_words(k)]
+            pool += [(normalise, k) for k in (2 * r, 2 * r + 1) if MODES[k] in "AW"]
+        pool += [(pool_bias, n) for n in POOL_BIAS]
+
+        feat_left = list(range(len(feat_order)))
+
+        def more_feat(count):
+            vector.extend((feat, feat_left.pop(0)) for i in range(min(count, len(feat_left))))
+
+        def weights_of(k):
+            if not by_words(k):
+                vector.append((group, k))
 
         more_feat(FEAT_AHEAD)
-        distances(0)
-        distances(1)
-        more_squares(WIDE_SQUARES_AHEAD)
-
-        last = EARLY_PAIRS + 2
-        for r in range(last + 1):
-            filling = r <= 2
-            next_job()
+        tensor += [(distances, 0), (distances, 1)]
+        for r in range(pairs):
+            a, b = 2 * r, 2 * r + 1
+            vector.append((minimum, a))
             if r >= 1:
-                reciprocal(r - 1)
-            if r == last:
-                normalise(2 * EARLY_PAIRS)
-                normalise(2 * EARLY_PAIRS + 1)
-                turn(EARLY_PAIRS)
-            if 3 <= r < last:
-                copy_out(r - 2, nc.scalar.copy)
-            if not filling:
-                multiply(2 * r - 6)
-            if last_plane(2 * r - 8):
-                bias(jobs[2 * r - 8][2])
-            if filling:
-                more_squares(WIDE_SQUARES_A_JOB)
-            more_feat(FEAT_A_MINIMUM)
-            if keep_gains:
-                keep_gains.pop(0)()
-            if r == 2:
-                copy_out(0, nc.vector.tensor_copy)
-            next_job()
-            if not filling:
-                multiply(2 * r - 5)
-            if last_plane(2 * r - 7):
-                bias(jobs[2 * r - 7][2])
-            more_feat(FEAT_A_MINIMUM)
-            if 2 <= r < last:
-                products(r - 2, ps_f, "f")
-            if r == last - 1:
-                next_job()
-            if r == last:
-                reciprocal(r)
-                normalise(2 * EARLY_PAIRS + 2)
-            if last_plane(2 * r - 5):
-                linear(jobs[2 * r - 5][2])
-            if 1 <= r <= EARLY_PAIRS:
-                normalise(2 * r - 1)
-                normalise(2 * r - 2)
-                turn(r - 1)
-                spent = [gained.get(k, expo[k][:]) for k in (2 * r - 2, 2 * r - 1)]
-                if unloaded:
-                    for buffer in spent:
-                        bias_on_pool(unloaded.pop(0), buffer)
-                elif r >= 2:
-                    gain_on_pool(2 * r + 1, spent[0])
-            more_squares(WIDE_SQUARES_A_JOB if filling else NARROW_SQUARES_A_TURN)
-
-        first_pair, second_pair, third_pair = range(EARLY_PAIRS, EARLY_PAIRS + PLANES)
-        sigmoid(0, 1)
-        copy_out(first_pair, nc.scalar.copy)
-        sigmoid(1, 1)
-        sigmoid(2, 2)
-        normalise(2 * second_pair + 1)
-        turn(second_pair)
-        products(first_pair, ps_f, "f")
-        bias(EARLY_TILES - 2)
-        bias(EARLY_TILES - 1)
-        copy_out(second_pair, nc.scalar.copy)
-        sigmoid(4, 2)
-        normalise(2 * third_pair)
-        normalise(2 * third_pair + 1)
-        turn(third_pair)
-        multiply(2 * first_pair)
-        products(second_pair, ps_d2, "d2")
-        multiply(2 * first_pair + 1)
-        logarithm(0, 2)
-        copy_out(third_pair, nc.vector.tensor_copy)
-        logarithm(2, 2)
-        multiply(2 * second_pair)
-        logarithm(4, 2)
-        products(third_pair, ps_f, "f")
-        multiply(2 * second_pair + 1)
-        multiply(2 * third_pair)
-        multiply(2 * third_pair + 1)
-        finish(0, 1)
-        linear(TILES - 1)
-        finish(1, 1)
-        for n in range(EARLY_TILES, TILES):
-            bias(n)
-            sigmoid(n, 1)
-        finish(2, 2)
-        finish(4, 2)
-        for n in range(EARLY_TILES, TILES):
-            logarithm(n, 1)
-            finish(n, 1)
+                vector.append((reciprocal, r - 1))
+            more_feat(FEAT_A_SLOT)
+            vector += [(normalise, k) for k in (a - 2, b - 2) if k >= 0 and MODES[k] == "V"]
+            if r >= 2:
+                weights_of(a - 4)
+                weights_of(b - 4)
+            vector.append((minimum, b))
+            more_feat(FEAT_A_SLOT)
+            if r >= 4 and jobs[a - 8][1] == PLANES - 1:
+                vector += [(bias, jobs[k][2]) for k in (a - 8, b - 8) if jobs[k][2] not in POOL_BIAS]
+            if r >= 3:
+                vector += [(multiply, a - 6), (multiply, b - 6)]
+            if r >= 2:
+                vector.append((quantise_weights, a - 4, 2))
+            tensor += [(distances, k) for k in (a + 2,) if k < JOBS] + [(turn, k) for k in (a - 2,) if k >= 0]
+            tensor += [(distances, k) for k in (b + 2,) if k < JOBS] + [(turn, k) for k in (b - 2,) if k >= 0]
+            if r >= 2:
+                tensor += [(products, a - 4), (products, b - 4)]
+            if r >= 3 and jobs[a - 6][1] == PLANES - 1:
+                vector.append((quantise_z, jobs[a - 6][2], 2))
+                tensor += [(linear, jobs[a - 6][2]), (linear, jobs[b - 6][2])]
+        late_bias = [(bias, n) for n in (4, 5) if n not in POOL_BIAS]
+        vector.append((reciprocal, 11))
+        weights_of(20)
+        vector += [(multiply, 18), (multiply, 19), (quantise_weights, 20, 2)] + late_bias
+        vector += [(quantise_weights, 22, 1), (multiply, 20), (quantise_weights, 23, 1), (multiply, 21), (multiply, 22)]
+        vector += [(multiply, 23), (quantise_z, 6, 1), (quantise_z, 7, 1), (bias, 6), (bias, 7)]
+        vector += [(finish, *part) for part in parts]
+        tensor += [(turn, 22), (turn, 23), (products, 20), (products, 21), (products, 22), (products, 23)]
+        tensor += [(linear, 6), (linear, 7)]
+        issue([vector, scalar, pool, tensor])

@@ -24,13 +24,16 @@ TINY = 2.0**-60
 
 CHUNKS = ((0, 4), (4, 2), (6, 2))
 MATMUL_BLOCKS = (0, 3)
-FEAT_AHEAD = 13
+FEAT_AHEAD = 14
 FEAT_A_SLOT = 2
 SQUARES_AHEAD = 3
-MARGIN = 0
-MODES = "VVAAAWAWAWAWAWAWAWAWAWXX"
+MARGIN = 1
+MODES = "VVAAAAAAWDWDWDWDWDWDWDWA"
 POOL_BIAS = ()
-TAILV = 0
+LATE = 4
+MATMUL_JOBS = (2, 3, 4, 5, 6, 7, 8, 9, 10, 11)
+COPY_LAG = 4
+COPY_AT = (1, 4)
 
 
 def tile_kplanesgaussiananchordecoder_w4_kernel(
@@ -142,6 +145,7 @@ def tile_kplanesgaussiananchordecoder_w4_kernel(
         turned, grouped, codes, feature, partial, z_pair, z_codes, linear_out = ({} for i in range(8))
         first_job = [[s for s, pl, n in jobs].index(s) for s in range(len(steps))]
         pairs = JOBS // 2
+        spent_pair, diagonal = {}, {}
 
         def by_words(k):
             return MODES[k] in "WX"
@@ -177,7 +181,7 @@ def tile_kplanesgaussiananchordecoder_w4_kernel(
                         rhs=ident[:],
                         start=(axis == 0),
                         stop=(axis == 1),
-                        is_transpose=not (axis == 0 and t in MATMUL_BLOCKS),
+                        is_transpose=not (axis == 0 and t in MATMUL_BLOCKS and k in MATMUL_JOBS),
                     )
 
         def minimum(k):
@@ -194,7 +198,7 @@ def tile_kplanesgaussiananchordecoder_w4_kernel(
 
         def exponential(k):
             values, least = scaled[k]
-            expo[k] = work.tile([128, M], F32, name="expo", bufs=8)
+            expo[k] = work.tile([128, M], F32, name="expo", bufs=10)
             if k % 2 == 0:
                 sums[k // 2] = work.tile([128, 2], F32, name="sums", bufs=3)
             nc.scalar.activation(
@@ -211,7 +215,7 @@ def tile_kplanesgaussiananchordecoder_w4_kernel(
             nc.vector.reciprocal(out=recips[r][:], in_=sums[r][:])
 
         def spent(k):
-            return k // 2 - 2 if MODES[k] == "W" else None
+            return spent_pair[k // 2] if MODES[k] == "W" else None
 
         def pool_gain(k):
             gained[k] = expo[k][:]
@@ -230,7 +234,10 @@ def tile_kplanesgaussiananchordecoder_w4_kernel(
             if by_words(k):
                 weights[k] = work.tile([128, M], BF16, name="weights", bufs=4)
                 source, target = gained[k], weights[k][:]
-            if MODES[k] == "X":
+            if MODES[k] == "D":
+                diagonal[k] = work.tile([128, 128], F32, name="diagonal")
+                nc.scalar.activation(out=diagonal[k][:], in_=ident[:], func=ACT.Copy, scale=factor)
+            elif MODES[k] == "X":
                 nc.scalar.activation(out=target, in_=source, func=ACT.Copy, scale=factor)
             elif MODES[k] == "V":
                 nc.vector.tensor_scalar(out=target, in0=source, scalar1=factor, scalar2=None, op0=ALU.mult)
@@ -242,11 +249,15 @@ def tile_kplanesgaussiananchordecoder_w4_kernel(
             source = weights[k][:].bitcast(F32) if by_words(k) else expo[k][:]
             turned[k] = ps_xt.tile([128, blocks, 128], F32, name="turned", tag="xt")
             for t in range(blocks):
-                nc.tensor.transpose(turned[k][:, t, :], source[:, 128 * t : 128 * t + 128], ident[:])
+                block = source[:, 128 * t : 128 * t + 128]
+                if MODES[k] == "D":
+                    nc.tensor.matmul(out=turned[k][:, t, :], lhsT=block, rhs=diagonal[k][:], start=True, stop=True)
+                else:
+                    nc.tensor.transpose(turned[k][:, t, :], block, ident[:])
 
         def group(k):
             if k // 2 not in grouped:
-                grouped[k // 2] = work.tile([128, 2, 128, 4], BF16, name="grouped", align_bytes=64, bufs=4)
+                grouped[k // 2] = work.tile([128, 2, 128, 4], BF16, name="grouped", align_bytes=64, bufs=7)
             target = grouped[k // 2][:, k % 2]
             if by_words(k):
                 nc.scalar.copy(out=target.bitcast(F32), in_=turned[k][:].rearrange("p u n -> p n u"))
@@ -259,8 +270,8 @@ def tile_kplanesgaussiananchordecoder_w4_kernel(
                 )
 
         def quantise(source, count, name):
-            words = work.tile([128, 128 * count], U32, name=name + "_words", tag=name + "_words", align_bytes=64)
-            scales = work.tile([128, 128 * count], U8, name=name + "_scales", tag=name + "_scales", align_bytes=64)
+            words = work.tile([128, 128 * count], U32, name=name + "_words", tag=name + "_words", align_bytes=64, bufs=3)
+            scales = work.tile([128, 128 * count], U8, name=name + "_scales", tag=name + "_scales", align_bytes=64, bufs=3)
             nc.vector.quantize_mx(out=words[:].bitcast(FP8X4), scales=scales[:], in_=source.rearrange("p j n t -> p (j n t)"))
             return [(words[:, 128 * j : 128 * j + 128].bitcast(FP8X4), scales[:, 128 * j : 128 * j + 128]) for j in range(count)]
 
@@ -359,7 +370,7 @@ def tile_kplanesgaussiananchordecoder_w4_kernel(
             if stage == minimum:
                 return [(distances, i), (exponential, i - 3)]
             if stage == exponential:
-                return [(minimum, i), (turn, i - 8)]
+                return [(minimum, i), (turn, i - 10)]
             if stage == reciprocal:
                 return [(exponential, 2 * i + 1)]
             if stage == pool_gain:
@@ -410,76 +421,134 @@ def tile_kplanesgaussiananchordecoder_w4_kernel(
         spread_points(1)
         vector, scalar, pool, tensor = [], [], [], []
 
-        squares_left = list(range(8 * len(steps)))
-
-        def more_squares(count):
-            scalar.extend((square, squares_left.pop(0)) for i in range(min(count, len(squares_left))))
-
-        more_squares(8 + SQUARES_AHEAD)
-        for k in range(JOBS):
-            scalar.append((exponential, k))
-            if k >= 3 and by_words(k - 3):
-                scalar.append((group, k - 3))
-            need = 0
-            for s in range(len(steps)):
-                left = len([q for q in squares_left if q // 8 <= s])
-                need = max(need, -(-left // max(first_job[s] - 1 - MARGIN - k, 1)))
-            more_squares(need)
-        last = JOBS - 1
-        scalar += [(group, last - 2), (normalise, last - 1), (normalise, last), (group, last - 1), (group, last)]
-        scalar += [(bias, n) for n in POOL_BIAS] + [(sigmoid, n, 2) for n in (0, 2, 4)] + [(sigmoid, 6, 1), (sigmoid, 7, 1)]
-        parts = [(0, 0, H // 2), (0, H // 2, H)] + [(n, 0, H) for n in range(1, TILES - 1)]
-        parts += [(TILES - 1, 0, H // 2), (TILES - 1, H // 2, H)]
-        scalar += [(logarithm, *part) for part in parts]
-
-        for r in range(pairs):
-            pool += [(pool_gain, k) for k in (2 * r, 2 * r + 1) if by_words(k)]
-            pool += [(normalise, k) for k in (2 * r, 2 * r + 1) if MODES[k] in "AW"]
-        pool += [(pool_bias, n) for n in POOL_BIAS]
-
         feat_left = list(range(len(feat_order)))
+        squares_left = list(range(8 * len(steps)))
+        last = JOBS - 1
 
         def more_feat(count):
             vector.extend((feat, feat_left.pop(0)) for i in range(min(count, len(feat_left))))
 
-        def weights_of(k):
-            if not by_words(k):
-                vector.append((group, k))
+        def closes(r):
+            return r >= 0 and jobs[2 * r][1] == PLANES - 1
 
-        more_feat(FEAT_AHEAD)
+        def paced_squares(k):
+            need = 0
+            for s in range(len(steps)):
+                left = sum(steps[q // 8][1] for q in squares_left if q // 8 <= s)
+                need = max(need, left / max(first_job[s] - 1 - MARGIN - k, 1))
+            while squares_left and need > 0:
+                need -= steps[squares_left[0] // 8][1]
+                scalar.append((square, squares_left.pop(0)))
+
+        def front(k):
+            vector.append((minimum, k))
+            scalar.append((exponential, k))
+            if k % 2 == 0:
+                scalar.extend((normalise, j) for j in (k - 2, k - 1) if j >= 0 and MODES[j] == "D")
+            if k >= COPY_LAG and by_words(k - COPY_LAG):
+                scalar.append((group, k - COPY_LAG))
+            paced_squares(k)
+            if k + 2 < JOBS:
+                tensor.append((distances, k + 2))
+
+        waiting, summed = [], []
+
+        def next_bias():
+            if summed:
+                n = summed.pop(0)
+                if n not in POOL_BIAS:
+                    vector.append((bias, n))
+                if waiting:
+                    summed.append(waiting[0])
+                    tensor.append((linear, waiting.pop(0)))
+
+        def close(n, count):
+            vector.append((quantise_z, n, count))
+            for j in range(n, n + count):
+                if len(summed) < 2:
+                    summed.append(j)
+                    tensor.append((linear, j))
+                else:
+                    waiting.append(j)
+
+        def gains(r):
+            vector.extend((group, k) for k in (2 * r, 2 * r + 1) if not by_words(k))
+
+        def weights_to_products(r):
+            vector.append((quantise_weights, 2 * r, 2))
+            tensor.extend([(products, 2 * r), (products, 2 * r + 1)])
+
+        scalar += [(square, squares_left.pop(0)) for i in range(8 + SQUARES_AHEAD)]
         tensor += [(distances, 0), (distances, 1)]
-        for r in range(pairs):
-            a, b = 2 * r, 2 * r + 1
-            vector.append((minimum, a))
+        more_feat(FEAT_AHEAD)
+        for r in range(pairs - 1):
+            spent_pair[r] = r - 2
+            front(2 * r)
             if r >= 1:
                 vector.append((reciprocal, r - 1))
             more_feat(FEAT_A_SLOT)
-            vector += [(normalise, k) for k in (a - 2, b - 2) if k >= 0 and MODES[k] == "V"]
+            vector += [(normalise, k) for k in (2 * r - 2, 2 * r - 1) if k >= 0 and MODES[k] == "V"]
             if r >= 2:
-                weights_of(a - 4)
-                weights_of(b - 4)
-            vector.append((minimum, b))
+                gains(r - 2)
+            if r < pairs - 2:
+                next_bias()
+            if r >= 1:
+                tensor += [(turn, k) for k in sorted((2 * r - 2, 2 * r - 1), key=by_words)]
+            front(2 * r + 1)
             more_feat(FEAT_A_SLOT)
-            if r >= 4 and jobs[a - 8][1] == PLANES - 1:
-                vector += [(bias, jobs[k][2]) for k in (a - 8, b - 8) if jobs[k][2] not in POOL_BIAS]
             if r >= 3:
-                vector += [(multiply, a - 6), (multiply, b - 6)]
+                vector.append((multiply, 2 * r - 6))
             if r >= 2:
-                vector.append((quantise_weights, a - 4, 2))
-            tensor += [(distances, k) for k in (a + 2,) if k < JOBS] + [(turn, k) for k in (a - 2,) if k >= 0]
-            tensor += [(distances, k) for k in (b + 2,) if k < JOBS] + [(turn, k) for k in (b - 2,) if k >= 0]
-            if r >= 2:
-                tensor += [(products, a - 4), (products, b - 4)]
-            if r >= 3 and jobs[a - 6][1] == PLANES - 1:
-                vector.append((quantise_z, jobs[a - 6][2], 2))
-                tensor += [(linear, jobs[a - 6][2]), (linear, jobs[b - 6][2])]
-        late_bias = [(bias, n) for n in (4, 5) if n not in POOL_BIAS]
+                weights_to_products(r - 2)
+            if closes(r - 4):
+                close(jobs[2 * r - 8][2], 2)
+            if r >= 3:
+                vector.append((multiply, 2 * r - 5))
+
+        spent_pair[11] = None
+        front(22)
+        vector.append((reciprocal, 10))
+        gains(9)
+        front(23)
+        tensor += [(turn, 21), (turn, 20)]
+        next_bias()
         vector.append((reciprocal, 11))
-        weights_of(20)
-        vector += [(multiply, 18), (multiply, 19), (quantise_weights, 20, 2)] + late_bias
-        vector += [(quantise_weights, 22, 1), (multiply, 20), (quantise_weights, 23, 1), (multiply, 21), (multiply, 22)]
-        vector += [(multiply, 23), (quantise_z, 6, 1), (quantise_z, 7, 1), (bias, 6), (bias, 7)]
-        vector += [(finish, *part) for part in parts]
-        tensor += [(turn, 22), (turn, 23), (products, 20), (products, 21), (products, 22), (products, 23)]
-        tensor += [(linear, 6), (linear, 7)]
+        vector.append((multiply, 16))
+        weights_to_products(9)
+        vector.append((multiply, 17))
+        next_bias()
+        gains(10)
+        next_bias()
+        tensor += [(turn, 22), (turn, 23)]
+        close(4, 2)
+        vector.append((multiply, 18))
+        weights_to_products(10)
+        vector.append((multiply, 19))
+        gains(11)
+        vector.append((multiply, 20))
+        weights_to_products(11)
+        vector.append((multiply, 21))
+        next_bias()
+        next_bias()
+        vector += [(multiply, 22), (multiply, 23)]
+        close(6, 1)
+        close(7, 1)
+        vector += [(finish, 0, 0, H)] if LATE else []
+        next_bias()
+        next_bias()
+        parts = [(LATE, 0, H // 2), (LATE, H // 2, H)] + [(n, 0, H) for n in range(LATE + 1, TILES - 1)]
+        parts += [(TILES - 1, 0, H // 2), (TILES - 1, H // 2, H)]
+        vector += [(finish, n, 0, H) for n in range(1, LATE)] + [(finish, *part) for part in parts]
+        copies = [(group, k) for k in range(JOBS - COPY_LAG, JOBS) if by_words(k)]
+        early = [(normalise, k) for k in (last - 1, last) if MODES[k] == "D"]
+        early += [(sigmoid, 0, 2), (sigmoid, 2, 1), (sigmoid, 3, 1)] + [(logarithm, n, 0, H) for n in range(LATE)]
+        for place, copy in zip(COPY_AT, copies):
+            early.insert(place, copy)
+        for n in POOL_BIAS:
+            early.insert(early.index((logarithm, 1, 0, H)) if LATE else len(early), (bias, n))
+        scalar += early + [(sigmoid, n, 1) for n in range(4, TILES)] + [(logarithm, *part) for part in parts]
+        for r in range(pairs):
+            pool += [(pool_gain, k) for k in (2 * r, 2 * r + 1) if by_words(k)]
+            pool += [(normalise, k) for k in (2 * r, 2 * r + 1) if MODES[k] in "AW"]
+        pool += [(pool_bias, n) for n in POOL_BIAS]
         issue([vector, scalar, pool, tensor])

@@ -28,12 +28,19 @@ FEAT_AHEAD = 14
 FEAT_A_SLOT = 2
 SQUARES_AHEAD = 3
 MARGIN = 1
-MODES = "VVAAAAAAWDWDWDWDWDWDWDWA"
+MODES = "VVAAAAWDWDWDWDWDWDWDWDAA"
 POOL_BIAS = ()
-LATE = 4
-MATMUL_JOBS = (2, 3, 4, 5, 6, 7, 8, 9, 10, 11)
+LATE = 6
+SOFT = 4
+CAP = 40.0
+EVAC = ()
+SOFT_AT = {17: (0, 1), 19: (2, 3)}
+CLAMP_AFTER = {7: (0, 1), 8: (2, 3)}
+EVAC_LAG = 6
+SPARE = 10
+MATMUL_JOBS = (2, 3, 4, 5, 6, 7, 8, 21, 23)
 COPY_LAG = 4
-COPY_AT = (1, 4)
+COPY_AT = (1, 2)
 
 
 def tile_kplanesgaussiananchordecoder_w4_kernel(
@@ -102,6 +109,10 @@ def tile_kplanesgaussiananchordecoder_w4_kernel(
         ident = keep.tile([128, 128], F32, name="ident")
         nc.scalar.activation(out=ident[:], in_=ident_bf[:], func=ACT.Copy)
 
+        if EVAC:
+            gain_f32 = keep.tile([128, 4], F32, name="gain_f32")
+            nc.gpsimd.tensor_copy(out=gain_f32[:], in_=channel_gain[:])
+
         steps = [(first, count, pl) for first, count in CHUNKS for pl in range(PLANES)]
         jobs = [(s, pl, first + i) for s, (first, count, pl) in enumerate(steps) for i in range(count)]
 
@@ -145,7 +156,8 @@ def tile_kplanesgaussiananchordecoder_w4_kernel(
         turned, grouped, codes, feature, partial, z_pair, z_codes, linear_out = ({} for i in range(8))
         first_job = [[s for s, pl, n in jobs].index(s) for s in range(len(steps))]
         pairs = JOBS // 2
-        spent_pair, diagonal = {}, {}
+        last = JOBS - 1
+        spent_pair, diagonal, both, whole, first = {}, {}, {}, [], {}
 
         def by_words(k):
             return MODES[k] in "WX"
@@ -273,15 +285,31 @@ def tile_kplanesgaussiananchordecoder_w4_kernel(
             words = work.tile([128, 128 * count], U32, name=name + "_words", tag=name + "_words", align_bytes=64, bufs=3)
             scales = work.tile([128, 128 * count], U8, name=name + "_scales", tag=name + "_scales", align_bytes=64, bufs=3)
             nc.vector.quantize_mx(out=words[:].bitcast(FP8X4), scales=scales[:], in_=source.rearrange("p j n t -> p (j n t)"))
+            whole.append((words[:].bitcast(FP8X4), scales[:]))
             return [(words[:, 128 * j : 128 * j + 128].bitcast(FP8X4), scales[:, 128 * j : 128 * j + 128]) for j in range(count)]
 
         def quantise_weights(k, count):
             for j, operand in enumerate(quantise(grouped[k // 2][:, k % 2 : k % 2 + count], count, "a")):
                 codes[k + j] = operand
+            both[k // 2] = whole[-1]
 
         def products(k):
             pl = jobs[k][1]
-            feature[k] = ps_f.tile([128, 4, 128], F32, name="feature", tag="f")
+            if k // 2 in EVAC:
+                feature[k] = ps_f.tile([128, 2, 256], F32, name="feature", tag="f")
+                for t in (2 * (k % 2), 2 * (k % 2) + 1):
+                    nc.tensor.matmul_mx(
+                        out=feature[k][:, t % 2, :],
+                        lhsT=feat_words[pl][:, 128 * t : 128 * t + 128].bitcast(FP8X4),
+                        lhsT_scale=feat_scales[pl][:, 128 * t : 128 * t + 128],
+                        rhs=both[k // 2][0],
+                        rhs_scale=both[k // 2][1],
+                        start=True,
+                        stop=True,
+                    )
+                return
+            pool_k, tag = (ps_d2, "d2") if k // 2 == SPARE else (ps_f, "f")
+            feature[k] = pool_k.tile([128, 4, 128], F32, name="feature", tag=tag)
             for t in range(4):
                 nc.tensor.matmul_mx(
                     out=feature[k][:, t, :],
@@ -295,12 +323,23 @@ def tile_kplanesgaussiananchordecoder_w4_kernel(
 
         def multiply(k):
             step, pl, n = jobs[k]
+            if k // 2 in EVAC:
+                if k // 2 not in first:
+                    first[k // 2] = work.tile([128, 4, 256], F32, name="first", bufs=1)
+                    for j in range(2):
+                        part = first[k // 2][:, :, 128 * j : 128 * j + 128]
+                        partial[jobs[k - k % 2 + j][2]] = part.rearrange("p t n -> p n t")
+                for t in (2 * (k % 2), 2 * (k % 2) + 1):
+                    nc.scalar.activation(
+                        out=first[k // 2][:, t, :], in_=feature[k][:, t % 2, :], func=ACT.Copy, scale=gain_f32[:, t : t + 1]
+                    )
+                return
             other = channel_gain[:].unsqueeze(1).to_broadcast([128, 128, 4]) if pl == 0 else partial[n][:]
             if pl < PLANES - 1:
                 partial[n] = work.tile([128, 128, 4], F32, name="partial", bufs=7)
                 result = partial[n][:]
             else:
-                if n % 2 == 0:
+                if n // 2 not in z_pair:
                     z_pair[n // 2] = work.tile([128, 2, 128, 4], BF16, name="z_pair", align_bytes=64)
                 result = z_pair[n // 2][:, n % 2]
             nc.vector.tensor_tensor(out=result, in0=feature[k][:].rearrange("p t n -> p n t"), in1=other, op=ALU.mult)
@@ -334,19 +373,30 @@ def tile_kplanesgaussiananchordecoder_w4_kernel(
         def pool_bias(n):
             nc.gpsimd.tensor_tensor(out=sums_b[:, n, :], in0=result_sb[:, n, :], in1=bias_row[:], op=ALU.add)
 
+        def clamp(n):
+            nc.gpsimd.tensor_scalar(
+                out=result_sb[:, n, :], in0=sums_b[:, n, :], scalar1=CAP, scalar2=-3.0e38, op0=ALU.min, op1=ALU.max
+            )
+
+        def soft_exp(n):
+            nc.scalar.activation(out=result_sb[:, n, :], in_=result_sb[:, n, :], func=ACT.Exp)
+
         def sigmoid(n, count):
             part = slice(n, n + count)
             nc.scalar.activation(out=result_sb[:, part, :], in_=sums_b[:, part, :], func=ACT.Sigmoid, scale=-1.0)
 
         def logarithm(n, lo, hi):
             part = result_sb[:, n, lo:hi]
-            nc.scalar.activation(out=part, in_=part, func=ACT.Ln, bias=TINY)
+            nc.scalar.activation(out=part, in_=part, func=ACT.Ln, bias=1.0 if n < SOFT else TINY)
 
         def finish(n, lo, hi):
             part = result_sb[:, n, lo:hi]
-            nc.vector.scalar_tensor_tensor(
-                out=part, in0=part, scalar=-1.0, in1=sums_b[:, n, lo:hi], op0=ALU.mult, op1=ALU.max
-            )
+            if n < SOFT:
+                nc.vector.tensor_tensor(out=part, in0=part, in1=sums_b[:, n, lo:hi], op=ALU.max)
+            else:
+                nc.vector.scalar_tensor_tensor(
+                    out=part, in0=part, scalar=-1.0, in1=sums_b[:, n, lo:hi], op0=ALU.mult, op1=ALU.max
+                )
             nc.sync.dma_start(out=out_tiles[:, n, lo:hi], in_=part)
 
         (widen0, inter0, quant0), (widen1, inter1, quant1), (widen2, inter2, quant2) = map(feat_parts, range(PLANES))
@@ -384,9 +434,12 @@ def tile_kplanesgaussiananchordecoder_w4_kernel(
             if stage == quantise_weights:
                 return [(group, i + j) for j in range(rest[0])]
             if stage == products:
-                return [(quantise_weights, i), (multiply, i - 2), (feat, feat_ready[jobs[i][1]])]
+                gone = i // 2 - (2 if i // 2 - 1 == SPARE else 1)
+                bank = (minimum, last) if i // 2 == SPARE else (multiply, 2 * gone + 1 - i % 2)
+                return [(quantise_weights, i), bank, (feat, feat_ready[jobs[i][1]])]
             if stage == multiply:
-                return [(products, i)]
+                earlier = [(multiply, i - i % 2 - 2 + j) for j in range(2) if i // 2 - 1 in EVAC]
+                return [(products, i)] + earlier
             if stage == quantise_z:
                 return [(multiply, last_job(i + j)) for j in range(rest[0])]
             if stage == linear:
@@ -397,8 +450,12 @@ def tile_kplanesgaussiananchordecoder_w4_kernel(
                 return [(bias, i)]
             if stage == sigmoid:
                 return [(pool_bias if i + j in POOL_BIAS else bias, i + j) for j in range(rest[0])]
+            if stage == clamp:
+                return [(bias, i)]
+            if stage == soft_exp:
+                return [(clamp, i)]
             if stage == logarithm:
-                return [(sigmoid, i)]
+                return [(sigmoid if i >= SOFT else soft_exp, i)]
             if stage == finish:
                 return [(logarithm, i, rest[0])]
             return []
@@ -423,7 +480,6 @@ def tile_kplanesgaussiananchordecoder_w4_kernel(
 
         feat_left = list(range(len(feat_order)))
         squares_left = list(range(8 * len(steps)))
-        last = JOBS - 1
 
         def more_feat(count):
             vector.extend((feat, feat_left.pop(0)) for i in range(min(count, len(feat_left))))
@@ -444,10 +500,12 @@ def tile_kplanesgaussiananchordecoder_w4_kernel(
             vector.append((minimum, k))
             scalar.append((exponential, k))
             if k % 2 == 0:
-                scalar.extend((normalise, j) for j in (k - 2, k - 1) if j >= 0 and MODES[j] == "D")
-            if k >= COPY_LAG and by_words(k - COPY_LAG):
+                scalar.extend((normalise, j) for j in (k - 2, k - 1) if 0 <= j and MODES[j] == "D")
+            if COPY_LAG <= k and by_words(k - COPY_LAG):
                 scalar.append((group, k - COPY_LAG))
+            scalar.extend((multiply, 2 * r + j) for r in EVAC for j in range(2) if k == 2 * r + EVAC_LAG)
             paced_squares(k)
+            scalar.extend((soft_exp, n) for n in SOFT_AT.get(k, ()))
             if k + 2 < JOBS:
                 tensor.append((distances, k + 2))
 
@@ -481,6 +539,9 @@ def tile_kplanesgaussiananchordecoder_w4_kernel(
         scalar += [(square, squares_left.pop(0)) for i in range(8 + SQUARES_AHEAD)]
         tensor += [(distances, 0), (distances, 1)]
         more_feat(FEAT_AHEAD)
+        def multiplies(r):
+            return [] if r in EVAC else [(multiply, 2 * r + 1), (multiply, 2 * r)]
+
         for r in range(pairs - 1):
             spent_pair[r] = r - 2
             front(2 * r)
@@ -490,65 +551,58 @@ def tile_kplanesgaussiananchordecoder_w4_kernel(
             vector += [(normalise, k) for k in (2 * r - 2, 2 * r - 1) if k >= 0 and MODES[k] == "V"]
             if r >= 2:
                 gains(r - 2)
-            if r < pairs - 2:
-                next_bias()
+            next_bias()
             if r >= 1:
                 tensor += [(turn, k) for k in sorted((2 * r - 2, 2 * r - 1), key=by_words)]
             front(2 * r + 1)
             more_feat(FEAT_A_SLOT)
+            next_bias()
             if r >= 3:
-                vector.append((multiply, 2 * r - 6))
+                vector += multiplies(r - 3)
             if r >= 2:
                 weights_to_products(r - 2)
-            if closes(r - 4):
-                close(jobs[2 * r - 8][2], 2)
-            if r >= 3:
-                vector.append((multiply, 2 * r - 5))
+            if closes(r - 3):
+                close(jobs[2 * r - 6][2], 2)
 
-        spent_pair[11] = None
+        spent_pair[11] = 10
         front(22)
         vector.append((reciprocal, 10))
         gains(9)
-        front(23)
         tensor += [(turn, 21), (turn, 20)]
-        next_bias()
-        vector.append((reciprocal, 11))
-        vector.append((multiply, 16))
+        front(23)
+        vector += multiplies(8)
         weights_to_products(9)
-        vector.append((multiply, 17))
-        next_bias()
-        gains(10)
-        next_bias()
-        tensor += [(turn, 22), (turn, 23)]
         close(4, 2)
-        vector.append((multiply, 18))
-        weights_to_products(10)
-        vector.append((multiply, 19))
+        vector.append((reciprocal, 11))
+        gains(10)
+        tensor += [(turn, 22)]
+        next_bias()
+        next_bias()
+        vector += multiplies(9)[:1]
+        vector.append((quantise_weights, 20, 2))
+        tensor += [(turn, 23), (products, 20), (products, 21)]
+        vector += multiplies(9)[1:]
         gains(11)
-        vector.append((multiply, 20))
-        weights_to_products(11)
-        vector.append((multiply, 21))
-        next_bias()
-        next_bias()
+        vector += [(quantise_weights, 22, 1), (multiply, 20), (quantise_weights, 23, 1), (multiply, 21)]
+        tensor += [(products, 22), (products, 23)]
         vector += [(multiply, 22), (multiply, 23)]
         close(6, 1)
         close(7, 1)
-        vector += [(finish, 0, 0, H)] if LATE else []
+        vector += [(finish, 0, 0, H)]
         next_bias()
         next_bias()
         parts = [(LATE, 0, H // 2), (LATE, H // 2, H)] + [(n, 0, H) for n in range(LATE + 1, TILES - 1)]
         parts += [(TILES - 1, 0, H // 2), (TILES - 1, H // 2, H)]
         vector += [(finish, n, 0, H) for n in range(1, LATE)] + [(finish, *part) for part in parts]
-        copies = [(group, k) for k in range(JOBS - COPY_LAG, JOBS) if by_words(k)]
-        early = [(normalise, k) for k in (last - 1, last) if MODES[k] == "D"]
-        early += [(sigmoid, 0, 2), (sigmoid, 2, 1), (sigmoid, 3, 1)] + [(logarithm, n, 0, H) for n in range(LATE)]
+        scalar += [(group, 20)]
+        early = [(sigmoid, n, 1) for n in range(SOFT, LATE)] + [(logarithm, n, 0, H) for n in range(LATE)]
+        copies = [(normalise, k) for k in (22, 23) if MODES[k] == "D"]
         for place, copy in zip(COPY_AT, copies):
             early.insert(place, copy)
-        for n in POOL_BIAS:
-            early.insert(early.index((logarithm, 1, 0, H)) if LATE else len(early), (bias, n))
-        scalar += early + [(sigmoid, n, 1) for n in range(4, TILES)] + [(logarithm, *part) for part in parts]
+        scalar += early + [(sigmoid, n, 1) for n in range(LATE, TILES)] + [(logarithm, *part) for part in parts]
         for r in range(pairs):
             pool += [(pool_gain, k) for k in (2 * r, 2 * r + 1) if by_words(k)]
             pool += [(normalise, k) for k in (2 * r, 2 * r + 1) if MODES[k] in "AW"]
+            pool += [(clamp, n) for n in CLAMP_AFTER.get(r, ())]
         pool += [(pool_bias, n) for n in POOL_BIAS]
         issue([vector, scalar, pool, tensor])

@@ -31,11 +31,16 @@ MARGIN = 1
 MODES = "VVAAAAWDWDWDWDWDWDWDWDAA"
 POOL_BIAS = ()
 LATE = 6
-SOFT = 4
+SOFT = 3
+COPY20 = 1
+BEFORE = 1
+BIASES = {8: 2, 9: 1, 10: 1}
+EXTRA = {}
+POOL_DIAG = ()
 CAP = 40.0
 EVAC = ()
-SOFT_AT = {17: (0, 1), 19: (2, 3)}
-CLAMP_AFTER = {7: (0, 1), 8: (2, 3)}
+SOFT_AT = {17: (0,), 19: (1,), 21: (2,)}
+CLAMP_AFTER = {7: (0,), 8: (1,), 9: (2,)}
 EVAC_LAG = 6
 SPARE = 10
 MATMUL_JOBS = (2, 3, 4, 5, 6, 7, 8, 21, 23)
@@ -248,7 +253,12 @@ def tile_kplanesgaussiananchordecoder_w4_kernel(
                 source, target = gained[k], weights[k][:]
             if MODES[k] == "D":
                 diagonal[k] = work.tile([128, 128], F32, name="diagonal")
-                nc.scalar.activation(out=diagonal[k][:], in_=ident[:], func=ACT.Copy, scale=factor)
+                if k in POOL_DIAG:
+                    nc.gpsimd.tensor_scalar(
+                        out=diagonal[k][:], in0=ident[:], scalar1=factor, scalar2=1.0, op0=ALU.mult, op1=ALU.mult
+                    )
+                else:
+                    nc.scalar.activation(out=diagonal[k][:], in_=ident[:], func=ACT.Copy, scale=factor)
             elif MODES[k] == "X":
                 nc.scalar.activation(out=target, in_=source, func=ACT.Copy, scale=factor)
             elif MODES[k] == "V":
@@ -492,6 +502,7 @@ def tile_kplanesgaussiananchordecoder_w4_kernel(
             for s in range(len(steps)):
                 left = sum(steps[q // 8][1] for q in squares_left if q // 8 <= s)
                 need = max(need, left / max(first_job[s] - 1 - MARGIN - k, 1))
+            need += EXTRA.get(k, 0)
             while squares_left and need > 0:
                 need -= steps[squares_left[0] // 8][1]
                 scalar.append((square, squares_left.pop(0)))
@@ -500,7 +511,7 @@ def tile_kplanesgaussiananchordecoder_w4_kernel(
             vector.append((minimum, k))
             scalar.append((exponential, k))
             if k % 2 == 0:
-                scalar.extend((normalise, j) for j in (k - 2, k - 1) if 0 <= j and MODES[j] == "D")
+                scalar.extend((normalise, j) for j in (k - 2, k - 1) if 0 <= j and MODES[j] == "D" and j not in POOL_DIAG)
             if COPY_LAG <= k and by_words(k - COPY_LAG):
                 scalar.append((group, k - COPY_LAG))
             scalar.extend((multiply, 2 * r + j) for r in EVAC for j in range(2) if k == 2 * r + EVAC_LAG)
@@ -551,12 +562,14 @@ def tile_kplanesgaussiananchordecoder_w4_kernel(
             vector += [(normalise, k) for k in (2 * r - 2, 2 * r - 1) if k >= 0 and MODES[k] == "V"]
             if r >= 2:
                 gains(r - 2)
-            next_bias()
+            if BIASES.get(r, 0) >= 1:
+                next_bias()
             if r >= 1:
                 tensor += [(turn, k) for k in sorted((2 * r - 2, 2 * r - 1), key=by_words)]
             front(2 * r + 1)
             more_feat(FEAT_A_SLOT)
-            next_bias()
+            if BIASES.get(r, 0) >= 2:
+                next_bias()
             if r >= 3:
                 vector += multiplies(r - 3)
             if r >= 2:
@@ -571,8 +584,9 @@ def tile_kplanesgaussiananchordecoder_w4_kernel(
         tensor += [(turn, 21), (turn, 20)]
         front(23)
         vector += multiplies(8)
-        weights_to_products(9)
+        vector.append((quantise_weights, 18, 2))
         close(4, 2)
+        tensor += [(products, 18), (products, 19)]
         vector.append((reciprocal, 11))
         gains(10)
         tensor += [(turn, 22)]
@@ -585,23 +599,24 @@ def tile_kplanesgaussiananchordecoder_w4_kernel(
         gains(11)
         vector += [(quantise_weights, 22, 1), (multiply, 20), (quantise_weights, 23, 1), (multiply, 21)]
         tensor += [(products, 22), (products, 23)]
-        vector += [(multiply, 22), (multiply, 23)]
+        vector += [(finish, n, 0, H) for n in range(BEFORE - 1)] + [(multiply, 22), (multiply, 23)]
         close(6, 1)
         close(7, 1)
-        vector += [(finish, 0, 0, H)]
+        vector += [(finish, BEFORE - 1, 0, H)]
         next_bias()
         next_bias()
         parts = [(LATE, 0, H // 2), (LATE, H // 2, H)] + [(n, 0, H) for n in range(LATE + 1, TILES - 1)]
         parts += [(TILES - 1, 0, H // 2), (TILES - 1, H // 2, H)]
-        vector += [(finish, n, 0, H) for n in range(1, LATE)] + [(finish, *part) for part in parts]
-        scalar += [(group, 20)]
+        vector += [(finish, n, 0, H) for n in range(BEFORE, LATE)] + [(finish, *part) for part in parts]
         early = [(sigmoid, n, 1) for n in range(SOFT, LATE)] + [(logarithm, n, 0, H) for n in range(LATE)]
+        early.insert(COPY20, (group, 20))
         copies = [(normalise, k) for k in (22, 23) if MODES[k] == "D"]
         for place, copy in zip(COPY_AT, copies):
             early.insert(place, copy)
         scalar += early + [(sigmoid, n, 1) for n in range(LATE, TILES)] + [(logarithm, *part) for part in parts]
         for r in range(pairs):
             pool += [(pool_gain, k) for k in (2 * r, 2 * r + 1) if by_words(k)]
+            pool += [(normalise, k) for k in (2 * r + 1, 2 * r) if MODES[k] == "D" and k in POOL_DIAG]
             pool += [(normalise, k) for k in (2 * r, 2 * r + 1) if MODES[k] in "AW"]
             pool += [(clamp, n) for n in CLAMP_AFTER.get(r, ())]
         pool += [(pool_bias, n) for n in POOL_BIAS]

@@ -28,22 +28,23 @@ FEAT_AHEAD = 14
 FEAT_A_SLOT = 2
 SQUARES_AHEAD = 3
 MARGIN = 1
-MODES = "VVAAAAWDWDWDWDWDWDWDWDAA"
+MODES = "VVAAWDWDWDWDWDWDWDWDWDAA"
 POOL_BIAS = ()
 LATE = 6
 SOFT = 3
+RECIP_LATE = (1, 3, 4, 5, 6, 7, 8, 9, 10)
 COPY20 = 1
 BEFORE = 1
 BIASES = {8: 2, 9: 1, 10: 1}
 EXTRA = {}
-POOL_DIAG = ()
+POOL_DIAG = (5, 7, 9, 11, 13)
 CAP = 40.0
 EVAC = ()
 SOFT_AT = {17: (0,), 19: (1,), 21: (2,)}
 CLAMP_AFTER = {7: (0,), 8: (1,), 9: (2,)}
 EVAC_LAG = 6
 SPARE = 10
-MATMUL_JOBS = (2, 3, 4, 5, 6, 7, 8, 21, 23)
+MATMUL_JOBS = (2, 3, 4, 5, 6, 7, 21)
 COPY_LAG = 4
 COPY_AT = (1, 2)
 
@@ -399,6 +400,10 @@ def tile_kplanesgaussiananchordecoder_w4_kernel(
             part = result_sb[:, n, lo:hi]
             nc.scalar.activation(out=part, in_=part, func=ACT.Ln, bias=1.0 if n < SOFT else TINY)
 
+        def logarithms(n, count):
+            part = result_sb[:, n : n + count, :]
+            nc.scalar.activation(out=part, in_=part, func=ACT.Ln, bias=1.0 if n < SOFT else TINY)
+
         def finish(n, lo, hi):
             part = result_sb[:, n, lo:hi]
             if n < SOFT:
@@ -466,8 +471,10 @@ def tile_kplanesgaussiananchordecoder_w4_kernel(
                 return [(clamp, i)]
             if stage == logarithm:
                 return [(sigmoid if i >= SOFT else soft_exp, i)]
+            if stage == logarithms:
+                return [(sigmoid if i >= SOFT else soft_exp, i + j) for j in range(rest[0])]
             if stage == finish:
-                return [(logarithm, i, rest[0])]
+                return [(logarithm, i, rest[0]) if i >= LATE else (logarithms, i)]
             return []
 
         def issue(orders):
@@ -477,7 +484,7 @@ def tile_kplanesgaussiananchordecoder_w4_kernel(
                     while order and all(need in made or need[1] < 0 for need in needs(*order[0])):
                         stage, i, *rest = order.pop(0)
                         stage(i, *rest)
-                        counted = stage in (quantise_weights, quantise_z, sigmoid)
+                        counted = stage in (quantise_weights, quantise_z, sigmoid, logarithms)
                         made.update((stage, i + j) for j in range(rest[0] if counted else 1))
                         if stage == logarithm:
                             made.add((stage, i, rest[0]))
@@ -556,12 +563,14 @@ def tile_kplanesgaussiananchordecoder_w4_kernel(
         for r in range(pairs - 1):
             spent_pair[r] = r - 2
             front(2 * r)
-            if r >= 1:
+            if r >= 1 and r not in RECIP_LATE:
                 vector.append((reciprocal, r - 1))
             more_feat(FEAT_A_SLOT)
-            vector += [(normalise, k) for k in (2 * r - 2, 2 * r - 1) if k >= 0 and MODES[k] == "V"]
             if r >= 2:
                 gains(r - 2)
+            if r in RECIP_LATE:
+                vector.append((reciprocal, r - 1))
+            vector += [(normalise, k) for k in (2 * r - 2, 2 * r - 1) if k >= 0 and MODES[k] == "V"]
             if BIASES.get(r, 0) >= 1:
                 next_bias()
             if r >= 1:
@@ -608,7 +617,7 @@ def tile_kplanesgaussiananchordecoder_w4_kernel(
         parts = [(LATE, 0, H // 2), (LATE, H // 2, H)] + [(n, 0, H) for n in range(LATE + 1, TILES - 1)]
         parts += [(TILES - 1, 0, H // 2), (TILES - 1, H // 2, H)]
         vector += [(finish, n, 0, H) for n in range(BEFORE, LATE)] + [(finish, *part) for part in parts]
-        early = [(sigmoid, n, 1) for n in range(SOFT, LATE)] + [(logarithm, n, 0, H) for n in range(LATE)]
+        early = [(sigmoid, n, 1) for n in range(SOFT, LATE)] + [(logarithms, 0, SOFT), (logarithms, SOFT, LATE - SOFT)]
         early.insert(COPY20, (group, 20))
         copies = [(normalise, k) for k in (22, 23) if MODES[k] == "D"]
         for place, copy in zip(COPY_AT, copies):

@@ -22,31 +22,19 @@ TILES = N // 128
 JOBS = TILES * PLANES
 TINY = 2.0**-60
 
+CAP = 40.0
+LOWEST = -3.0e38
+
 CHUNKS = ((0, 4), (4, 2), (6, 2))
 MATMUL_BLOCKS = (0, 3)
 FEAT_AHEAD = 14
 FEAT_A_SLOT = 2
 SQUARES_AHEAD = 3
 MARGIN = 1
-MODES = "VVAAWDWDWDWDWDWDWDWDWDAA"
-POOL_BIAS = ()
-LATE = 6
-SOFT = 3
-RECIP_LATE = (1, 3, 4, 5, 6, 7, 8, 9, 10)
-COPY20 = 1
-BEFORE = 1
-BIASES = {8: 2, 9: 1, 10: 1}
-EXTRA = {}
-POOL_DIAG = (5, 7, 9, 11, 13)
-CAP = 40.0
-EVAC = ()
-SOFT_AT = {17: (0,), 19: (1,), 21: (2,)}
-CLAMP_AFTER = {7: (0,), 8: (1,), 9: (2,)}
-EVAC_LAG = 6
-SPARE = 10
-MATMUL_JOBS = (2, 3, 4, 5, 6, 7, 21)
-COPY_LAG = 4
-COPY_AT = (1, 2)
+EXP_TILES = 3
+EARLY_TILES = TILES - 2
+EXPO_BUFFERS = 10
+VECTOR, POOL, WORDS, DIAGONAL = "vector", "pool", "words", "diagonal"
 
 
 def tile_kplanesgaussiananchordecoder_w4_kernel(
@@ -115,10 +103,6 @@ def tile_kplanesgaussiananchordecoder_w4_kernel(
         ident = keep.tile([128, 128], F32, name="ident")
         nc.scalar.activation(out=ident[:], in_=ident_bf[:], func=ACT.Copy)
 
-        if EVAC:
-            gain_f32 = keep.tile([128, 4], F32, name="gain_f32")
-            nc.gpsimd.tensor_copy(out=gain_f32[:], in_=channel_gain[:])
-
         steps = [(first, count, pl) for first, count in CHUNKS for pl in range(PLANES)]
         jobs = [(s, pl, first + i) for s, (first, count, pl) in enumerate(steps) for i in range(count)]
 
@@ -163,10 +147,24 @@ def tile_kplanesgaussiananchordecoder_w4_kernel(
         first_job = [[s for s, pl, n in jobs].index(s) for s in range(len(steps))]
         pairs = JOBS // 2
         last = JOBS - 1
-        spent_pair, diagonal, both, whole, first = {}, {}, {}, [], {}
+        diagonal = {}
+        first_bias = [jobs[2 * r][1] for r in range(pairs)].index(PLANES - 1) + 4
+
+        def road(k):
+            if k < 2:
+                return VECTOR
+            if k // 2 in (1, pairs - 1):
+                return POOL
+            return DIAGONAL if k % 2 else WORDS
 
         def by_words(k):
-            return MODES[k] in "WX"
+            return road(k) == WORDS
+
+        def diagonal_on_pool(k):
+            return road(k) == DIAGONAL and k // 2 < first_bias - 1
+
+        def keeps_clock(k):
+            return 2 <= k < 2 * CHUNKS[0][1] or k == last - 2
 
         def square(q):
             step, within = divmod(q, 8)
@@ -199,7 +197,7 @@ def tile_kplanesgaussiananchordecoder_w4_kernel(
                         rhs=ident[:],
                         start=(axis == 0),
                         stop=(axis == 1),
-                        is_transpose=not (axis == 0 and t in MATMUL_BLOCKS and k in MATMUL_JOBS),
+                        is_transpose=not (axis == 0 and t in MATMUL_BLOCKS and keeps_clock(k)),
                     )
 
         def minimum(k):
@@ -207,8 +205,8 @@ def tile_kplanesgaussiananchordecoder_w4_kernel(
             least = work.tile([128, 1], F32, name="least", bufs=3)
             target, source = values[:], distance[k][:].rearrange("n t p -> n (t p)")
             if by_words(k):
-                target = values[:].rearrange("n (u p e) -> n u p e", u=2, e=2)
-                source = distance[k][:].rearrange("n (u e) p -> n u p e", u=2)
+                target = values[:].rearrange("n (p t) -> n p t", t=4)
+                source = distance[k][:].rearrange("n t p -> n p t")
             nc.vector.tensor_scalar(
                 out=target, in0=source, scalar1=1.0 / WIDTH2, scalar2=None, op0=ALU.mult, op1=ALU.min, accum_out=least[:]
             )
@@ -216,7 +214,7 @@ def tile_kplanesgaussiananchordecoder_w4_kernel(
 
         def exponential(k):
             values, least = scaled[k]
-            expo[k] = work.tile([128, M], F32, name="expo", bufs=10)
+            expo[k] = work.tile([128, M], F32, name="expo", bufs=EXPO_BUFFERS)
             if k % 2 == 0:
                 sums[k // 2] = work.tile([128, 2], F32, name="sums", bufs=3)
             nc.scalar.activation(
@@ -232,38 +230,24 @@ def tile_kplanesgaussiananchordecoder_w4_kernel(
             recips[r] = work.tile([128, 2], F32, name="recips", bufs=3)
             nc.vector.reciprocal(out=recips[r][:], in_=sums[r][:])
 
-        def spent(k):
-            return spent_pair[k // 2] if MODES[k] == "W" else None
-
         def pool_gain(k):
-            gained[k] = expo[k][:]
-            if spent(k) is not None:
-                gained[k] = grouped[spent(k)][:].rearrange("p j n t -> p (j n t)").bitcast(F32)
-            nc.gpsimd.tensor_tensor(
-                out=gained[k].rearrange("n (u p e) -> n u p e", u=2, e=2),
-                in0=expo[k][:].rearrange("n (u p e) -> n u p e", u=2, e=2),
-                in1=gain_all[:, jobs[k][1], :].rearrange("n (p u e) -> n u p e", u=2, e=2),
-                op=ALU.mult,
-            )
+            gained[k] = grouped[k // 2 - 2][:].rearrange("p j n t -> p (j n t)").bitcast(F32)
+            nc.gpsimd.tensor_tensor(out=gained[k], in0=expo[k][:], in1=gain_all[:, jobs[k][1], :], op=ALU.mult)
 
         def normalise(k):
             source = target = expo[k][:]
             factor = recips[k // 2][:, k % 2 : k % 2 + 1]
-            if by_words(k):
+            if road(k) == WORDS:
                 weights[k] = work.tile([128, M], BF16, name="weights", bufs=4)
-                source, target = gained[k], weights[k][:]
-            if MODES[k] == "D":
+                source = gained[k].rearrange("n (p u e) -> n u p e", u=2, e=2)
+                target = weights[k][:].rearrange("n (u p e) -> n u p e", u=2, e=2)
+            if road(k) == DIAGONAL:
                 diagonal[k] = work.tile([128, 128], F32, name="diagonal")
-                if k in POOL_DIAG:
-                    nc.gpsimd.tensor_scalar(
-                        out=diagonal[k][:], in0=ident[:], scalar1=factor, scalar2=1.0, op0=ALU.mult, op1=ALU.mult
-                    )
-                else:
-                    nc.scalar.activation(out=diagonal[k][:], in_=ident[:], func=ACT.Copy, scale=factor)
-            elif MODES[k] == "X":
-                nc.scalar.activation(out=target, in_=source, func=ACT.Copy, scale=factor)
-            elif MODES[k] == "V":
+                source, target = ident[:], diagonal[k][:]
+            if road(k) == VECTOR:
                 nc.vector.tensor_scalar(out=target, in0=source, scalar1=factor, scalar2=None, op0=ALU.mult)
+            elif road(k) == DIAGONAL and not diagonal_on_pool(k):
+                nc.scalar.activation(out=target, in_=source, func=ACT.Copy, scale=factor)
             else:
                 nc.gpsimd.tensor_scalar(out=target, in0=source, scalar1=factor, scalar2=1.0, op0=ALU.mult, op1=ALU.mult)
 
@@ -273,7 +257,7 @@ def tile_kplanesgaussiananchordecoder_w4_kernel(
             turned[k] = ps_xt.tile([128, blocks, 128], F32, name="turned", tag="xt")
             for t in range(blocks):
                 block = source[:, 128 * t : 128 * t + 128]
-                if MODES[k] == "D":
+                if road(k) == DIAGONAL:
                     nc.tensor.matmul(out=turned[k][:, t, :], lhsT=block, rhs=diagonal[k][:], start=True, stop=True)
                 else:
                     nc.tensor.transpose(turned[k][:, t, :], block, ident[:])
@@ -295,32 +279,19 @@ def tile_kplanesgaussiananchordecoder_w4_kernel(
         def quantise(source, count, name):
             words = work.tile([128, 128 * count], U32, name=name + "_words", tag=name + "_words", align_bytes=64, bufs=3)
             scales = work.tile([128, 128 * count], U8, name=name + "_scales", tag=name + "_scales", align_bytes=64, bufs=3)
-            nc.vector.quantize_mx(out=words[:].bitcast(FP8X4), scales=scales[:], in_=source.rearrange("p j n t -> p (j n t)"))
-            whole.append((words[:].bitcast(FP8X4), scales[:]))
-            return [(words[:, 128 * j : 128 * j + 128].bitcast(FP8X4), scales[:, 128 * j : 128 * j + 128]) for j in range(count)]
+            flat = source.rearrange("p j n t -> p (j n t)")
+            nc.vector.quantize_mx(out=words[:].bitcast(FP8X4), scales=scales[:], in_=flat)
+            columns = [slice(128 * j, 128 * j + 128) for j in range(count)]
+            return [(words[:, part].bitcast(FP8X4), scales[:, part]) for part in columns]
 
         def quantise_weights(k, count):
             for j, operand in enumerate(quantise(grouped[k // 2][:, k % 2 : k % 2 + count], count, "a")):
                 codes[k + j] = operand
-            both[k // 2] = whole[-1]
 
         def products(k):
             pl = jobs[k][1]
-            if k // 2 in EVAC:
-                feature[k] = ps_f.tile([128, 2, 256], F32, name="feature", tag="f")
-                for t in (2 * (k % 2), 2 * (k % 2) + 1):
-                    nc.tensor.matmul_mx(
-                        out=feature[k][:, t % 2, :],
-                        lhsT=feat_words[pl][:, 128 * t : 128 * t + 128].bitcast(FP8X4),
-                        lhsT_scale=feat_scales[pl][:, 128 * t : 128 * t + 128],
-                        rhs=both[k // 2][0],
-                        rhs_scale=both[k // 2][1],
-                        start=True,
-                        stop=True,
-                    )
-                return
-            pool_k, tag = (ps_d2, "d2") if k // 2 == SPARE else (ps_f, "f")
-            feature[k] = pool_k.tile([128, 4, 128], F32, name="feature", tag=tag)
+            banks, tag = (ps_d2, "d2") if k // 2 == pairs - 2 else (ps_f, "f")
+            feature[k] = banks.tile([128, 4, 128], F32, name="feature", tag=tag)
             for t in range(4):
                 nc.tensor.matmul_mx(
                     out=feature[k][:, t, :],
@@ -334,17 +305,6 @@ def tile_kplanesgaussiananchordecoder_w4_kernel(
 
         def multiply(k):
             step, pl, n = jobs[k]
-            if k // 2 in EVAC:
-                if k // 2 not in first:
-                    first[k // 2] = work.tile([128, 4, 256], F32, name="first", bufs=1)
-                    for j in range(2):
-                        part = first[k // 2][:, :, 128 * j : 128 * j + 128]
-                        partial[jobs[k - k % 2 + j][2]] = part.rearrange("p t n -> p n t")
-                for t in (2 * (k % 2), 2 * (k % 2) + 1):
-                    nc.scalar.activation(
-                        out=first[k // 2][:, t, :], in_=feature[k][:, t % 2, :], func=ACT.Copy, scale=gain_f32[:, t : t + 1]
-                    )
-                return
             other = channel_gain[:].unsqueeze(1).to_broadcast([128, 128, 4]) if pl == 0 else partial[n][:]
             if pl < PLANES - 1:
                 partial[n] = work.tile([128, 128, 4], F32, name="partial", bufs=7)
@@ -376,37 +336,31 @@ def tile_kplanesgaussiananchordecoder_w4_kernel(
         out_tiles = out.rearrange("(j p) h -> p j h", p=128)
 
         def bias(n):
-            if n in POOL_BIAS:
-                nc.scalar.copy(out=result_sb[:, n, :], in_=linear_out[n][:])
-            else:
-                nc.vector.tensor_tensor(out=sums_b[:, n, :], in0=linear_out[n][:], in1=bias_row[:], op=ALU.add)
+            nc.vector.tensor_tensor(out=sums_b[:, n, :], in0=linear_out[n][:], in1=bias_row[:], op=ALU.add)
 
-        def pool_bias(n):
-            nc.gpsimd.tensor_tensor(out=sums_b[:, n, :], in0=result_sb[:, n, :], in1=bias_row[:], op=ALU.add)
-
-        def clamp(n):
+        def cap(n):
             nc.gpsimd.tensor_scalar(
-                out=result_sb[:, n, :], in0=sums_b[:, n, :], scalar1=CAP, scalar2=-3.0e38, op0=ALU.min, op1=ALU.max
+                out=result_sb[:, n, :], in0=sums_b[:, n, :], scalar1=CAP, scalar2=LOWEST, op0=ALU.min, op1=ALU.max
             )
 
         def soft_exp(n):
             nc.scalar.activation(out=result_sb[:, n, :], in_=result_sb[:, n, :], func=ACT.Exp)
 
-        def sigmoid(n, count):
-            part = slice(n, n + count)
+        def sigmoid(n):
+            part = slice(n, n + 1)
             nc.scalar.activation(out=result_sb[:, part, :], in_=sums_b[:, part, :], func=ACT.Sigmoid, scale=-1.0)
-
-        def logarithm(n, lo, hi):
-            part = result_sb[:, n, lo:hi]
-            nc.scalar.activation(out=part, in_=part, func=ACT.Ln, bias=1.0 if n < SOFT else TINY)
 
         def logarithms(n, count):
             part = result_sb[:, n : n + count, :]
-            nc.scalar.activation(out=part, in_=part, func=ACT.Ln, bias=1.0 if n < SOFT else TINY)
+            nc.scalar.activation(out=part, in_=part, func=ACT.Ln, bias=1.0 if n < EXP_TILES else TINY)
+
+        def logarithm(n, lo, hi):
+            part = result_sb[:, n, lo:hi]
+            nc.scalar.activation(out=part, in_=part, func=ACT.Ln, bias=TINY)
 
         def finish(n, lo, hi):
             part = result_sb[:, n, lo:hi]
-            if n < SOFT:
+            if n < EXP_TILES:
                 nc.vector.tensor_tensor(out=part, in0=part, in1=sums_b[:, n, lo:hi], op=ALU.max)
             else:
                 nc.vector.scalar_tensor_tensor(
@@ -427,19 +381,19 @@ def tile_kplanesgaussiananchordecoder_w4_kernel(
         made = set()
 
         def needs(stage, i, *rest):
-            if stage == distances:
-                return [(square, 8 * jobs[i][0] + 7), (minimum, i - 2)]
             if stage == square:
                 same = [s for s in range(i // 8) if steps[s][1] == steps[i // 8][1]]
                 return [(distances, first_job[same[-3]] + steps[same[-3]][1] - 1)] if len(same) >= 3 else []
+            if stage == distances:
+                return [(square, 8 * jobs[i][0] + 7), (minimum, i - 2)]
             if stage == minimum:
                 return [(distances, i), (exponential, i - 3)]
             if stage == exponential:
-                return [(minimum, i), (turn, i - 10)]
+                return [(minimum, i), (turn, i - EXPO_BUFFERS)]
             if stage == reciprocal:
                 return [(exponential, 2 * i + 1)]
             if stage == pool_gain:
-                return [(exponential, i)] + ([(quantise_weights, 2 * spent(i))] if spent(i) is not None else [])
+                return [(exponential, i), (quantise_weights, i - 4)]
             if stage == normalise:
                 return [(reciprocal, i // 2)] + ([(pool_gain, i)] if by_words(i) else [])
             if stage == turn:
@@ -449,32 +403,27 @@ def tile_kplanesgaussiananchordecoder_w4_kernel(
             if stage == quantise_weights:
                 return [(group, i + j) for j in range(rest[0])]
             if stage == products:
-                gone = i // 2 - (2 if i // 2 - 1 == SPARE else 1)
-                bank = (minimum, last) if i // 2 == SPARE else (multiply, 2 * gone + 1 - i % 2)
+                before = i // 2 - (2 if i // 2 == pairs - 1 else 1)
+                bank = (minimum, last) if i // 2 == pairs - 2 else (multiply, 2 * before + 1 - i % 2)
                 return [(quantise_weights, i), bank, (feat, feat_ready[jobs[i][1]])]
             if stage == multiply:
-                earlier = [(multiply, i - i % 2 - 2 + j) for j in range(2) if i // 2 - 1 in EVAC]
-                return [(products, i)] + earlier
+                return [(products, i)]
             if stage == quantise_z:
                 return [(multiply, last_job(i + j)) for j in range(rest[0])]
             if stage == linear:
                 return [(quantise_z, i), (bias, i - 2)]
             if stage == bias:
                 return [(linear, i)]
-            if stage == pool_bias:
-                return [(bias, i)]
-            if stage == sigmoid:
-                return [(pool_bias if i + j in POOL_BIAS else bias, i + j) for j in range(rest[0])]
-            if stage == clamp:
+            if stage in (cap, sigmoid):
                 return [(bias, i)]
             if stage == soft_exp:
-                return [(clamp, i)]
-            if stage == logarithm:
-                return [(sigmoid if i >= SOFT else soft_exp, i)]
+                return [(cap, i)]
             if stage == logarithms:
-                return [(sigmoid if i >= SOFT else soft_exp, i + j) for j in range(rest[0])]
+                return [(soft_exp if i < EXP_TILES else sigmoid, i + j) for j in range(rest[0])]
+            if stage == logarithm:
+                return [(sigmoid, i)]
             if stage == finish:
-                return [(logarithm, i, rest[0]) if i >= LATE else (logarithms, i)]
+                return [(logarithms, i) if i < EARLY_TILES else (logarithm, i, rest[0])]
             return []
 
         def issue(orders):
@@ -484,8 +433,8 @@ def tile_kplanesgaussiananchordecoder_w4_kernel(
                     while order and all(need in made or need[1] < 0 for need in needs(*order[0])):
                         stage, i, *rest = order.pop(0)
                         stage(i, *rest)
-                        counted = stage in (quantise_weights, quantise_z, sigmoid, logarithms)
-                        made.update((stage, i + j) for j in range(rest[0] if counted else 1))
+                        several = stage in (quantise_weights, quantise_z, logarithms)
+                        made.update((stage, i + j) for j in range(rest[0] if several else 1))
                         if stage == logarithm:
                             made.add((stage, i, rest[0]))
                         moved = True
@@ -494,22 +443,18 @@ def tile_kplanesgaussiananchordecoder_w4_kernel(
         spread_points(0)
         spread_points(1)
         vector, scalar, pool, tensor = [], [], [], []
-
         feat_left = list(range(len(feat_order)))
         squares_left = list(range(8 * len(steps)))
+        summed, waiting = [], []
 
         def more_feat(count):
             vector.extend((feat, feat_left.pop(0)) for i in range(min(count, len(feat_left))))
-
-        def closes(r):
-            return r >= 0 and jobs[2 * r][1] == PLANES - 1
 
         def paced_squares(k):
             need = 0
             for s in range(len(steps)):
                 left = sum(steps[q // 8][1] for q in squares_left if q // 8 <= s)
                 need = max(need, left / max(first_job[s] - 1 - MARGIN - k, 1))
-            need += EXTRA.get(k, 0)
             while squares_left and need > 0:
                 need -= steps[squares_left[0] // 8][1]
                 scalar.append((square, squares_left.pop(0)))
@@ -517,26 +462,22 @@ def tile_kplanesgaussiananchordecoder_w4_kernel(
         def front(k):
             vector.append((minimum, k))
             scalar.append((exponential, k))
-            if k % 2 == 0:
-                scalar.extend((normalise, j) for j in (k - 2, k - 1) if 0 <= j and MODES[j] == "D" and j not in POOL_DIAG)
-            if COPY_LAG <= k and by_words(k - COPY_LAG):
-                scalar.append((group, k - COPY_LAG))
-            scalar.extend((multiply, 2 * r + j) for r in EVAC for j in range(2) if k == 2 * r + EVAC_LAG)
+            if k % 2 == 0 and road(k - 1) == DIAGONAL and not diagonal_on_pool(k - 1):
+                scalar.append((normalise, k - 1))
+            if by_words(k - 4):
+                scalar.append((group, k - 4))
             paced_squares(k)
-            scalar.extend((soft_exp, n) for n in SOFT_AT.get(k, ()))
+            capped = k // 2 - first_bias
+            if k % 2 and 0 <= capped < EXP_TILES:
+                scalar.append((soft_exp, capped))
             if k + 2 < JOBS:
                 tensor.append((distances, k + 2))
 
-        waiting, summed = [], []
+        def gains(r):
+            vector.extend((group, k) for k in (2 * r, 2 * r + 1) if not by_words(k))
 
-        def next_bias():
-            if summed:
-                n = summed.pop(0)
-                if n not in POOL_BIAS:
-                    vector.append((bias, n))
-                if waiting:
-                    summed.append(waiting[0])
-                    tensor.append((linear, waiting.pop(0)))
+        def multiplies(r):
+            return [(multiply, 2 * r + 1), (multiply, 2 * r)]
 
         def close(n, count):
             vector.append((quantise_z, n, count))
@@ -547,86 +488,82 @@ def tile_kplanesgaussiananchordecoder_w4_kernel(
                 else:
                     waiting.append(j)
 
-        def gains(r):
-            vector.extend((group, k) for k in (2 * r, 2 * r + 1) if not by_words(k))
-
-        def weights_to_products(r):
-            vector.append((quantise_weights, 2 * r, 2))
-            tensor.extend([(products, 2 * r), (products, 2 * r + 1)])
+        def next_bias():
+            if summed:
+                vector.append((bias, summed.pop(0)))
+                if waiting:
+                    summed.append(waiting[0])
+                    tensor.append((linear, waiting.pop(0)))
 
         scalar += [(square, squares_left.pop(0)) for i in range(8 + SQUARES_AHEAD)]
         tensor += [(distances, 0), (distances, 1)]
         more_feat(FEAT_AHEAD)
-        def multiplies(r):
-            return [] if r in EVAC else [(multiply, 2 * r + 1), (multiply, 2 * r)]
 
         for r in range(pairs - 1):
-            spent_pair[r] = r - 2
+            at_once = r >= 1 and road(2 * r - 1) == POOL
             front(2 * r)
-            if r >= 1 and r not in RECIP_LATE:
+            if at_once:
                 vector.append((reciprocal, r - 1))
             more_feat(FEAT_A_SLOT)
             if r >= 2:
                 gains(r - 2)
-            if r in RECIP_LATE:
+            if r >= 1 and not at_once:
                 vector.append((reciprocal, r - 1))
-            vector += [(normalise, k) for k in (2 * r - 2, 2 * r - 1) if k >= 0 and MODES[k] == "V"]
-            if BIASES.get(r, 0) >= 1:
-                next_bias()
+            if r == 1:
+                vector += [(normalise, 0), (normalise, 1)]
+            next_bias()
             if r >= 1:
                 tensor += [(turn, k) for k in sorted((2 * r - 2, 2 * r - 1), key=by_words)]
             front(2 * r + 1)
             more_feat(FEAT_A_SLOT)
-            if BIASES.get(r, 0) >= 2:
+            if r == first_bias:
                 next_bias()
             if r >= 3:
                 vector += multiplies(r - 3)
             if r >= 2:
-                weights_to_products(r - 2)
-            if closes(r - 3):
+                vector.append((quantise_weights, 2 * r - 4, 2))
+                tensor += [(products, 2 * r - 4), (products, 2 * r - 3)]
+            if r >= 3 and jobs[2 * r - 6][1] == PLANES - 1:
                 close(jobs[2 * r - 6][2], 2)
 
-        spent_pair[11] = 10
-        front(22)
-        vector.append((reciprocal, 10))
-        gains(9)
-        tensor += [(turn, 21), (turn, 20)]
-        front(23)
-        vector += multiplies(8)
-        vector.append((quantise_weights, 18, 2))
-        close(4, 2)
-        tensor += [(products, 18), (products, 19)]
-        vector.append((reciprocal, 11))
-        gains(10)
-        tensor += [(turn, 22)]
+        p0, p1, p2 = pairs - 3, pairs - 2, pairs - 1
+        front(2 * p2)
+        vector.append((reciprocal, p1))
+        gains(p0)
+        tensor += [(turn, 2 * p1 + 1), (turn, 2 * p1)]
+        front(2 * p2 + 1)
+        vector += multiplies(p0 - 1) + [(quantise_weights, 2 * p0, 2)]
+        close(EARLY_TILES - 2, 2)
+        tensor += [(products, 2 * p0), (products, 2 * p0 + 1), (turn, 2 * p2)]
+        vector.append((reciprocal, p2))
+        gains(p1)
         next_bias()
         next_bias()
-        vector += multiplies(9)[:1]
-        vector.append((quantise_weights, 20, 2))
-        tensor += [(turn, 23), (products, 20), (products, 21)]
-        vector += multiplies(9)[1:]
-        gains(11)
-        vector += [(quantise_weights, 22, 1), (multiply, 20), (quantise_weights, 23, 1), (multiply, 21)]
-        tensor += [(products, 22), (products, 23)]
-        vector += [(finish, n, 0, H) for n in range(BEFORE - 1)] + [(multiply, 22), (multiply, 23)]
-        close(6, 1)
-        close(7, 1)
-        vector += [(finish, BEFORE - 1, 0, H)]
+        vector += [(multiply, 2 * p0 + 1), (quantise_weights, 2 * p1, 2), (multiply, 2 * p0)]
+        tensor += [(turn, 2 * p2 + 1), (products, 2 * p1), (products, 2 * p1 + 1)]
+        gains(p2)
+        for j in range(2):
+            vector += [(quantise_weights, 2 * p2 + j, 1), (multiply, 2 * p1 + j)]
+            tensor.append((products, 2 * p2 + j))
+        vector += [(multiply, 2 * p2), (multiply, 2 * p2 + 1)]
+        close(TILES - 2, 1)
+        close(TILES - 1, 1)
+        vector.append((finish, 0, 0, H))
         next_bias()
         next_bias()
-        parts = [(LATE, 0, H // 2), (LATE, H // 2, H)] + [(n, 0, H) for n in range(LATE + 1, TILES - 1)]
-        parts += [(TILES - 1, 0, H // 2), (TILES - 1, H // 2, H)]
-        vector += [(finish, n, 0, H) for n in range(BEFORE, LATE)] + [(finish, *part) for part in parts]
-        early = [(sigmoid, n, 1) for n in range(SOFT, LATE)] + [(logarithms, 0, SOFT), (logarithms, SOFT, LATE - SOFT)]
-        early.insert(COPY20, (group, 20))
-        copies = [(normalise, k) for k in (22, 23) if MODES[k] == "D"]
-        for place, copy in zip(COPY_AT, copies):
-            early.insert(place, copy)
-        scalar += early + [(sigmoid, n, 1) for n in range(LATE, TILES)] + [(logarithm, *part) for part in parts]
+        halves = [(n, lo, lo + H // 2) for n in range(EARLY_TILES, TILES) for lo in (0, H // 2)]
+        vector += [(finish, n, 0, H) for n in range(1, EARLY_TILES)] + [(finish, *part) for part in halves]
+
+        scalar += [(sigmoid, EXP_TILES), (group, 2 * p1)] + [(sigmoid, n) for n in range(EXP_TILES + 1, EARLY_TILES)]
+        scalar += [(logarithms, 0, EXP_TILES), (logarithms, EXP_TILES, EARLY_TILES - EXP_TILES)]
+        scalar += [(sigmoid, n) for n in range(EARLY_TILES, TILES)] + [(logarithm, *part) for part in halves]
+
         for r in range(pairs):
-            pool += [(pool_gain, k) for k in (2 * r, 2 * r + 1) if by_words(k)]
-            pool += [(normalise, k) for k in (2 * r + 1, 2 * r) if MODES[k] == "D" and k in POOL_DIAG]
-            pool += [(normalise, k) for k in (2 * r, 2 * r + 1) if MODES[k] in "AW"]
-            pool += [(clamp, n) for n in CLAMP_AFTER.get(r, ())]
-        pool += [(pool_bias, n) for n in POOL_BIAS]
+            a, b = 2 * r, 2 * r + 1
+            if by_words(a):
+                pool += [(pool_gain, a)] + ([(normalise, b)] if diagonal_on_pool(b) else []) + [(normalise, a)]
+            if road(a) == POOL:
+                pool += [(normalise, a), (normalise, b)]
+            if 0 <= r + 1 - first_bias < EXP_TILES:
+                pool.append((cap, r + 1 - first_bias))
         issue([vector, scalar, pool, tensor])

@@ -132,8 +132,8 @@ def tile_kplanesgaussiananchordecoder_w4_kernel(
 
             def interleave(h):
                 nc.vector.tensor_copy(
-                    out=side_by_side[:].rearrange("p (t m j) -> p t m j", t=4, j=4)[:, 2 * h : 2 * h + 2],
-                    in_=widened[:].rearrange("p j (m t) -> p t m j", t=4)[:, 2 * h : 2 * h + 2],
+                    out=side_by_side[:].rearrange("p (t m i j) -> p m t i j", t=4, i=2, j=4)[:, 32 * h : 32 * h + 32],
+                    in_=widened[:].rearrange("p j (m i t) -> p m t i j", i=2, t=4)[:, 32 * h : 32 * h + 32],
                 )
 
             def quantise():

@@ -132,8 +132,8 @@ def tile_kplanesgaussiananchordecoder_w4_kernel(
 
             def interleave(h):
                 nc.vector.tensor_copy(
-                    out=side_by_side[:].rearrange("p (t m i j) -> p m t i j", t=4, i=2, j=4)[:, 32 * h : 32 * h + 32],
-                    in_=widened[:].rearrange("p j (m i t) -> p m t i j", i=2, t=4)[:, 32 * h : 32 * h + 32],
+                    out=side_by_side[:].rearrange("p (t m i j) -> p m j i t", t=4, i=2, j=4)[:, 32 * h : 32 * h + 32],
+                    in_=widened[:].rearrange("p j (m i t) -> p m j i t", i=2, t=4)[:, 32 * h : 32 * h + 32],
                 )
 
             def quantise():

@@ -27,8 +27,9 @@ LOWEST = -3.0e38
 
 CHUNKS = ((0, 4), (4, 2), (6, 2))
 MATMUL_BLOCKS = (0, 3)
-FEAT_AHEAD = 14
+FEAT_AHEAD = 13
 FEAT_A_SLOT = 2
+SCALAR_ROW = (0, 1)
 SQUARES_AHEAD = 3
 MARGIN = 1
 EXP_TILES = 3
@@ -122,6 +123,10 @@ def tile_kplanesgaussiananchordecoder_w4_kernel(
             side_by_side = work.tile([128, 4 * C], BF16, name="side_by_side", align_bytes=64)
 
             def widen(j):
+                if (pl, j) == SCALAR_ROW:
+                    codes = bytes_sb[pl][:, j, :].bitcast(FP8)
+                    nc.scalar.activation(out=widened[:, j, :], in_=codes, func=ACT.Copy, scale=scale_sb[:, j : j + 1])
+                    return
                 nc.vector.tensor_scalar(
                     out=widened[:, j, :],
                     in0=bytes_sb[pl][:, j, :].bitcast(FP8),
@@ -381,6 +386,8 @@ def tile_kplanesgaussiananchordecoder_w4_kernel(
         made = set()
 
         def needs(stage, i, *rest):
+            if stage == feat:
+                return [(feat, SCALAR_ROW[1])] if feat_order[i] in inter0 else []
             if stage == square:
                 same = [s for s in range(i // 8) if steps[s][1] == steps[i // 8][1]]
                 return [(distances, first_job[same[-3]] + steps[same[-3]][1] - 1)] if len(same) >= 3 else []
@@ -443,7 +450,7 @@ def tile_kplanesgaussiananchordecoder_w4_kernel(
         spread_points(0)
         spread_points(1)
         vector, scalar, pool, tensor = [], [], [], []
-        feat_left = list(range(len(feat_order)))
+        feat_left = [i for i in range(len(feat_order)) if i != SCALAR_ROW[1]]
         squares_left = list(range(8 * len(steps)))
         summed, waiting = [], []
 
@@ -495,7 +502,7 @@ def tile_kplanesgaussiananchordecoder_w4_kernel(
                     summed.append(waiting[0])
                     tensor.append((linear, waiting.pop(0)))
 
-        scalar += [(square, squares_left.pop(0)) for i in range(8 + SQUARES_AHEAD)]
+        scalar += [(feat, SCALAR_ROW[1])] + [(square, squares_left.pop(0)) for i in range(8 + SQUARES_AHEAD)]
         tensor += [(distances, 0), (distances, 1)]
         more_feat(FEAT_AHEAD)
 

@@ -25,16 +25,29 @@ TINY = 2.0**-60
 CAP = 40.0
 LOWEST = -3.0e38
 
-CHUNKS = ((0, 4), (4, 2), (6, 2))
-MATMUL_BLOCKS = (0, 3)
+HALF = TILES // 2
 FEAT_AHEAD = 13
-FEAT_A_SLOT = 2
+FEAT_SLOTS = (2, 2, 1, 2)
 SCALAR_ROW = (0, 1)
 SQUARES_AHEAD = 3
-MARGIN = 1
-EXP_TILES = 3
-EARLY_TILES = TILES - 2
 EXPO_BUFFERS = 10
+POOL_DIAG = (1, 11)
+SCALAR_GAIN = {12: 18, 13: 18, 14: 20, 15: 20}
+HEAD = ("vector", "diagonal", "pool")
+LAST = ("words", "diagonal")
+VECTOR_DIAG = (1,)
+BIAS_AT = (17, 18, 19, 20)
+CAP_VECTOR = (9, 10)
+EVAC_AT = {}
+PACES = (1, 4, 0, 4)
+RECIP0 = 0
+COPY_VECTOR = ()
+POOL_FEAT = False
+TURN_FIRST = True
+WIDE = (6, 7)
+CLOCK = ((3, 0), (3, 1), (3, 2))
+CAP_AT = ()
+SOFT_AT = (21, 24)
 VECTOR, POOL, WORDS, DIAGONAL = "vector", "pool", "words", "diagonal"
 
 
@@ -51,7 +64,7 @@ def tile_kplanesgaussiananchordecoder_w4_kernel(
         ps_o = ctx.enter_context(tc.psum_pool(name="ps_o", bufs=2))
         ctx.enter_context(tc.manual_schedule())
 
-        head_tiles = CHUNKS[0][1]
+        head_tiles = HALF
         head_points = keep.tile([128, head_tiles, 4], BF16, name="head_points")
         nc.scalar.dma_start(
             out=head_points[:, :, 0:3], in_=pts[0 : 128 * head_tiles, :].rearrange("(j p) x -> p j x", p=128)
@@ -89,6 +102,7 @@ def tile_kplanesgaussiananchordecoder_w4_kernel(
         load_points(1)
         channel_gain = keep.tile([128, 4], BF16, name="channel_gain")
         nc.sync.dma_start(out=channel_gain[:], in_=gc.rearrange("(p t) -> p t", t=4))
+        channel_gain32 = keep.tile([128, 4], F32, name="channel_gain32")
         w_words = keep.tile([128, 2 * H], U8, name="w_words", align_bytes=64)
         nc.sync.dma_start(out=w_words[:], in_=w1_words[0])
         w_scales = keep.tile([128, H], U8, name="w_scales", align_bytes=64)
@@ -104,7 +118,7 @@ def tile_kplanesgaussiananchordecoder_w4_kernel(
         ident = keep.tile([128, 128], F32, name="ident")
         nc.scalar.activation(out=ident[:], in_=ident_bf[:], func=ACT.Copy)
 
-        steps = [(first, count, pl) for first, count in CHUNKS for pl in range(PLANES)]
+        steps = [(first, HALF, pl) for first in (0, HALF) for pl in range(PLANES)]
         jobs = [(s, pl, first + i) for s, (first, count, pl) in enumerate(steps) for i in range(count)]
 
         head_coords = []
@@ -136,6 +150,14 @@ def tile_kplanesgaussiananchordecoder_w4_kernel(
                 )
 
             def interleave(h):
+                if POOL_FEAT and pl == 2:
+                    if h == 0:
+                        nc.gpsimd.tensor_scalar(
+                            out=side_by_side[:].rearrange("p (t m j) -> p t m j", t=4, j=4),
+                            in0=widened[:].rearrange("p j (m t) -> p t m j", t=4),
+                            scalar1=1.0, scalar2=1.0, op0=ALU.mult, op1=ALU.mult,
+                        )
+                    return
                 nc.vector.tensor_copy(
                     out=side_by_side[:].rearrange("p (t m i j) -> p m j i t", t=4, i=2, j=4)[:, 32 * h : 32 * h + 32],
                     in_=widened[:].rearrange("p j (m i t) -> p m j i t", i=2, t=4)[:, 32 * h : 32 * h + 32],
@@ -152,28 +174,24 @@ def tile_kplanesgaussiananchordecoder_w4_kernel(
         first_job = [[s for s, pl, n in jobs].index(s) for s in range(len(steps))]
         pairs = JOBS // 2
         last = JOBS - 1
-        diagonal = {}
-        first_bias = [jobs[2 * r][1] for r in range(pairs)].index(PLANES - 1) + 4
+        diagonal, pair_codes, whole, pair_blocks = {}, {}, [], {}
 
         def road(k):
-            if k < 2:
-                return VECTOR
-            if k // 2 in (1, pairs - 1):
-                return POOL
+            if k < 3:
+                return HEAD[k]
+            if k >= last - 1:
+                return LAST[k - last + 1]
             return DIAGONAL if k % 2 else WORDS
 
         def by_words(k):
             return road(k) == WORDS
 
         def diagonal_on_pool(k):
-            return road(k) == DIAGONAL and k // 2 < first_bias - 1
-
-        def keeps_clock(k):
-            return 2 <= k < 2 * CHUNKS[0][1] or k == last - 2
+            return road(k) == DIAGONAL and POOL_DIAG[0] <= k // 2 < POOL_DIAG[1]
 
         def square(q):
             step, within = divmod(q, 8)
-            axis, t = divmod(within, 4)
+            t, axis = divmod(within, 2)
             first, count, pl = steps[step]
             if within == 0:
                 squared[step] = work.tile([128, 2, 4, count * 128], F32, name="squared", tag="squared%d" % count, bufs=3)
@@ -202,7 +220,7 @@ def tile_kplanesgaussiananchordecoder_w4_kernel(
                         rhs=ident[:],
                         start=(axis == 0),
                         stop=(axis == 1),
-                        is_transpose=not (axis == 0 and t in MATMUL_BLOCKS and keeps_clock(k)),
+                        is_transpose=not (axis == 0 and (k, t) in CLOCK),
                     )
 
         def minimum(k):
@@ -236,7 +254,10 @@ def tile_kplanesgaussiananchordecoder_w4_kernel(
             nc.vector.reciprocal(out=recips[r][:], in_=sums[r][:])
 
         def pool_gain(k):
-            gained[k] = grouped[k // 2 - 2][:].rearrange("p j n t -> p (j n t)").bitcast(F32)
+            if 4 <= k < last:
+                gained[k] = grouped[k // 2 - 2][:].rearrange("p j n t -> p (j n t)").bitcast(F32)
+            else:
+                gained[k] = expo[k][:]
             nc.gpsimd.tensor_tensor(out=gained[k], in0=expo[k][:], in1=gain_all[:, jobs[k][1], :], op=ALU.mult)
 
         def normalise(k):
@@ -249,7 +270,7 @@ def tile_kplanesgaussiananchordecoder_w4_kernel(
             if road(k) == DIAGONAL:
                 diagonal[k] = work.tile([128, 128], F32, name="diagonal")
                 source, target = ident[:], diagonal[k][:]
-            if road(k) == VECTOR:
+            if road(k) == VECTOR or k in VECTOR_DIAG:
                 nc.vector.tensor_scalar(out=target, in0=source, scalar1=factor, scalar2=None, op0=ALU.mult)
             elif road(k) == DIAGONAL and not diagonal_on_pool(k):
                 nc.scalar.activation(out=target, in_=source, func=ACT.Copy, scale=factor)
@@ -272,7 +293,8 @@ def tile_kplanesgaussiananchordecoder_w4_kernel(
                 grouped[k // 2] = work.tile([128, 2, 128, 4], BF16, name="grouped", align_bytes=64, bufs=7)
             target = grouped[k // 2][:, k % 2]
             if by_words(k):
-                nc.scalar.copy(out=target.bitcast(F32), in_=turned[k][:].rearrange("p u n -> p n u"))
+                copy = nc.vector.tensor_copy if k in COPY_VECTOR else nc.scalar.copy
+                copy(out=target.bitcast(F32), in_=turned[k][:].rearrange("p u n -> p n u"))
             else:
                 nc.vector.tensor_tensor(
                     out=target,
@@ -286,16 +308,32 @@ def tile_kplanesgaussiananchordecoder_w4_kernel(
             scales = work.tile([128, 128 * count], U8, name=name + "_scales", tag=name + "_scales", align_bytes=64, bufs=3)
             flat = source.rearrange("p j n t -> p (j n t)")
             nc.vector.quantize_mx(out=words[:].bitcast(FP8X4), scales=scales[:], in_=flat)
+            whole.append((words[:].bitcast(FP8X4), scales[:]))
             columns = [slice(128 * j, 128 * j + 128) for j in range(count)]
             return [(words[:, part].bitcast(FP8X4), scales[:, part]) for part in columns]
 
         def quantise_weights(k, count):
             for j, operand in enumerate(quantise(grouped[k // 2][:, k % 2 : k % 2 + count], count, "a")):
                 codes[k + j] = operand
+            pair_codes[k // 2] = whole[-1]
 
         def products(k):
             pl = jobs[k][1]
-            banks, tag = (ps_d2, "d2") if k // 2 == pairs - 2 else (ps_f, "f")
+            banks, tag = (ps_d2, "d2") if k // 2 in (pairs - 3, pairs - 1) else (ps_f, "f")
+            if k // 2 in WIDE:
+                feature[k] = banks.tile([128, 2, 256], F32, name="feature", tag=tag)
+                for i in range(2):
+                    t = 2 * (k % 2) + i
+                    nc.tensor.matmul_mx(
+                        out=feature[k][:, i, :],
+                        lhsT=feat_words[pl][:, 128 * t : 128 * t + 128].bitcast(FP8X4),
+                        lhsT_scale=feat_scales[pl][:, 128 * t : 128 * t + 128],
+                        rhs=pair_codes[k // 2][0],
+                        rhs_scale=pair_codes[k // 2][1],
+                        start=True,
+                        stop=True,
+                    )
+                return
             feature[k] = banks.tile([128, 4, 128], F32, name="feature", tag=tag)
             for t in range(4):
                 nc.tensor.matmul_mx(
@@ -310,10 +348,33 @@ def tile_kplanesgaussiananchordecoder_w4_kernel(
 
         def multiply(k):
             step, pl, n = jobs[k]
-            other = channel_gain[:].unsqueeze(1).to_broadcast([128, 128, 4]) if pl == 0 else partial[n][:]
+            other = channel_gain[:].unsqueeze(1).to_broadcast([128, 128, 4]) if pl == 0 else partial[n]
+            if k // 2 in WIDE:
+                if k // 2 not in pair_blocks:
+                    pair_blocks[k // 2] = keep.tile([128, 4, 256], F32, name="blocks%d" % (k // 2))
+                    for j in range(2):
+                        part = pair_blocks[k // 2][:, :, 128 * j : 128 * j + 128]
+                        partial[n - k % 2 + j] = part.rearrange("p t n -> p n t")
+                for i in range(2):
+                    t = 2 * (k % 2) + i
+                    nc.scalar.activation(
+                        out=pair_blocks[k // 2][:, t, :],
+                        in_=feature[k][:, i, :],
+                        func=ACT.Copy,
+                        scale=channel_gain32[:, t : t + 1],
+                    )
+                return
+            if pl == 0 and k in SCALAR_GAIN:
+                blocks = work.tile([128, 4, 128], F32, name="partial", bufs=7)
+                for t in range(4):
+                    nc.scalar.activation(
+                        out=blocks[:, t, :], in_=feature[k][:, t, :], func=ACT.Copy, scale=channel_gain32[:, t : t + 1]
+                    )
+                partial[n] = blocks[:].rearrange("p t n -> p n t")
+                return
             if pl < PLANES - 1:
-                partial[n] = work.tile([128, 128, 4], F32, name="partial", bufs=7)
-                result = partial[n][:]
+                result = work.tile([128, 128, 4], F32, name="partial", bufs=7)[:]
+                partial[n] = result
             else:
                 if n // 2 not in z_pair:
                     z_pair[n // 2] = work.tile([128, 2, 128, 4], BF16, name="z_pair", align_bytes=64)
@@ -325,7 +386,8 @@ def tile_kplanesgaussiananchordecoder_w4_kernel(
                 z_codes[n + j] = operand
 
         def linear(n):
-            linear_out[n] = ps_o.tile([128, H], F32, name="linear_out", tag="o")
+            banks, tag = (ps_o, "o") if n < TILES - 2 else (ps_f, "f")
+            linear_out[n] = banks.tile([128, H], F32, name="linear_out", tag=tag)
             nc.tensor.matmul_mx(
                 out=linear_out[n][:],
                 lhsT=z_codes[n][0],
@@ -344,12 +406,12 @@ def tile_kplanesgaussiananchordecoder_w4_kernel(
             nc.vector.tensor_tensor(out=sums_b[:, n, :], in0=linear_out[n][:], in1=bias_row[:], op=ALU.add)
 
         def cap(n):
-            nc.gpsimd.tensor_scalar(
-                out=result_sb[:, n, :], in0=sums_b[:, n, :], scalar1=CAP, scalar2=LOWEST, op0=ALU.min, op1=ALU.max
+            (nc.gpsimd if n // 2 < len(CAP_AT) else nc.vector).tensor_scalar(
+                out=result_sb[:, n : n + 2, :], in0=sums_b[:, n : n + 2, :], scalar1=CAP, scalar2=LOWEST, op0=ALU.min, op1=ALU.max
             )
 
         def soft_exp(n):
-            nc.scalar.activation(out=result_sb[:, n, :], in_=result_sb[:, n, :], func=ACT.Exp)
+            nc.scalar.activation(out=result_sb[:, n : n + 2, :], in_=result_sb[:, n : n + 2, :], func=ACT.Exp)
 
         def sigmoid(n):
             part = slice(n, n + 1)
@@ -357,7 +419,7 @@ def tile_kplanesgaussiananchordecoder_w4_kernel(
 
         def logarithms(n, count):
             part = result_sb[:, n : n + count, :]
-            nc.scalar.activation(out=part, in_=part, func=ACT.Ln, bias=1.0 if n < EXP_TILES else TINY)
+            nc.scalar.activation(out=part, in_=part, func=ACT.Ln, bias=1.0 if n < HALF else TINY)
 
         def logarithm(n, lo, hi):
             part = result_sb[:, n, lo:hi]
@@ -365,7 +427,7 @@ def tile_kplanesgaussiananchordecoder_w4_kernel(
 
         def finish(n, lo, hi):
             part = result_sb[:, n, lo:hi]
-            if n < EXP_TILES:
+            if n < HALF:
                 nc.vector.tensor_tensor(out=part, in0=part, in1=sums_b[:, n, lo:hi], op=ALU.max)
             else:
                 nc.vector.scalar_tensor_tensor(
@@ -375,6 +437,8 @@ def tile_kplanesgaussiananchordecoder_w4_kernel(
 
         (widen0, inter0, quant0), (widen1, inter1, quant1), (widen2, inter2, quant2) = map(feat_parts, range(PLANES))
         feat_order = widen0 + widen1 + inter0 + inter1[:1] + quant0 + inter1[1:] + widen2 + quant1 + inter2 + quant2
+        if POOL_FEAT:
+            feat_order = widen0 + widen1 + inter0 + widen2 + inter1[:1] + quant0 + inter1[1:] + quant1 + quant2 + inter2[:1]
         feat_ready = [feat_order.index(part[0]) for part in (quant0, quant1, quant2)]
 
         def feat(i):
@@ -387,6 +451,10 @@ def tile_kplanesgaussiananchordecoder_w4_kernel(
 
         def needs(stage, i, *rest):
             if stage == feat:
+                if POOL_FEAT and feat_order[i] in quant2:
+                    return [(feat, len(feat_order) - 1)]
+                if POOL_FEAT and feat_order[i] in inter2:
+                    return [(feat, feat_ready[0])]
                 return [(feat, SCALAR_ROW[1])] if feat_order[i] in inter0 else []
             if stage == square:
                 same = [s for s in range(i // 8) if steps[s][1] == steps[i // 8][1]]
@@ -410,27 +478,29 @@ def tile_kplanesgaussiananchordecoder_w4_kernel(
             if stage == quantise_weights:
                 return [(group, i + j) for j in range(rest[0])]
             if stage == products:
-                before = i // 2 - (2 if i // 2 == pairs - 1 else 1)
-                bank = (minimum, last) if i // 2 == pairs - 2 else (multiply, 2 * before + 1 - i % 2)
+                before = i // 2 - (2 if i // 2 >= pairs - 2 else 1)
+                bank = (minimum, last) if i // 2 == pairs - 3 else (multiply, 2 * before)
                 return [(quantise_weights, i), bank, (feat, feat_ready[jobs[i][1]])]
             if stage == multiply:
-                return [(products, i)]
+                return [(products, i), (multiply, i - 4), (multiply, i - 4 + 1 - 2 * (i % 2))]
             if stage == quantise_z:
                 return [(multiply, last_job(i + j)) for j in range(rest[0])]
             if stage == linear:
-                return [(quantise_z, i), (bias, i - 2)]
+                return [(quantise_z, i), (bias, i - 2 if i < TILES - 2 else -1), (multiply, last - 2 if i >= TILES - 2 else -1)]
             if stage == bias:
                 return [(linear, i)]
-            if stage in (cap, sigmoid):
+            if stage == cap:
+                return [(bias, i), (bias, i + 1)]
+            if stage == sigmoid:
                 return [(bias, i)]
             if stage == soft_exp:
                 return [(cap, i)]
             if stage == logarithms:
-                return [(soft_exp if i < EXP_TILES else sigmoid, i + j) for j in range(rest[0])]
+                return [(soft_exp, 0), (soft_exp, 2)]
             if stage == logarithm:
-                return [(sigmoid, i)]
+                return [(sigmoid, TILES - 2)]
             if stage == finish:
-                return [(logarithms, i) if i < EARLY_TILES else (logarithm, i, rest[0])]
+                return [(logarithms, i) if i < HALF else (logarithm, i, rest[0])]
             return []
 
         def issue(orders):
@@ -447,130 +517,127 @@ def tile_kplanesgaussiananchordecoder_w4_kernel(
                         moved = True
                 assert moved
 
+        def widen_gain(i):
+            nc.vector.tensor_copy(out=channel_gain32[:], in_=channel_gain[:])
+
         spread_points(0)
         spread_points(1)
         vector, scalar, pool, tensor = [], [], [], []
         feat_left = [i for i in range(len(feat_order)) if i != SCALAR_ROW[1]]
+        if POOL_FEAT:
+            pool.append((feat, feat_left.pop()))
         squares_left = list(range(8 * len(steps)))
-        summed, waiting = [], []
 
         def more_feat(count):
             vector.extend((feat, feat_left.pop(0)) for i in range(min(count, len(feat_left))))
 
-        def paced_squares(k):
-            need = 0
-            for s in range(len(steps)):
-                left = sum(steps[q // 8][1] for q in squares_left if q // 8 <= s)
-                need = max(need, left / max(first_job[s] - 1 - MARGIN - k, 1))
-            while squares_left and need > 0:
-                need -= steps[squares_left[0] // 8][1]
-                scalar.append((square, squares_left.pop(0)))
+        def more_squares(count):
+            scalar.extend((square, squares_left.pop(0)) for i in range(min(count, len(squares_left))))
 
         def front(k):
             vector.append((minimum, k))
             scalar.append((exponential, k))
-            if k % 2 == 0 and road(k - 1) == DIAGONAL and not diagonal_on_pool(k - 1):
-                scalar.append((normalise, k - 1))
-            if by_words(k - 4):
+            if k % 2 == 0 and k:
+                scalar.extend((normalise, j) for j in (k - 2, k - 1) if road(j) == DIAGONAL and not diagonal_on_pool(j) and j not in VECTOR_DIAG)
+            if k >= 4 and by_words(k - 4) and k - 4 not in COPY_VECTOR:
                 scalar.append((group, k - 4))
-            paced_squares(k)
-            capped = k // 2 - first_bias
-            if k % 2 and 0 <= capped < EXP_TILES:
-                scalar.append((soft_exp, capped))
+            scalar.extend((multiply, j) for j in sorted(SCALAR_GAIN, reverse=True) if SCALAR_GAIN[j] == k)
+            more_squares(PACES[k] if k < len(PACES) else 2)
+            if k in SOFT_AT:
+                scalar.append((soft_exp, 2 * SOFT_AT.index(k)))
             if k + 2 < JOBS:
                 tensor.append((distances, k + 2))
 
         def gains(r):
-            vector.extend((group, k) for k in (2 * r, 2 * r + 1) if not by_words(k))
+            vector.extend((group, k) for k in (2 * r + 1, 2 * r) if not by_words(k))
 
         def multiplies(r):
-            return [(multiply, 2 * r + 1), (multiply, 2 * r)]
+            return [(multiply, k) for k in (2 * r + 1, 2 * r) if k not in SCALAR_GAIN]
 
         def close(n, count):
             vector.append((quantise_z, n, count))
-            for j in range(n, n + count):
-                if len(summed) < 2:
-                    summed.append(j)
-                    tensor.append((linear, j))
-                else:
-                    waiting.append(j)
 
-        def next_bias():
-            if summed:
-                vector.append((bias, summed.pop(0)))
-                if waiting:
-                    summed.append(waiting[0])
-                    tensor.append((linear, waiting.pop(0)))
+        def biases(k):
+            if k in BIAS_AT:
+                n = BIAS_AT.index(k)
+                vector.append((bias, n))
+                if n == 1:
+                    tensor.append((linear, 3))
 
-        scalar += [(feat, SCALAR_ROW[1])] + [(square, squares_left.pop(0)) for i in range(8 + SQUARES_AHEAD)]
+        scalar.append((feat, SCALAR_ROW[1]))
+        more_squares(8 + SQUARES_AHEAD)
         tensor += [(distances, 0), (distances, 1)]
         more_feat(FEAT_AHEAD)
 
         for r in range(pairs - 1):
-            at_once = r >= 1 and road(2 * r - 1) == POOL
+            at_once = 1 <= r <= 2
+            if r == 1 and RECIP0:
+                more_feat(RECIP0)
+                vector.append((reciprocal, 0))
             front(2 * r)
-            if at_once:
+            if at_once and not (r == 1 and RECIP0):
                 vector.append((reciprocal, r - 1))
-            more_feat(FEAT_A_SLOT)
+            more_feat(FEAT_SLOTS[2 * r] if 2 * r < len(FEAT_SLOTS) else 0)
+            if r == 1:
+                vector += [(normalise, k) for k in (1, 0) if road(k) == VECTOR or k in VECTOR_DIAG]
             if r >= 2:
                 gains(r - 2)
             if r >= 1 and not at_once:
                 vector.append((reciprocal, r - 1))
-            if r == 1:
-                vector += [(normalise, 0), (normalise, 1)]
-            next_bias()
+            biases(2 * r)
             if r >= 1:
-                tensor += [(turn, k) for k in sorted((2 * r - 2, 2 * r - 1), key=by_words)]
+                later = [tensor.pop()] if r == 1 and TURN_FIRST else []
+                tensor += [(turn, k) for k in sorted((2 * r - 1, 2 * r - 2), key=by_words)] + later
             front(2 * r + 1)
-            more_feat(FEAT_A_SLOT)
-            if r == first_bias:
-                next_bias()
+            more_feat(FEAT_SLOTS[2 * r + 1] if 2 * r < len(FEAT_SLOTS) else 0)
+            biases(2 * r + 1)
             if r >= 3:
-                vector += multiplies(r - 3)
+                vector += multiplies(r - 3)[:1]
+            if 2 * r - 4 in COPY_VECTOR:
+                vector.append((group, 2 * r - 4))
+            if r >= 3:
+                vector += multiplies(r - 3)[1:]
             if r >= 2:
                 vector.append((quantise_weights, 2 * r - 4, 2))
                 tensor += [(products, 2 * r - 4), (products, 2 * r - 3)]
+            if r == 4 and SCALAR_GAIN:
+                vector.append((widen_gain, 0))
             if r >= 3 and jobs[2 * r - 6][1] == PLANES - 1:
-                close(jobs[2 * r - 6][2], 2)
+                n = jobs[2 * r - 6][2]
+                close(n, 2)
+                tensor += [(linear, n)] + ([(linear, 1)] if n == 0 else [])
+            if r in CAP_VECTOR:
+                vector.append((cap, 2 * (len(CAP_AT) + CAP_VECTOR.index(r))))
 
-        p0, p1, p2 = pairs - 3, pairs - 2, pairs - 1
-        front(2 * p2)
+        p1, p2 = pairs - 2, pairs - 1
+        a, b = 2 * p2, 2 * p2 + 1
+        p0 = p1 - 1
+        front(a)
         vector.append((reciprocal, p1))
         gains(p0)
         tensor += [(turn, 2 * p1 + 1), (turn, 2 * p1)]
-        front(2 * p2 + 1)
-        vector += multiplies(p0 - 1) + [(quantise_weights, 2 * p0, 2)]
-        close(EARLY_TILES - 2, 2)
-        tensor += [(products, 2 * p0), (products, 2 * p0 + 1), (turn, 2 * p2)]
-        vector.append((reciprocal, p2))
+        front(b)
+        vector += [(multiply, 2 * p0 - 1), (quantise_weights, 2 * p0, 2), (reciprocal, p2), (multiply, 2 * p0 - 2)]
+        tensor += [(products, 2 * p0), (products, 2 * p0 + 1), (turn, b)]
         gains(p1)
-        next_bias()
-        next_bias()
-        vector += [(multiply, 2 * p0 + 1), (quantise_weights, 2 * p1, 2), (multiply, 2 * p0)]
-        tensor += [(turn, 2 * p2 + 1), (products, 2 * p1), (products, 2 * p1 + 1)]
-        gains(p2)
-        for j in range(2):
-            vector += [(quantise_weights, 2 * p2 + j, 1), (multiply, 2 * p1 + j)]
-            tensor.append((products, 2 * p2 + j))
-        vector += [(multiply, 2 * p2), (multiply, 2 * p2 + 1)]
-        close(TILES - 2, 1)
-        close(TILES - 1, 1)
-        vector.append((finish, 0, 0, H))
-        next_bias()
-        next_bias()
-        halves = [(n, lo, lo + H // 2) for n in range(EARLY_TILES, TILES) for lo in (0, H // 2)]
-        vector += [(finish, n, 0, H) for n in range(1, EARLY_TILES)] + [(finish, *part) for part in halves]
+        vector += [(multiply, 2 * p0 + 1), (multiply, 2 * p0), (quantise_weights, 2 * p1, 2)]
+        tensor += [(turn, a), (products, 2 * p1), (products, 2 * p1 + 1)]
+        vector += [(group, b), (multiply, 2 * p1), (quantise_weights, b, 1), (multiply, 2 * p1 + 1), (quantise_weights, a, 1)]
+        tensor += [(products, b), (products, a), (linear, HALF), (linear, HALF + 1), (linear, HALF + 3), (linear, HALF + 2)]
+        vector += [(quantise_z, HALF, 2), (multiply, b), (multiply, a), (quantise_z, HALF + 3, 1), (bias, HALF)]
+        vector += [(quantise_z, HALF + 2, 1), (bias, HALF + 1), (bias, HALF + 3), (bias, HALF + 2), (finish, 0, 0, H), (finish, 1, 0, H)]
+        parts = [(n, 0, H) for n in range(HALF, TILES - 1)] + [(TILES - 1, lo, lo + H // 2) for lo in (0, H // 2)]
+        vector += [(finish, n, 0, H) for n in range(2, HALF)] + [(finish, *part) for part in parts]
 
-        scalar += [(sigmoid, EXP_TILES), (group, 2 * p1)] + [(sigmoid, n) for n in range(EXP_TILES + 1, EARLY_TILES)]
-        scalar += [(logarithms, 0, EXP_TILES), (logarithms, EXP_TILES, EARLY_TILES - EXP_TILES)]
-        scalar += [(sigmoid, n) for n in range(EARLY_TILES, TILES)] + [(logarithm, *part) for part in halves]
+        scalar += [(soft_exp, 2)] * (24 in SOFT_AT) + [(normalise, k) for k in (b, a) if road(k) == DIAGONAL]
+        scalar += [(group, 2 * p1)] + [(logarithms, 0, 1)] + [(group, k) for k in (a, b) if by_words(k)] + [(logarithms, 1, 3)]
+        scalar += [(sigmoid, n) for n in (4, 5, 7, 6)] + [(logarithm, *part) for part in parts]
 
         for r in range(pairs):
-            a, b = 2 * r, 2 * r + 1
-            if by_words(a):
-                pool += [(pool_gain, a)] + ([(normalise, b)] if diagonal_on_pool(b) else []) + [(normalise, a)]
-            if road(a) == POOL:
-                pool += [(normalise, a), (normalise, b)]
-            if 0 <= r + 1 - first_bias < EXP_TILES:
-                pool.append((cap, r + 1 - first_bias))
+            both = (2 * r, 2 * r + 1)
+            pool += [(pool_gain, k) for k in both if by_words(k)]
+            pool += [(normalise, k) for k in both if diagonal_on_pool(k)]
+            pool += [(normalise, k) for k in both if road(k) in (WORDS, POOL)]
+            if r in CAP_AT:
+                pool.append((cap, 2 * CAP_AT.index(r)))
         issue([vector, scalar, pool, tensor])

@@ -27,8 +27,8 @@ LOWEST = -3.0e38
 
 HALF = TILES // 2
 FEAT_AHEAD = 13
-FEAT_SLOTS = (2, 2, 1, 2)
-SCALAR_ROW = (0, 1)
+FEAT_SLOTS = (2, 2, 1, 1)
+SCALAR_ROW = 1
 SQUARES_AHEAD = 3
 EXPO_BUFFERS = 10
 POOL_DIAG = (1, 11)
@@ -37,17 +37,32 @@ HEAD = ("vector", "diagonal", "pool")
 LAST = ("words", "diagonal")
 VECTOR_DIAG = (1,)
 BIAS_AT = (17, 18, 19, 20)
-CAP_VECTOR = (9, 10)
 EVAC_AT = {}
 PACES = (1, 4, 0, 4)
 RECIP0 = 0
-COPY_VECTOR = ()
+COPY_VECTOR = (4, 8)
 POOL_FEAT = False
 TURN_FIRST = True
 WIDE = (6, 7)
-CLOCK = ((3, 0), (3, 1), (3, 2))
+DV = "n22 r10 g19 n23 m17 q18.2 r11 m16 g21 m19 q20.2 m18 g23 m20 q23.1 m21 q22.1 z4.2 m23 m22 z7.1 b4 z6.1 b5 b7 b6 f0 f1 f2 f3 f4 f5 f6 f7.0.2 f7.2.4"
+DS = "e22 g18 e23 x0 d23 g20 x2 L0.1 g22 L1.3 s4 s5 s7 s6 k4 k5 k6 k7.0.2 k7.2.4"
+DT = "t21 t20 p18 p19 t23 p20 p21 t22 p23 p22 l4 l5 l7 l6"
+NORM_AFTER = True
+SPARE = (2, 3)
+VALUES = 6
+HV = "W0 W2 W3 W4 I0 W5 W6 W7 U0 I1.0.1 n0 I1.1.2 n1 I2.0.1 n2 I2.1.2 n3 U1.1 r0 U2.1 d1 d0 n4 r1 n5 g1 g0"
+H3 = "q0.2"
+HS = "W1 Q0 Q1 Q2 Q3 Q4 Q5 Q6 Q7 Q8 Q9 Q10 Q11 Q12 Q13 Q14 Q15 e0 e1 e2 e3 Q16 Q17 Q18 Q19 e4 Q20 Q21 e5 Q22 Q23"
+HT = "D0 D1 D2 D3 D4 D5 t1 t0 D6 t3 t2 D7 p0 p1"
+HG = "w0 d3 d2"
+PARTS = ((4, 0, 128), (4, 128, 512), (5, 0, 512), (6, 0, 512), (7, 0, 256), (7, 256, 512))
+ABS = {0: 21}
+CAP_VECTOR = {10: 2}
+HEAD2 = 0
+TURN2 = False
+CLOCK = ((5, 0), (5, 1), (5, 2))
 CAP_AT = ()
-SOFT_AT = (21, 24)
+SOFT_AT = ()
 VECTOR, POOL, WORDS, DIAGONAL = "vector", "pool", "words", "diagonal"
 
 
@@ -71,11 +86,13 @@ def tile_kplanesgaussiananchordecoder_w4_kernel(
         )
         scale_sb = keep.tile([128, 4], F32, name="scale_sb")
         nc.sync.dma_start(out=scale_sb[:], in_=feat_scale.rearrange("o (p t) x -> p (o t x)", t=4))
-        bytes_sb = [keep.tile([128, 4, C], U8, name="bytes_sb%d" % pl) for pl in range(PLANES)]
+        first_bytes = keep.tile([128, 4, C], U8, name="first_bytes")
+        later_bytes = keep.tile([128, 4, 2, C], U8, name="later_bytes")
 
         def load_feat(pl, lo, hi):
             rows = feat_bytes[pl].rearrange("(p t) c -> p t c", t=4)
-            nc.sync.dma_start(out=bytes_sb[pl][:, lo:hi, :], in_=rows[:, lo:hi, :])
+            target = first_bytes[:, lo:hi, :] if pl == 0 else later_bytes[:, lo:hi, pl - 1, :]
+            nc.sync.dma_start(out=target, in_=rows[:, lo:hi, :])
 
         centres = keep.tile([128, PLANES, 8], BF16, name="centres")
         nc.scalar.dma_start(out=centres[:], in_=cen.rearrange("x (p t) axis -> p x (t axis)", t=4))
@@ -84,6 +101,7 @@ def tile_kplanesgaussiananchordecoder_w4_kernel(
         gain_rows = keep.tile([128, PLANES, 4], BF16, name="gain_rows")
         nc.sync.dma_start(out=gain_rows[:], in_=ga.rearrange("x (p t) -> p x t", t=4))
         load_feat(1, 0, 4)
+        load_feat(2, 0, 4)
         half = N // 2
         points = [keep.tile([128, half, 3], BF16, name="points%d" % h) for h in range(2)]
 
@@ -94,7 +112,6 @@ def tile_kplanesgaussiananchordecoder_w4_kernel(
             )
 
         load_points(0)
-        load_feat(2, 0, 4)
         gain_all = keep.tile([128, PLANES, M], BF16, name="gain_all")
         nc.sync.dma_start(
             out=gain_all[:].rearrange("n x m -> n (x m)"), in_=ga.rearrange("x m -> (x m)").partition_broadcast(128)
@@ -129,45 +146,37 @@ def tile_kplanesgaussiananchordecoder_w4_kernel(
                 nc.tensor.transpose(bank[:, j, :], head_points[:, j, x : x + 1].to_broadcast([128, 128]), ident_bf[:])
             head_coords.append(bank[:].rearrange("p j n -> p (j n)"))
 
-        feat_words = [keep.tile([128, C], U32, name="feat_words%d" % pl, align_bytes=64) for pl in range(PLANES)]
-        feat_scales = [keep.tile([128, C], U8, name="feat_scales%d" % pl, align_bytes=64) for pl in range(PLANES)]
+        feat_words = keep.tile([128, PLANES, C], U32, name="feat_words", align_bytes=64)
+        feat_scales = keep.tile([128, PLANES, C], U8, name="feat_scales", align_bytes=64)
 
-        def feat_parts(pl):
-            widened = work.tile([128, 4, C], BF16, name="widened", bufs=PLANES)
-            side_by_side = work.tile([128, 4 * C], BF16, name="side_by_side", align_bytes=64)
+        first_wide = keep.tile([128, 4, C], BF16, name="first_wide")
+        later_wide = keep.tile([128, 4, 2, C], BF16, name="later_wide")
+        side_by_side = keep.tile([128, PLANES, 4 * C], BF16, name="side_by_side", align_bytes=64)
 
-            def widen(j):
-                if (pl, j) == SCALAR_ROW:
-                    codes = bytes_sb[pl][:, j, :].bitcast(FP8)
-                    nc.scalar.activation(out=widened[:, j, :], in_=codes, func=ACT.Copy, scale=scale_sb[:, j : j + 1])
-                    return
-                nc.vector.tensor_scalar(
-                    out=widened[:, j, :],
-                    in0=bytes_sb[pl][:, j, :].bitcast(FP8),
-                    scalar1=scale_sb[:, j : j + 1],
-                    scalar2=None,
-                    op0=ALU.mult,
-                )
+        def widen(j):
+            t = j % 4
+            source = first_bytes[:, t, :] if j < 4 else later_bytes[:, t].rearrange("p x c -> p (x c)")
+            target = first_wide[:, t, :] if j < 4 else later_wide[:, t].rearrange("p x c -> p (x c)")
+            if j == SCALAR_ROW:
+                nc.scalar.activation(out=target, in_=source.bitcast(FP8), func=ACT.Copy, scale=scale_sb[:, t : t + 1])
+                return
+            nc.vector.tensor_scalar(
+                out=target, in0=source.bitcast(FP8), scalar1=scale_sb[:, t : t + 1], scalar2=None, op0=ALU.mult
+            )
 
-            def interleave(h):
-                if POOL_FEAT and pl == 2:
-                    if h == 0:
-                        nc.gpsimd.tensor_scalar(
-                            out=side_by_side[:].rearrange("p (t m j) -> p t m j", t=4, j=4),
-                            in0=widened[:].rearrange("p j (m t) -> p t m j", t=4),
-                            scalar1=1.0, scalar2=1.0, op0=ALU.mult, op1=ALU.mult,
-                        )
-                    return
-                nc.vector.tensor_copy(
-                    out=side_by_side[:].rearrange("p (t m i j) -> p m j i t", t=4, i=2, j=4)[:, 32 * h : 32 * h + 32],
-                    in_=widened[:].rearrange("p j (m i t) -> p m j i t", i=2, t=4)[:, 32 * h : 32 * h + 32],
-                )
+        def interleave(pl, lo=0, hi=2):
+            widened = first_wide[:] if pl == 0 else later_wide[:, :, pl - 1, :]
+            nc.vector.tensor_copy(
+                out=side_by_side[:, pl].rearrange("p (t m i j) -> p m j i t", t=4, i=2, j=4)[:, 32 * lo : 32 * hi],
+                in_=widened.rearrange("p j (m i t) -> p m j i t", i=2, t=4)[:, 32 * lo : 32 * hi],
+            )
 
-            def quantise():
-                codes = feat_words[pl][:].bitcast(FP8X4)
-                nc.vector.quantize_mx(out=codes, scales=feat_scales[pl][:], in_=side_by_side[:])
-
-            return [lambda j=j: widen(j) for j in range(4)], [lambda h=h: interleave(h) for h in range(2)], [quantise]
+        def quantise_feat(pl, count=1):
+            nc.vector.quantize_mx(
+                out=feat_words[:, pl : pl + count].rearrange("p x c -> p (x c)").bitcast(FP8X4),
+                scales=feat_scales[:, pl : pl + count].rearrange("p x c -> p (x c)"),
+                in_=side_by_side[:, pl : pl + count].rearrange("p x c -> p (x c)"),
+            )
 
         squared, distance, scaled, expo, sums, recips, gained, weights = ({} for i in range(8))
         turned, grouped, codes, feature, partial, z_pair, z_codes, linear_out = ({} for i in range(8))
@@ -177,7 +186,7 @@ def tile_kplanesgaussiananchordecoder_w4_kernel(
         diagonal, pair_codes, whole, pair_blocks = {}, {}, [], {}
 
         def road(k):
-            if k < 3:
+            if k < len(HEAD):
                 return HEAD[k]
             if k >= last - 1:
                 return LAST[k - last + 1]
@@ -187,7 +196,7 @@ def tile_kplanesgaussiananchordecoder_w4_kernel(
             return road(k) == WORDS
 
         def diagonal_on_pool(k):
-            return road(k) == DIAGONAL and POOL_DIAG[0] <= k // 2 < POOL_DIAG[1]
+            return road(k) == DIAGONAL and k not in VECTOR_DIAG and POOL_DIAG[0] <= k // 2 < POOL_DIAG[1]
 
         def square(q):
             step, within = divmod(q, 8)
@@ -211,7 +220,8 @@ def tile_kplanesgaussiananchordecoder_w4_kernel(
         def distances(k):
             step, pl, n = jobs[k]
             i = n - steps[step][0]
-            distance[k] = ps_d2.tile([128, 4, 128], F32, name="d2", tag="d2")
+            banks, tag = (ps_f, "f") if k in SPARE else (ps_d2, "d2")
+            distance[k] = banks.tile([128, 4, 128], F32, name="d2", tag=tag)
             for t in range(4):
                 for axis in range(2):
                     nc.tensor.matmul(
@@ -224,8 +234,8 @@ def tile_kplanesgaussiananchordecoder_w4_kernel(
                     )
 
         def minimum(k):
-            values = work.tile([128, M], F32, name="values", bufs=3)
-            least = work.tile([128, 1], F32, name="least", bufs=3)
+            values = work.tile([128, M], F32, name="values", bufs=VALUES)
+            least = work.tile([128, 1], F32, name="least", bufs=VALUES)
             target, source = values[:], distance[k][:].rearrange("n t p -> n (t p)")
             if by_words(k):
                 target = values[:].rearrange("n (p t) -> n p t", t=4)
@@ -264,7 +274,10 @@ def tile_kplanesgaussiananchordecoder_w4_kernel(
             source = target = expo[k][:]
             factor = recips[k // 2][:, k % 2 : k % 2 + 1]
             if road(k) == WORDS:
-                weights[k] = work.tile([128, M], BF16, name="weights", bufs=4)
+                if k == last - 1 and NORM_AFTER:
+                    weights[k] = grouped[k // 2 - 1][:, 0].rearrange("p n t -> p (n t)")
+                else:
+                    weights[k] = work.tile([128, M], BF16, name="weights", bufs=4)
                 source = gained[k].rearrange("n (p u e) -> n u p e", u=2, e=2)
                 target = weights[k][:].rearrange("n (u p e) -> n u p e", u=2, e=2)
             if road(k) == DIAGONAL:
@@ -326,8 +339,8 @@ def tile_kplanesgaussiananchordecoder_w4_kernel(
                     t = 2 * (k % 2) + i
                     nc.tensor.matmul_mx(
                         out=feature[k][:, i, :],
-                        lhsT=feat_words[pl][:, 128 * t : 128 * t + 128].bitcast(FP8X4),
-                        lhsT_scale=feat_scales[pl][:, 128 * t : 128 * t + 128],
+                        lhsT=feat_words[:, pl, 128 * t : 128 * t + 128].bitcast(FP8X4),
+                        lhsT_scale=feat_scales[:, pl, 128 * t : 128 * t + 128],
                         rhs=pair_codes[k // 2][0],
                         rhs_scale=pair_codes[k // 2][1],
                         start=True,
@@ -338,8 +351,8 @@ def tile_kplanesgaussiananchordecoder_w4_kernel(
             for t in range(4):
                 nc.tensor.matmul_mx(
                     out=feature[k][:, t, :],
-                    lhsT=feat_words[pl][:, 128 * t : 128 * t + 128].bitcast(FP8X4),
-                    lhsT_scale=feat_scales[pl][:, 128 * t : 128 * t + 128],
+                    lhsT=feat_words[:, pl, 128 * t : 128 * t + 128].bitcast(FP8X4),
+                    lhsT_scale=feat_scales[:, pl, 128 * t : 128 * t + 128],
                     rhs=codes[k][0],
                     rhs_scale=codes[k][1],
                     start=True,
@@ -402,20 +415,22 @@ def tile_kplanesgaussiananchordecoder_w4_kernel(
         result_sb = keep.tile([128, TILES, H], F32, name="result_sb")
         out_tiles = out.rearrange("(j p) h -> p j h", p=128)
 
-        def bias(n):
-            nc.vector.tensor_tensor(out=sums_b[:, n, :], in0=linear_out[n][:], in1=bias_row[:], op=ALU.add)
+        def bias(n, lo=0, hi=H):
+            nc.vector.tensor_tensor(out=sums_b[:, n, lo:hi], in0=linear_out[n][:, lo:hi], in1=bias_row[:, lo:hi], op=ALU.add)
 
         def cap(n):
+            if n in ABS:
+                nc.scalar.activation(out=result_sb[:, n : n + 2, :], in_=sums_b[:, n : n + 2, :], func=ACT.Abs)
+                return
             (nc.gpsimd if n // 2 < len(CAP_AT) else nc.vector).tensor_scalar(
                 out=result_sb[:, n : n + 2, :], in0=sums_b[:, n : n + 2, :], scalar1=CAP, scalar2=LOWEST, op0=ALU.min, op1=ALU.max
             )
 
         def soft_exp(n):
-            nc.scalar.activation(out=result_sb[:, n : n + 2, :], in_=result_sb[:, n : n + 2, :], func=ACT.Exp)
+            nc.scalar.activation(out=result_sb[:, n : n + 2, :], in_=result_sb[:, n : n + 2, :], func=ACT.Exp, scale=-1.0 if n in ABS else 1.0)
 
-        def sigmoid(n):
-            part = slice(n, n + 1)
-            nc.scalar.activation(out=result_sb[:, part, :], in_=sums_b[:, part, :], func=ACT.Sigmoid, scale=-1.0)
+        def sigmoid(n, lo=0, hi=H):
+            nc.scalar.activation(out=result_sb[:, n, lo:hi], in_=sums_b[:, n, lo:hi], func=ACT.Sigmoid, scale=-1.0)
 
         def logarithms(n, count):
             part = result_sb[:, n : n + count, :]
@@ -427,7 +442,11 @@ def tile_kplanesgaussiananchordecoder_w4_kernel(
 
         def finish(n, lo, hi):
             part = result_sb[:, n, lo:hi]
-            if n < HALF:
+            if n - n % 2 in ABS:
+                nc.vector.scalar_tensor_tensor(
+                    out=part, in0=sums_b[:, n, lo:hi], scalar=0.0, in1=part, op0=ALU.max, op1=ALU.add
+                )
+            elif n < HALF:
                 nc.vector.tensor_tensor(out=part, in0=part, in1=sums_b[:, n, lo:hi], op=ALU.max)
             else:
                 nc.vector.scalar_tensor_tensor(
@@ -435,34 +454,21 @@ def tile_kplanesgaussiananchordecoder_w4_kernel(
                 )
             nc.sync.dma_start(out=out_tiles[:, n, lo:hi], in_=part)
 
-        (widen0, inter0, quant0), (widen1, inter1, quant1), (widen2, inter2, quant2) = map(feat_parts, range(PLANES))
-        feat_order = widen0 + widen1 + inter0 + inter1[:1] + quant0 + inter1[1:] + widen2 + quant1 + inter2 + quant2
-        if POOL_FEAT:
-            feat_order = widen0 + widen1 + inter0 + widen2 + inter1[:1] + quant0 + inter1[1:] + quant1 + quant2 + inter2[:1]
-        feat_ready = [feat_order.index(part[0]) for part in (quant0, quant1, quant2)]
-
-        def feat(i):
-            feat_order[i]()
-
         def last_job(n):
             return [k for k in range(JOBS) if jobs[k][1:] == (PLANES - 1, n)][0]
 
         made = set()
 
         def needs(stage, i, *rest):
-            if stage == feat:
-                if POOL_FEAT and feat_order[i] in quant2:
-                    return [(feat, len(feat_order) - 1)]
-                if POOL_FEAT and feat_order[i] in inter2:
-                    return [(feat, feat_ready[0])]
-                return [(feat, SCALAR_ROW[1])] if feat_order[i] in inter0 else []
+            if stage == interleave:
+                return [(widen, j) for j in (range(4) if i == 0 else range(4, 8))]
             if stage == square:
                 same = [s for s in range(i // 8) if steps[s][1] == steps[i // 8][1]]
                 return [(distances, first_job[same[-3]] + steps[same[-3]][1] - 1)] if len(same) >= 3 else []
             if stage == distances:
-                return [(square, 8 * jobs[i][0] + 7), (minimum, i - 2)]
+                return [(square, 8 * jobs[i][0] + 7), (minimum, i - (4 if SPARE and i < SPARE[-1] + 3 else 2))]
             if stage == minimum:
-                return [(distances, i), (exponential, i - 3)]
+                return [(distances, i), (exponential, i - VALUES)]
             if stage == exponential:
                 return [(minimum, i), (turn, i - EXPO_BUFFERS)]
             if stage == reciprocal:
@@ -470,7 +476,7 @@ def tile_kplanesgaussiananchordecoder_w4_kernel(
             if stage == pool_gain:
                 return [(exponential, i), (quantise_weights, i - 4)]
             if stage == normalise:
-                return [(reciprocal, i // 2)] + ([(pool_gain, i)] if by_words(i) else [])
+                return [(reciprocal, i // 2)] + ([(pool_gain, i)] if by_words(i) else []) + [(quantise_weights, i - 2 if i == last - 1 and NORM_AFTER else -1)]
             if stage == turn:
                 return [(normalise, i), (group, i - 2)]
             if stage == group:
@@ -480,7 +486,7 @@ def tile_kplanesgaussiananchordecoder_w4_kernel(
             if stage == products:
                 before = i // 2 - (2 if i // 2 >= pairs - 2 else 1)
                 bank = (minimum, last) if i // 2 == pairs - 3 else (multiply, 2 * before)
-                return [(quantise_weights, i), bank, (feat, feat_ready[jobs[i][1]])]
+                return [(quantise_weights, i), bank, (quantise_feat, jobs[i][1])]
             if stage == multiply:
                 return [(products, i), (multiply, i - 4), (multiply, i - 4 + 1 - 2 * (i % 2))]
             if stage == quantise_z:
@@ -492,7 +498,7 @@ def tile_kplanesgaussiananchordecoder_w4_kernel(
             if stage == cap:
                 return [(bias, i), (bias, i + 1)]
             if stage == sigmoid:
-                return [(bias, i)]
+                return [(bias, i, *rest[:1])]
             if stage == soft_exp:
                 return [(cap, i)]
             if stage == logarithms:
@@ -510,26 +516,20 @@ def tile_kplanesgaussiananchordecoder_w4_kernel(
                     while order and all(need in made or need[1] < 0 for need in needs(*order[0])):
                         stage, i, *rest = order.pop(0)
                         stage(i, *rest)
-                        several = stage in (quantise_weights, quantise_z, logarithms)
+                        several = stage in (quantise_weights, quantise_z, logarithms) or (stage == quantise_feat and rest)
                         made.update((stage, i + j) for j in range(rest[0] if several else 1))
-                        if stage == logarithm:
+                        if stage in (logarithm, bias, sigmoid) and rest:
                             made.add((stage, i, rest[0]))
                         moved = True
                 assert moved
 
         def widen_gain(i):
-            nc.vector.tensor_copy(out=channel_gain32[:], in_=channel_gain[:])
+            nc.gpsimd.tensor_copy(out=channel_gain32[:], in_=channel_gain[:])
 
         spread_points(0)
         spread_points(1)
         vector, scalar, pool, tensor = [], [], [], []
-        feat_left = [i for i in range(len(feat_order)) if i != SCALAR_ROW[1]]
-        if POOL_FEAT:
-            pool.append((feat, feat_left.pop()))
         squares_left = list(range(8 * len(steps)))
-
-        def more_feat(count):
-            vector.extend((feat, feat_left.pop(0)) for i in range(min(count, len(feat_left))))
 
         def more_squares(count):
             scalar.extend((square, squares_left.pop(0)) for i in range(min(count, len(squares_left))))
@@ -543,6 +543,7 @@ def tile_kplanesgaussiananchordecoder_w4_kernel(
                 scalar.append((group, k - 4))
             scalar.extend((multiply, j) for j in sorted(SCALAR_GAIN, reverse=True) if SCALAR_GAIN[j] == k)
             more_squares(PACES[k] if k < len(PACES) else 2)
+            scalar.extend((cap, n) for n in ABS if ABS[n] == k)
             if k in SOFT_AT:
                 scalar.append((soft_exp, 2 * SOFT_AT.index(k)))
             if k + 2 < JOBS:
@@ -564,32 +565,44 @@ def tile_kplanesgaussiananchordecoder_w4_kernel(
                 if n == 1:
                     tensor.append((linear, 3))
 
-        scalar.append((feat, SCALAR_ROW[1]))
-        more_squares(8 + SQUARES_AHEAD)
-        tensor += [(distances, 0), (distances, 1)]
-        more_feat(FEAT_AHEAD)
+        names = dict(m=multiply, g=group, r=reciprocal, n=minimum, b=bias, e=exponential, d=normalise, s=sigmoid, t=turn, p=products, l=linear, x=soft_exp, c=cap, D=distances, W=widen, Q=square, G=pool_gain, w=widen_gain)
 
-        for r in range(pairs - 1):
-            at_once = 1 <= r <= 2
-            if r == 1 and RECIP0:
-                more_feat(RECIP0)
-                vector.append((reciprocal, 0))
+        def parse(text):
+            out = []
+            for w in text.split():
+                i = [int(v) for v in w[1:].split(".")]
+                if w[0] == "q":
+                    out.append((quantise_weights, i[0], i[1]))
+                elif w[0] in "IU":
+                    out.append(({"I": interleave, "U": quantise_feat}[w[0]], *i))
+                elif w[0] == "z":
+                    out.append((quantise_z, i[0], i[1]))
+                elif w[0] == "L":
+                    out.append((logarithms, i[0], i[1]))
+                elif w[0] in "fk" or len(i) > 1:
+                    lo, hi = (128 * i[1], 128 * i[2]) if len(i) > 1 else (0, H)
+                    out.append(({"f": finish, "k": logarithm, "b": bias, "s": sigmoid}[w[0]], i[0], lo, hi))
+                else:
+                    out.append((names[w[0]], i[0]))
+            return out
+
+        vector += parse(HV)
+        scalar += parse(HS)
+        tensor += parse(HT)
+        pool += parse(HG)
+        squares_left = [q for q in squares_left if (square, q) not in scalar + pool]
+
+        for r in range(3, pairs - 1):
             front(2 * r)
-            if at_once and not (r == 1 and RECIP0):
-                vector.append((reciprocal, r - 1))
-            more_feat(FEAT_SLOTS[2 * r] if 2 * r < len(FEAT_SLOTS) else 0)
-            if r == 1:
-                vector += [(normalise, k) for k in (1, 0) if road(k) == VECTOR or k in VECTOR_DIAG]
-            if r >= 2:
-                gains(r - 2)
-            if r >= 1 and not at_once:
-                vector.append((reciprocal, r - 1))
+            if r == 3:
+                vector += parse(H3)
+            gains(r - 2)
+            vector.append((reciprocal, r - 1))
             biases(2 * r)
             if r >= 1:
-                later = [tensor.pop()] if r == 1 and TURN_FIRST else []
+                later = []
                 tensor += [(turn, k) for k in sorted((2 * r - 1, 2 * r - 2), key=by_words)] + later
             front(2 * r + 1)
-            more_feat(FEAT_SLOTS[2 * r + 1] if 2 * r < len(FEAT_SLOTS) else 0)
             biases(2 * r + 1)
             if r >= 3:
                 vector += multiplies(r - 3)[:1]
@@ -600,44 +613,22 @@ def tile_kplanesgaussiananchordecoder_w4_kernel(
             if r >= 2:
                 vector.append((quantise_weights, 2 * r - 4, 2))
                 tensor += [(products, 2 * r - 4), (products, 2 * r - 3)]
-            if r == 4 and SCALAR_GAIN:
-                vector.append((widen_gain, 0))
             if r >= 3 and jobs[2 * r - 6][1] == PLANES - 1:
                 n = jobs[2 * r - 6][2]
                 close(n, 2)
                 tensor += [(linear, n)] + ([(linear, 1)] if n == 0 else [])
             if r in CAP_VECTOR:
-                vector.append((cap, 2 * (len(CAP_AT) + CAP_VECTOR.index(r))))
+                vector.append((cap, CAP_VECTOR[r]))
 
-        p1, p2 = pairs - 2, pairs - 1
-        a, b = 2 * p2, 2 * p2 + 1
-        p0 = p1 - 1
-        front(a)
-        vector.append((reciprocal, p1))
-        gains(p0)
-        tensor += [(turn, 2 * p1 + 1), (turn, 2 * p1)]
-        front(b)
-        vector += [(multiply, 2 * p0 - 1), (quantise_weights, 2 * p0, 2), (reciprocal, p2), (multiply, 2 * p0 - 2)]
-        tensor += [(products, 2 * p0), (products, 2 * p0 + 1), (turn, b)]
-        gains(p1)
-        vector += [(multiply, 2 * p0 + 1), (multiply, 2 * p0), (quantise_weights, 2 * p1, 2)]
-        tensor += [(turn, a), (products, 2 * p1), (products, 2 * p1 + 1)]
-        vector += [(group, b), (multiply, 2 * p1), (quantise_weights, b, 1), (multiply, 2 * p1 + 1), (quantise_weights, a, 1)]
-        tensor += [(products, b), (products, a), (linear, HALF), (linear, HALF + 1), (linear, HALF + 3), (linear, HALF + 2)]
-        vector += [(quantise_z, HALF, 2), (multiply, b), (multiply, a), (quantise_z, HALF + 3, 1), (bias, HALF)]
-        vector += [(quantise_z, HALF + 2, 1), (bias, HALF + 1), (bias, HALF + 3), (bias, HALF + 2), (finish, 0, 0, H), (finish, 1, 0, H)]
-        parts = [(n, 0, H) for n in range(HALF, TILES - 1)] + [(TILES - 1, lo, lo + H // 2) for lo in (0, H // 2)]
-        vector += [(finish, n, 0, H) for n in range(2, HALF)] + [(finish, *part) for part in parts]
+        vector += parse(DV)
+        scalar += parse(DS)
+        tensor += parse(DT)
 
-        scalar += [(soft_exp, 2)] * (24 in SOFT_AT) + [(normalise, k) for k in (b, a) if road(k) == DIAGONAL]
-        scalar += [(group, 2 * p1)] + [(logarithms, 0, 1)] + [(group, k) for k in (a, b) if by_words(k)] + [(logarithms, 1, 3)]
-        scalar += [(sigmoid, n) for n in (4, 5, 7, 6)] + [(logarithm, *part) for part in parts]
-
-        for r in range(pairs):
+        for r in range(2, pairs):
             both = (2 * r, 2 * r + 1)
             pool += [(pool_gain, k) for k in both if by_words(k)]
             pool += [(normalise, k) for k in both if diagonal_on_pool(k)]
-            pool += [(normalise, k) for k in both if road(k) in (WORDS, POOL)]
+            pool += [(normalise, k) for k in both[::-1] if road(k) in (WORDS, POOL)]
             if r in CAP_AT:
                 pool.append((cap, 2 * CAP_AT.index(r)))
         issue([vector, scalar, pool, tensor])

@@ -40,7 +40,8 @@ BIAS_AT = (17, 18, 19, 20)
 EVAC_AT = {}
 PACES = (1, 4, 0, 4)
 RECIP0 = 0
-COPY_VECTOR = (4, 8)
+COPY_VECTOR = ()
+PAIRED = False
 POOL_FEAT = False
 TURN_FIRST = True
 WIDE = (6, 7)
@@ -50,11 +51,11 @@ DT = "t21 t20 p18 p19 t23 p20 p21 t22 p23 p22 l4 l5 l7 l6"
 NORM_AFTER = True
 SPARE = (2, 3)
 VALUES = 6
-HV = "W0 W2 W3 W4 I0 W5 W6 W7 U0 I1.0.1 n0 I1.1.2 n1 I2.0.1 n2 I2.1.2 n3 U1.1 r0 U2.1 d1 d0 n4 r1 n5 g1 g0"
+HV = "W0 W2 W3 I0 W4 W5 W6 W7 U0 I1.0.1 n0 I1.1.2 n1 I2.0.1 n2 n3 I2.1.2 r0 U1.1 d1 d0 U2.1 r1 n4 g1 n5 g0"
 H3 = "q0.2"
 HS = "W1 Q0 Q1 Q2 Q3 Q4 Q5 Q6 Q7 Q8 Q9 Q10 Q11 Q12 Q13 Q14 Q15 e0 e1 e2 e3 Q16 Q17 Q18 Q19 e4 Q20 Q21 e5 Q22 Q23"
 HT = "D0 D1 D2 D3 D4 D5 t1 t0 D6 t3 t2 D7 p0 p1"
-HG = "w0 d3 d2"
+HG = "d3 d2 w0"
 PARTS = ((4, 0, 128), (4, 128, 512), (5, 0, 512), (6, 0, 512), (7, 0, 256), (7, 256, 512))
 ABS = {0: 21}
 CAP_VECTOR = {10: 2}
@@ -98,8 +99,6 @@ def tile_kplanesgaussiananchordecoder_w4_kernel(
         nc.scalar.dma_start(out=centres[:], in_=cen.rearrange("x (p t) axis -> p x (t axis)", t=4))
         load_feat(0, 0, 2)
         load_feat(0, 2, 4)
-        gain_rows = keep.tile([128, PLANES, 4], BF16, name="gain_rows")
-        nc.sync.dma_start(out=gain_rows[:], in_=ga.rearrange("x (p t) -> p x t", t=4))
         load_feat(1, 0, 4)
         load_feat(2, 0, 4)
         half = N // 2
@@ -112,6 +111,8 @@ def tile_kplanesgaussiananchordecoder_w4_kernel(
             )
 
         load_points(0)
+        gain_rows = keep.tile([128, PLANES, 4], BF16, name="gain_rows")
+        nc.sync.dma_start(out=gain_rows[:], in_=ga.rearrange("x (p t) -> p x t", t=4))
         gain_all = keep.tile([128, PLANES, M], BF16, name="gain_all")
         nc.sync.dma_start(
             out=gain_all[:].rearrange("n x m -> n (x m)"), in_=ga.rearrange("x m -> (x m)").partition_broadcast(128)
@@ -160,11 +161,20 @@ def tile_kplanesgaussiananchordecoder_w4_kernel(
             if j == SCALAR_ROW:
                 nc.scalar.activation(out=target, in_=source.bitcast(FP8), func=ACT.Copy, scale=scale_sb[:, t : t + 1])
                 return
+            if PAIRED and j >= 4:
+                target = later_wide[:].rearrange("p (u a) x c -> p u (a x c)", u=2)[:, t // 2].rearrange("p (c e) -> p c e", e=2)[:, :, t % 2]
             nc.vector.tensor_scalar(
                 out=target, in0=source.bitcast(FP8), scalar1=scale_sb[:, t : t + 1], scalar2=None, op0=ALU.mult
             )
 
         def interleave(pl, lo=0, hi=2):
+            if PAIRED and pl:
+                words = later_wide[:].rearrange("p (u a) x c -> p u (a x c)", u=2).bitcast(F32)[:, :, C * (pl - 1) : C * pl]
+                nc.vector.tensor_copy(
+                    out=side_by_side[:, pl].bitcast(F32).rearrange("p (t m i u) -> p m u i t", t=4, i=2, u=2)[:, 32 * lo : 32 * hi],
+                    in_=words.rearrange("p u (m i t) -> p m u i t", i=2, t=4)[:, 32 * lo : 32 * hi],
+                )
+                return
             widened = first_wide[:] if pl == 0 else later_wide[:, :, pl - 1, :]
             nc.vector.tensor_copy(
                 out=side_by_side[:, pl].rearrange("p (t m i j) -> p m j i t", t=4, i=2, j=4)[:, 32 * lo : 32 * hi],

@@ -46,7 +46,7 @@ POOL_FEAT = False
 TURN_FIRST = True
 WIDE = (6, 7)
 DV = "n22 r10 g19 n23 m17 q18.2 r11 m16 g21 m19 q20.2 m18 g23 m20 q23.1 m21 q22.1 z4.2 m23 m22 z7.1 b4 z6.1 b5 b7 b6 f0 f1 f2 f3 f4 f5 f6 f7.0.2 f7.2.4"
-DS = "e22 g18 e23 x0 d23 g20 x2 L0.1 g22 L1.3 s4 s5 s7 s6 k4 k5 k6 k7.0.2 k7.2.4"
+DS = "e22 g18 e23 x2.2 d23 g20 L0.2 g22 L2.2 s4 s5 s7 s6 k4 k5 k6 k7.0.2 k7.2.4"
 DT = "t21 t20 p18 p19 t23 p20 p21 t22 p23 p22 l4 l5 l7 l6"
 NORM_AFTER = True
 SPARE = (2, 3)
@@ -57,8 +57,11 @@ HS = "W1 Q0 Q1 Q2 Q3 Q4 Q5 Q6 Q7 Q8 Q9 Q10 Q11 Q12 Q13 Q14 Q15 e0 e1 e2 e3 Q16 Q
 HT = "D0 D1 D2 D3 D4 D5 t1 t0 D6 t3 t2 D7 p0 p1"
 HG = "d3 d2 w0"
 PARTS = ((4, 0, 128), (4, 128, 512), (5, 0, 512), (6, 0, 512), (7, 0, 256), (7, 256, 512))
-ABS = {0: 21}
-CAP_VECTOR = {10: 2}
+ABS = (0,)
+POOL_CAPS = ()
+EXTRA_S = {19: "c0.1", 21: "x0.1 x1.1"}
+EXTRA_V = {9: "c1.1", 10: "c2.2"}
+EXTRA_G = {}
 HEAD2 = 0
 TURN2 = False
 CLOCK = ((5, 0), (5, 1), (5, 2))
@@ -428,16 +431,20 @@ def tile_kplanesgaussiananchordecoder_w4_kernel(
         def bias(n, lo=0, hi=H):
             nc.vector.tensor_tensor(out=sums_b[:, n, lo:hi], in0=linear_out[n][:, lo:hi], in1=bias_row[:, lo:hi], op=ALU.add)
 
-        def cap(n):
+        def cap(n, count):
+            part = slice(n, n + count)
             if n in ABS:
-                nc.scalar.activation(out=result_sb[:, n : n + 2, :], in_=sums_b[:, n : n + 2, :], func=ACT.Abs)
+                nc.scalar.activation(out=result_sb[:, part, :], in_=sums_b[:, part, :], func=ACT.Abs)
                 return
-            (nc.gpsimd if n // 2 < len(CAP_AT) else nc.vector).tensor_scalar(
-                out=result_sb[:, n : n + 2, :], in0=sums_b[:, n : n + 2, :], scalar1=CAP, scalar2=LOWEST, op0=ALU.min, op1=ALU.max
+            (nc.gpsimd if n in POOL_CAPS else nc.vector).tensor_scalar(
+                out=result_sb[:, part, :], in0=sums_b[:, part, :], scalar1=CAP, scalar2=LOWEST, op0=ALU.min, op1=ALU.max
             )
 
-        def soft_exp(n):
-            nc.scalar.activation(out=result_sb[:, n : n + 2, :], in_=result_sb[:, n : n + 2, :], func=ACT.Exp, scale=-1.0 if n in ABS else 1.0)
+        def soft_exp(n, count):
+            part = slice(n, n + count)
+            nc.scalar.activation(
+                out=result_sb[:, part, :], in_=result_sb[:, part, :], func=ACT.Exp, scale=-1.0 if n in ABS else 1.0
+            )
 
         def sigmoid(n, lo=0, hi=H):
             nc.scalar.activation(out=result_sb[:, n, lo:hi], in_=sums_b[:, n, lo:hi], func=ACT.Sigmoid, scale=-1.0)
@@ -452,7 +459,7 @@ def tile_kplanesgaussiananchordecoder_w4_kernel(
 
         def finish(n, lo, hi):
             part = result_sb[:, n, lo:hi]
-            if n - n % 2 in ABS:
+            if n in ABS:
                 nc.vector.scalar_tensor_tensor(
                     out=part, in0=sums_b[:, n, lo:hi], scalar=0.0, in1=part, op0=ALU.max, op1=ALU.add
                 )
@@ -506,13 +513,13 @@ def tile_kplanesgaussiananchordecoder_w4_kernel(
             if stage == bias:
                 return [(linear, i)]
             if stage == cap:
-                return [(bias, i), (bias, i + 1)]
+                return [(bias, i + j) for j in range(rest[0])]
             if stage == sigmoid:
                 return [(bias, i, *rest[:1])]
             if stage == soft_exp:
-                return [(cap, i)]
+                return [(cap, i + j) for j in range(rest[0])]
             if stage == logarithms:
-                return [(soft_exp, 0), (soft_exp, 2)]
+                return [(soft_exp, j) for j in range(HALF)]
             if stage == logarithm:
                 return [(sigmoid, TILES - 2)]
             if stage == finish:
@@ -526,7 +533,7 @@ def tile_kplanesgaussiananchordecoder_w4_kernel(
                     while order and all(need in made or need[1] < 0 for need in needs(*order[0])):
                         stage, i, *rest = order.pop(0)
                         stage(i, *rest)
-                        several = stage in (quantise_weights, quantise_z, logarithms) or (stage == quantise_feat and rest)
+                        several = stage in (quantise_weights, quantise_z, logarithms, cap, soft_exp) or (stage == quantise_feat and rest)
                         made.update((stage, i + j) for j in range(rest[0] if several else 1))
                         if stage in (logarithm, bias, sigmoid) and rest:
                             made.add((stage, i, rest[0]))
@@ -553,9 +560,7 @@ def tile_kplanesgaussiananchordecoder_w4_kernel(
                 scalar.append((group, k - 4))
             scalar.extend((multiply, j) for j in sorted(SCALAR_GAIN, reverse=True) if SCALAR_GAIN[j] == k)
             more_squares(PACES[k] if k < len(PACES) else 2)
-            scalar.extend((cap, n) for n in ABS if ABS[n] == k)
-            if k in SOFT_AT:
-                scalar.append((soft_exp, 2 * SOFT_AT.index(k)))
+            scalar.extend(parse(EXTRA_S.get(k, "")))
             if k + 2 < JOBS:
                 tensor.append((distances, k + 2))
 
@@ -587,6 +592,8 @@ def tile_kplanesgaussiananchordecoder_w4_kernel(
                     out.append(({"I": interleave, "U": quantise_feat}[w[0]], *i))
                 elif w[0] == "z":
                     out.append((quantise_z, i[0], i[1]))
+                elif w[0] in "cx":
+                    out.append(({"c": cap, "x": soft_exp}[w[0]], i[0], i[1]))
                 elif w[0] == "L":
                     out.append((logarithms, i[0], i[1]))
                 elif w[0] in "fk" or len(i) > 1:
@@ -627,8 +634,7 @@ def tile_kplanesgaussiananchordecoder_w4_kernel(
                 n = jobs[2 * r - 6][2]
                 close(n, 2)
                 tensor += [(linear, n)] + ([(linear, 1)] if n == 0 else [])
-            if r in CAP_VECTOR:
-                vector.append((cap, CAP_VECTOR[r]))
+            vector += parse(EXTRA_V.get(r, ""))
 
         vector += parse(DV)
         scalar += parse(DS)
@@ -639,6 +645,5 @@ def tile_kplanesgaussiananchordecoder_w4_kernel(
             pool += [(pool_gain, k) for k in both if by_words(k)]
             pool += [(normalise, k) for k in both if diagonal_on_pool(k)]
             pool += [(normalise, k) for k in both[::-1] if road(k) in (WORDS, POOL)]
-            if r in CAP_AT:
-                pool.append((cap, 2 * CAP_AT.index(r)))
+            pool += parse(EXTRA_G.get(r, ""))
         issue([vector, scalar, pool, tensor])

@@ -38,10 +38,10 @@ LAST = ("words", "diagonal")
 VECTOR_DIAG = (1,)
 BIAS_AT = (17, 18, 19, 20)
 EVAC_AT = {}
-PACES = (1, 4, 0, 4)
+PACES = {}
 RECIP0 = 0
 COPY_VECTOR = ()
-PAIRED = False
+PAIRED = True
 POOL_FEAT = False
 TURN_FIRST = True
 WIDE = (6, 7)
@@ -50,12 +50,14 @@ DS = "e22 g18 e23 x2.2 d23 g20 L0.2 g22 L2.2 s4 s5 s7 s6 k4 k5 k6 k7.0.2 k7.2.4"
 DT = "t21 t20 p18 p19 t23 p20 p21 t22 p23 p22 l4 l5 l7 l6"
 NORM_AFTER = True
 SPARE = (2, 3)
+POOL_SQ = (23,)
+GAIN_ON = "vector"
 VALUES = 6
-HV = "W0 W2 W3 I0 W4 W5 W6 W7 U0 I1.0.1 n0 I1.1.2 n1 I2.0.1 n2 n3 I2.1.2 r0 U1.1 d1 d0 U2.1 r1 n4 g1 n5 g0"
-H3 = "q0.2"
-HS = "W1 Q0 Q1 Q2 Q3 Q4 Q5 Q6 Q7 Q8 Q9 Q10 Q11 Q12 Q13 Q14 Q15 e0 e1 e2 e3 Q16 Q17 Q18 Q19 e4 Q20 Q21 e5 Q22 Q23"
+HV = "W0 W2 W3 I0 W4 W5 W6 W7 U0 I1 I2 n0 n1 n2 n3 n4 r0 U1.1 d1 d0 U2.1 r1 n5 g1 g0"
+H3 = "q0.2 w0"
+HS = "W1 Q0 Q1 Q2 Q3 Q4 Q5 Q6 Q7 Q8 Q9 Q10 Q11 Q12 Q13 Q14 Q15 e0 e1 e2 e3 Q16 Q17 Q18 Q19 e4 Q20 Q21 e5 Q22"
 HT = "D0 D1 D2 D3 D4 D5 t1 t0 D6 t3 t2 D7 p0 p1"
-HG = "d3 d2 w0"
+HG = "S23 Q23 d3 d2"
 PARTS = ((4, 0, 128), (4, 128, 512), (5, 0, 512), (6, 0, 512), (7, 0, 256), (7, 256, 512))
 ABS = (0,)
 POOL_CAPS = ()
@@ -211,17 +213,38 @@ def tile_kplanesgaussiananchordecoder_w4_kernel(
         def diagonal_on_pool(k):
             return road(k) == DIAGONAL and k not in VECTOR_DIAG and POOL_DIAG[0] <= k // 2 < POOL_DIAG[1]
 
+        def differences(q):
+            i = POOL_SQ.index(q)
+            return later_wide[:].rearrange("p j x c -> p (j x c)").bitcast(F32)[:, 1024 * i + 512 : 1024 * i + 1024]
+
+        def subtract(q):
+            step, within = divmod(q, 8)
+            t, axis = divmod(within, 2)
+            first, count, pl = steps[step]
+            nc.gpsimd.tensor_scalar(
+                out=differences(q),
+                in0=points[first // HALF][:, :, COORDS[pl][axis]],
+                scalar1=-1.0,
+                scalar2=centres[:, pl, 2 * t + axis : 2 * t + axis + 1],
+                op0=ALU.mult,
+                op1=ALU.add,
+            )
+
         def square(q):
             step, within = divmod(q, 8)
             t, axis = divmod(within, 2)
             first, count, pl = steps[step]
-            if within == 0:
+            if step not in squared:
                 squared[step] = work.tile([128, 2, 4, count * 128], F32, name="squared", tag="squared%d" % count, bufs=3)
             if step == 0:
                 coordinate = head_coords[axis]
             else:
                 h, start = divmod(128 * first, half)
                 coordinate = points[h][:, start : start + 128 * count, COORDS[pl][axis]]
+            if q in POOL_SQ:
+                both = differences(q)
+                nc.gpsimd.tensor_tensor(out=squared[step][:, axis, t, :], in0=both, in1=both, op=ALU.mult)
+                return
             nc.scalar.activation(
                 out=squared[step][:, axis, t, :],
                 in_=coordinate,
@@ -233,7 +256,7 @@ def tile_kplanesgaussiananchordecoder_w4_kernel(
         def distances(k):
             step, pl, n = jobs[k]
             i = n - steps[step][0]
-            banks, tag = (ps_f, "f") if k in SPARE else (ps_d2, "d2")
+            banks, tag = {1: (ps_f, "f"), 2: (ps_o, "o")}.get(k // 2, (ps_d2, "d2"))
             distance[k] = banks.tile([128, 4, 128], F32, name="d2", tag=tag)
             for t in range(4):
                 for axis in range(2):
@@ -479,11 +502,13 @@ def tile_kplanesgaussiananchordecoder_w4_kernel(
         def needs(stage, i, *rest):
             if stage == interleave:
                 return [(widen, j) for j in (range(4) if i == 0 else range(4, 8))]
+            if stage == subtract:
+                return [(quantise_feat, 0), (minimum, 0)]
             if stage == square:
                 same = [s for s in range(i // 8) if steps[s][1] == steps[i // 8][1]]
                 return [(distances, first_job[same[-3]] + steps[same[-3]][1] - 1)] if len(same) >= 3 else []
             if stage == distances:
-                return [(square, 8 * jobs[i][0] + 7), (minimum, i - (4 if SPARE and i < SPARE[-1] + 3 else 2))]
+                return [(square, 8 * jobs[i][0] + j) for j in range(8)] + [(minimum, i - (6 if i < 8 else 2))]
             if stage == minimum:
                 return [(distances, i), (exponential, i - VALUES)]
             if stage == exponential:
@@ -541,7 +566,7 @@ def tile_kplanesgaussiananchordecoder_w4_kernel(
                 assert moved
 
         def widen_gain(i):
-            nc.gpsimd.tensor_copy(out=channel_gain32[:], in_=channel_gain[:])
+            (nc.vector if GAIN_ON == "vector" else nc.gpsimd).tensor_copy(out=channel_gain32[:], in_=channel_gain[:])
 
         spread_points(0)
         spread_points(1)
@@ -559,7 +584,7 @@ def tile_kplanesgaussiananchordecoder_w4_kernel(
             if k >= 4 and by_words(k - 4) and k - 4 not in COPY_VECTOR:
                 scalar.append((group, k - 4))
             scalar.extend((multiply, j) for j in sorted(SCALAR_GAIN, reverse=True) if SCALAR_GAIN[j] == k)
-            more_squares(PACES[k] if k < len(PACES) else 2)
+            more_squares(PACES.get(k, 2))
             scalar.extend(parse(EXTRA_S.get(k, "")))
             if k + 2 < JOBS:
                 tensor.append((distances, k + 2))
@@ -580,7 +605,7 @@ def tile_kplanesgaussiananchordecoder_w4_kernel(
                 if n == 1:
                     tensor.append((linear, 3))
 
-        names = dict(m=multiply, g=group, r=reciprocal, n=minimum, b=bias, e=exponential, d=normalise, s=sigmoid, t=turn, p=products, l=linear, x=soft_exp, c=cap, D=distances, W=widen, Q=square, G=pool_gain, w=widen_gain)
+        names = dict(m=multiply, g=group, r=reciprocal, n=minimum, b=bias, e=exponential, d=normalise, s=sigmoid, t=turn, p=products, l=linear, x=soft_exp, c=cap, D=distances, W=widen, Q=square, G=pool_gain, w=widen_gain, S=subtract)
 
         def parse(text):
             out = []
@@ -607,7 +632,7 @@ def tile_kplanesgaussiananchordecoder_w4_kernel(
         scalar += parse(HS)
         tensor += parse(HT)
         pool += parse(HG)
-        squares_left = [q for q in squares_left if (square, q) not in scalar + pool]
+        squares_left = [q for q in squares_left if (square, q) not in scalar + pool and q not in POOL_SQ]
 
         for r in range(3, pairs - 1):
             front(2 * r)

@@ -26,49 +26,12 @@ CAP = 40.0
 LOWEST = -3.0e38
 
 HALF = TILES // 2
-FEAT_AHEAD = 13
-FEAT_SLOTS = (2, 2, 1, 1)
 SCALAR_ROW = 1
-SQUARES_AHEAD = 3
+POOL_SQUARE = 8 * 3 - 1
+CLOCK_JOB, CLOCK_BLOCKS = 5, 3
+ABS_TILE = 0
 EXPO_BUFFERS = 10
-POOL_DIAG = (1, 11)
-SCALAR_GAIN = {12: 18, 13: 18, 14: 20, 15: 20}
-HEAD = ("vector", "diagonal", "pool")
-LAST = ("words", "diagonal")
-VECTOR_DIAG = (1,)
-BIAS_AT = (17, 18, 19, 20)
-EVAC_AT = {}
-PACES = {}
-RECIP0 = 0
-COPY_VECTOR = ()
-PAIRED = True
-POOL_FEAT = False
-TURN_FIRST = True
-WIDE = (6, 7)
-DV = "n22 r10 g19 n23 m17 q18.2 r11 m16 g21 m19 q20.2 m18 g23 m20 q23.1 m21 q22.1 z4.2 m23 m22 z7.1 b4 z6.1 b5 b7 b6 f0 f1 f2 f3 f4 f5 f6 f7.0.2 f7.2.4"
-DS = "e22 g18 e23 x2.2 d23 g20 L0.2 g22 L2.2 s4 s5 s7 s6 k4 k5 k6 k7.0.2 k7.2.4"
-DT = "t21 t20 p18 p19 t23 p20 p21 t22 p23 p22 l4 l5 l7 l6"
-NORM_AFTER = True
-SPARE = (2, 3)
-POOL_SQ = (23,)
-GAIN_ON = "vector"
-VALUES = 6
-HV = "W0 W2 W3 I0 W4 W5 W6 W7 U0 I1 I2 n0 n1 n2 n3 n4 r0 U1.1 d1 d0 U2.1 r1 n5 g1 g0"
-H3 = "q0.2 w0"
-HS = "W1 Q0 Q1 Q2 Q3 Q4 Q5 Q6 Q7 Q8 Q9 Q10 Q11 Q12 Q13 Q14 Q15 e0 e1 e2 e3 Q16 Q17 Q18 Q19 e4 Q20 Q21 e5 Q22"
-HT = "D0 D1 D2 D3 D4 D5 t1 t0 D6 t3 t2 D7 p0 p1"
-HG = "S23 Q23 d3 d2"
-PARTS = ((4, 0, 128), (4, 128, 512), (5, 0, 512), (6, 0, 512), (7, 0, 256), (7, 256, 512))
-ABS = (0,)
-POOL_CAPS = ()
-EXTRA_S = {19: "c0.1", 21: "x0.1 x1.1"}
-EXTRA_V = {9: "c1.1", 10: "c2.2"}
-EXTRA_G = {}
-HEAD2 = 0
-TURN2 = False
-CLOCK = ((5, 0), (5, 1), (5, 2))
-CAP_AT = ()
-SOFT_AT = ()
+VALUE_BUFFERS = 6
 VECTOR, POOL, WORDS, DIAGONAL = "vector", "pool", "words", "diagonal"
 
 
@@ -85,11 +48,8 @@ def tile_kplanesgaussiananchordecoder_w4_kernel(
         ps_o = ctx.enter_context(tc.psum_pool(name="ps_o", bufs=2))
         ctx.enter_context(tc.manual_schedule())
 
-        head_tiles = HALF
-        head_points = keep.tile([128, head_tiles, 4], BF16, name="head_points")
-        nc.scalar.dma_start(
-            out=head_points[:, :, 0:3], in_=pts[0 : 128 * head_tiles, :].rearrange("(j p) x -> p j x", p=128)
-        )
+        head_points = keep.tile([128, HALF * 3], BF16, name="head_points")
+        nc.scalar.dma_start(out=head_points[:], in_=pts[0 : 128 * HALF, :].rearrange("(p j) x -> p (j x)", j=HALF))
         scale_sb = keep.tile([128, 4], F32, name="scale_sb")
         nc.sync.dma_start(out=scale_sb[:], in_=feat_scale.rearrange("o (p t) x -> p (o t x)", t=4))
         first_bytes = keep.tile([128, 4, C], U8, name="first_bytes")
@@ -100,8 +60,9 @@ def tile_kplanesgaussiananchordecoder_w4_kernel(
             target = first_bytes[:, lo:hi, :] if pl == 0 else later_bytes[:, lo:hi, pl - 1, :]
             nc.sync.dma_start(out=target, in_=rows[:, lo:hi, :])
 
-        centres = keep.tile([128, PLANES, 8], BF16, name="centres")
-        nc.scalar.dma_start(out=centres[:], in_=cen.rearrange("x (p t) axis -> p x (t axis)", t=4))
+        centre_rows = cen.rearrange("x (p t) axis -> p x (t axis)", t=4)
+        first_centres = keep.tile([128, 8], BF16, name="first_centres")
+        nc.scalar.dma_start(out=first_centres[:], in_=centre_rows[:, 0, :])
         load_feat(0, 0, 2)
         load_feat(0, 2, 4)
         load_feat(1, 0, 4)
@@ -116,6 +77,9 @@ def tile_kplanesgaussiananchordecoder_w4_kernel(
             )
 
         load_points(0)
+        later_centres = keep.tile([128, PLANES - 1, 8], BF16, name="later_centres")
+        nc.sync.dma_start(out=later_centres[:], in_=centre_rows[:, 1:PLANES, :])
+        centres = [first_centres[:]] + [later_centres[:, i, :] for i in range(PLANES - 1)]
         gain_rows = keep.tile([128, PLANES, 4], BF16, name="gain_rows")
         nc.sync.dma_start(out=gain_rows[:], in_=ga.rearrange("x (p t) -> p x t", t=4))
         gain_all = keep.tile([128, PLANES, M], BF16, name="gain_all")
@@ -141,117 +105,96 @@ def tile_kplanesgaussiananchordecoder_w4_kernel(
         ident = keep.tile([128, 128], F32, name="ident")
         nc.scalar.activation(out=ident[:], in_=ident_bf[:], func=ACT.Copy)
 
-        steps = [(first, HALF, pl) for first in (0, HALF) for pl in range(PLANES)]
-        jobs = [(s, pl, first + i) for s, (first, count, pl) in enumerate(steps) for i in range(count)]
+        steps = [(first, pl) for first in (0, HALF) for pl in range(PLANES)]
+        jobs = [(s, pl, first + i) for s, (first, pl) in enumerate(steps) for i in range(HALF)]
 
         head_coords = []
 
         def spread_points(x):
-            bank = ps_o.tile([128, head_tiles, 128], BF16, name="head_bank", tag="o")
-            for j in range(head_tiles):
-                nc.tensor.transpose(bank[:, j, :], head_points[:, j, x : x + 1].to_broadcast([128, 128]), ident_bf[:])
-            head_coords.append(bank[:].rearrange("p j n -> p (j n)"))
+            bank = ps_o.tile([128, HALF, 128], BF16, name="head_bank", tag="o")
+            for j in range(HALF):
+                column = head_points[:, 3 * j + x : 3 * j + x + 1]
+                nc.tensor.transpose(bank[:, j, :], column.to_broadcast([128, 128]), ident_bf[:])
+            head_coords.append(bank[:].rearrange("p j n -> p n j"))
 
         feat_words = keep.tile([128, PLANES, C], U32, name="feat_words", align_bytes=64)
         feat_scales = keep.tile([128, PLANES, C], U8, name="feat_scales", align_bytes=64)
 
         first_wide = keep.tile([128, 4, C], BF16, name="first_wide")
-        later_wide = keep.tile([128, 4, 2, C], BF16, name="later_wide")
+        later_wide = keep.tile([128, 2, 2 * C, 2], BF16, name="later_wide")
+        later_words = later_wide[:].rearrange("p u c e -> p u (c e)").bitcast(F32)
         side_by_side = keep.tile([128, PLANES, 4 * C], BF16, name="side_by_side", align_bytes=64)
 
         def widen(j):
             t = j % 4
             source = first_bytes[:, t, :] if j < 4 else later_bytes[:, t].rearrange("p x c -> p (x c)")
-            target = first_wide[:, t, :] if j < 4 else later_wide[:, t].rearrange("p x c -> p (x c)")
+            target = first_wide[:, t, :] if j < 4 else later_wide[:, t // 2, :, t % 2]
             if j == SCALAR_ROW:
                 nc.scalar.activation(out=target, in_=source.bitcast(FP8), func=ACT.Copy, scale=scale_sb[:, t : t + 1])
-                return
-            if PAIRED and j >= 4:
-                target = later_wide[:].rearrange("p (u a) x c -> p u (a x c)", u=2)[:, t // 2].rearrange("p (c e) -> p c e", e=2)[:, :, t % 2]
-            nc.vector.tensor_scalar(
-                out=target, in0=source.bitcast(FP8), scalar1=scale_sb[:, t : t + 1], scalar2=None, op0=ALU.mult
-            )
-
-        def interleave(pl, lo=0, hi=2):
-            if PAIRED and pl:
-                words = later_wide[:].rearrange("p (u a) x c -> p u (a x c)", u=2).bitcast(F32)[:, :, C * (pl - 1) : C * pl]
-                nc.vector.tensor_copy(
-                    out=side_by_side[:, pl].bitcast(F32).rearrange("p (t m i u) -> p m u i t", t=4, i=2, u=2)[:, 32 * lo : 32 * hi],
-                    in_=words.rearrange("p u (m i t) -> p m u i t", i=2, t=4)[:, 32 * lo : 32 * hi],
+            else:
+                nc.vector.tensor_scalar(
+                    out=target, in0=source.bitcast(FP8), scalar1=scale_sb[:, t : t + 1], scalar2=None, op0=ALU.mult
                 )
-                return
-            widened = first_wide[:] if pl == 0 else later_wide[:, :, pl - 1, :]
-            nc.vector.tensor_copy(
-                out=side_by_side[:, pl].rearrange("p (t m i j) -> p m j i t", t=4, i=2, j=4)[:, 32 * lo : 32 * hi],
-                in_=widened.rearrange("p j (m i t) -> p m j i t", i=2, t=4)[:, 32 * lo : 32 * hi],
-            )
 
-        def quantise_feat(pl, count=1):
-            nc.vector.quantize_mx(
-                out=feat_words[:, pl : pl + count].rearrange("p x c -> p (x c)").bitcast(FP8X4),
-                scales=feat_scales[:, pl : pl + count].rearrange("p x c -> p (x c)"),
-                in_=side_by_side[:, pl : pl + count].rearrange("p x c -> p (x c)"),
-            )
+        def interleave(pl):
+            if pl == 0:
+                target = side_by_side[:, pl].rearrange("p (t m i j) -> p m j i t", t=4, i=2, j=4)
+                source = first_wide[:].rearrange("p j (m i t) -> p m j i t", i=2, t=4)
+            else:
+                target = side_by_side[:, pl].bitcast(F32).rearrange("p (t m i u) -> p m u i t", t=4, i=2, u=2)
+                source = later_words[:, :, C * (pl - 1) : C * pl].rearrange("p u (m i t) -> p m u i t", i=2, t=4)
+            nc.vector.tensor_copy(out=target, in_=source)
+
+        def quantise_feat(pl):
+            nc.vector.quantize_mx(out=feat_words[:, pl].bitcast(FP8X4), scales=feat_scales[:, pl], in_=side_by_side[:, pl])
+
+        def widen_gain(i):
+            nc.vector.tensor_copy(out=channel_gain32[:], in_=channel_gain[:])
 
         squared, distance, scaled, expo, sums, recips, gained, weights = ({} for i in range(8))
         turned, grouped, codes, feature, partial, z_pair, z_codes, linear_out = ({} for i in range(8))
-        first_job = [[s for s, pl, n in jobs].index(s) for s in range(len(steps))]
+        diagonal, pair_codes, pair_blocks = {}, {}, {}
         pairs = JOBS // 2
         last = JOBS - 1
-        diagonal, pair_codes, whole, pair_blocks = {}, {}, [], {}
+        emptied_by_scalar = (pairs // 2, pairs // 2 + 1)
 
         def road(k):
-            if k < len(HEAD):
-                return HEAD[k]
-            if k >= last - 1:
-                return LAST[k - last + 1]
-            return DIAGONAL if k % 2 else WORDS
+            if k % 2:
+                return DIAGONAL
+            return {0: VECTOR, 2: POOL}.get(k, WORDS)
 
         def by_words(k):
             return road(k) == WORDS
 
-        def diagonal_on_pool(k):
-            return road(k) == DIAGONAL and k not in VECTOR_DIAG and POOL_DIAG[0] <= k // 2 < POOL_DIAG[1]
+        def normaliser(k):
+            return nc.vector if k < 2 else nc.scalar if k == last else nc.gpsimd
 
-        def differences(q):
-            i = POOL_SQ.index(q)
-            return later_wide[:].rearrange("p j x c -> p (j x c)").bitcast(F32)[:, 1024 * i + 512 : 1024 * i + 1024]
-
-        def subtract(q):
+        def square_operands(q):
             step, within = divmod(q, 8)
             t, axis = divmod(within, 2)
-            first, count, pl = steps[step]
+            first, pl = steps[step]
+            coordinate = head_coords[axis] if step == 0 else points[first // HALF][:, :, COORDS[pl][axis]]
+            return step, t, axis, coordinate, centres[pl][:, 2 * t + axis : 2 * t + axis + 1]
+
+        differences = later_words[:, 0, C : 2 * C]
+
+        def subtract(q):
+            step, t, axis, coordinate, centre = square_operands(q)
             nc.gpsimd.tensor_scalar(
-                out=differences(q),
-                in0=points[first // HALF][:, :, COORDS[pl][axis]],
-                scalar1=-1.0,
-                scalar2=centres[:, pl, 2 * t + axis : 2 * t + axis + 1],
-                op0=ALU.mult,
-                op1=ALU.add,
+                out=differences, in0=coordinate, scalar1=-1.0, scalar2=centre, op0=ALU.mult, op1=ALU.add
             )
 
         def square(q):
-            step, within = divmod(q, 8)
-            t, axis = divmod(within, 2)
-            first, count, pl = steps[step]
+            step, t, axis, coordinate, centre = square_operands(q)
             if step not in squared:
-                squared[step] = work.tile([128, 2, 4, count * 128], F32, name="squared", tag="squared%d" % count, bufs=3)
+                squared[step] = work.tile([128, 2, 4, half], F32, name="squared", bufs=3)
+            target = squared[step][:, axis, t, :]
             if step == 0:
-                coordinate = head_coords[axis]
+                target = target.rearrange("p (n j) -> p n j", j=HALF)
+            if q == POOL_SQUARE:
+                nc.gpsimd.tensor_tensor(out=target, in0=differences, in1=differences, op=ALU.mult)
             else:
-                h, start = divmod(128 * first, half)
-                coordinate = points[h][:, start : start + 128 * count, COORDS[pl][axis]]
-            if q in POOL_SQ:
-                both = differences(q)
-                nc.gpsimd.tensor_tensor(out=squared[step][:, axis, t, :], in0=both, in1=both, op=ALU.mult)
-                return
-            nc.scalar.activation(
-                out=squared[step][:, axis, t, :],
-                in_=coordinate,
-                func=ACT.Square,
-                scale=-1.0,
-                bias=centres[:, pl, 2 * t + axis : 2 * t + axis + 1],
-            )
+                nc.scalar.activation(out=target, in_=coordinate, func=ACT.Square, scale=-1.0, bias=centre)
 
         def distances(k):
             step, pl, n = jobs[k]
@@ -266,12 +209,12 @@ def tile_kplanesgaussiananchordecoder_w4_kernel(
                         rhs=ident[:],
                         start=(axis == 0),
                         stop=(axis == 1),
-                        is_transpose=not (axis == 0 and (k, t) in CLOCK),
+                        is_transpose=not (axis == 0 and k == CLOCK_JOB and t < CLOCK_BLOCKS),
                     )
 
         def minimum(k):
-            values = work.tile([128, M], F32, name="values", bufs=VALUES)
-            least = work.tile([128, 1], F32, name="least", bufs=VALUES)
+            values = work.tile([128, M], F32, name="values", bufs=VALUE_BUFFERS)
+            least = work.tile([128, 1], F32, name="least", bufs=VALUE_BUFFERS)
             target, source = values[:], distance[k][:].rearrange("n t p -> n (t p)")
             if by_words(k):
                 target = values[:].rearrange("n (p t) -> n p t", t=4)
@@ -300,17 +243,14 @@ def tile_kplanesgaussiananchordecoder_w4_kernel(
             nc.vector.reciprocal(out=recips[r][:], in_=sums[r][:])
 
         def pool_gain(k):
-            if 4 <= k < last:
-                gained[k] = grouped[k // 2 - 2][:].rearrange("p j n t -> p (j n t)").bitcast(F32)
-            else:
-                gained[k] = expo[k][:]
+            gained[k] = grouped[k // 2 - 2][:].rearrange("p j n t -> p (j n t)").bitcast(F32)
             nc.gpsimd.tensor_tensor(out=gained[k], in0=expo[k][:], in1=gain_all[:, jobs[k][1], :], op=ALU.mult)
 
         def normalise(k):
             source = target = expo[k][:]
             factor = recips[k // 2][:, k % 2 : k % 2 + 1]
             if road(k) == WORDS:
-                if k == last - 1 and NORM_AFTER:
+                if k == last - 1:
                     weights[k] = grouped[k // 2 - 1][:, 0].rearrange("p n t -> p (n t)")
                 else:
                     weights[k] = work.tile([128, M], BF16, name="weights", bufs=4)
@@ -319,9 +259,9 @@ def tile_kplanesgaussiananchordecoder_w4_kernel(
             if road(k) == DIAGONAL:
                 diagonal[k] = work.tile([128, 128], F32, name="diagonal")
                 source, target = ident[:], diagonal[k][:]
-            if road(k) == VECTOR or k in VECTOR_DIAG:
+            if normaliser(k) is nc.vector:
                 nc.vector.tensor_scalar(out=target, in0=source, scalar1=factor, scalar2=None, op0=ALU.mult)
-            elif road(k) == DIAGONAL and not diagonal_on_pool(k):
+            elif normaliser(k) is nc.scalar:
                 nc.scalar.activation(out=target, in_=source, func=ACT.Copy, scale=factor)
             else:
                 nc.gpsimd.tensor_scalar(out=target, in0=source, scalar1=factor, scalar2=1.0, op0=ALU.mult, op1=ALU.mult)
@@ -342,8 +282,7 @@ def tile_kplanesgaussiananchordecoder_w4_kernel(
                 grouped[k // 2] = work.tile([128, 2, 128, 4], BF16, name="grouped", align_bytes=64, bufs=7)
             target = grouped[k // 2][:, k % 2]
             if by_words(k):
-                copy = nc.vector.tensor_copy if k in COPY_VECTOR else nc.scalar.copy
-                copy(out=target.bitcast(F32), in_=turned[k][:].rearrange("p u n -> p n u"))
+                nc.scalar.copy(out=target.bitcast(F32), in_=turned[k][:].rearrange("p u n -> p n u"))
             else:
                 nc.vector.tensor_tensor(
                     out=target,
@@ -357,70 +296,56 @@ def tile_kplanesgaussiananchordecoder_w4_kernel(
             scales = work.tile([128, 128 * count], U8, name=name + "_scales", tag=name + "_scales", align_bytes=64, bufs=3)
             flat = source.rearrange("p j n t -> p (j n t)")
             nc.vector.quantize_mx(out=words[:].bitcast(FP8X4), scales=scales[:], in_=flat)
-            whole.append((words[:].bitcast(FP8X4), scales[:]))
-            columns = [slice(128 * j, 128 * j + 128) for j in range(count)]
-            return [(words[:, part].bitcast(FP8X4), scales[:, part]) for part in columns]
+            return words, scales
+
+        def operand(words, scales, lo, hi):
+            return words[:, 128 * lo : 128 * hi].bitcast(FP8X4), scales[:, 128 * lo : 128 * hi]
 
         def quantise_weights(k, count):
-            for j, operand in enumerate(quantise(grouped[k // 2][:, k % 2 : k % 2 + count], count, "a")):
-                codes[k + j] = operand
-            pair_codes[k // 2] = whole[-1]
+            words, scales = quantise(grouped[k // 2][:, k % 2 : k % 2 + count], count, "a")
+            pair_codes[k // 2] = operand(words, scales, 0, count)
+            for j in range(count):
+                codes[k + j] = operand(words, scales, j, j + 1)
 
         def products(k):
             pl = jobs[k][1]
+            wide = k // 2 in emptied_by_scalar
+            blocks = range(2 * (k % 2), 2 * (k % 2) + 2) if wide else range(4)
+            moving = pair_codes[k // 2] if wide else codes[k]
             banks, tag = (ps_d2, "d2") if k // 2 in (pairs - 3, pairs - 1) else (ps_f, "f")
-            if k // 2 in WIDE:
-                feature[k] = banks.tile([128, 2, 256], F32, name="feature", tag=tag)
-                for i in range(2):
-                    t = 2 * (k % 2) + i
-                    nc.tensor.matmul_mx(
-                        out=feature[k][:, i, :],
-                        lhsT=feat_words[:, pl, 128 * t : 128 * t + 128].bitcast(FP8X4),
-                        lhsT_scale=feat_scales[:, pl, 128 * t : 128 * t + 128],
-                        rhs=pair_codes[k // 2][0],
-                        rhs_scale=pair_codes[k // 2][1],
-                        start=True,
-                        stop=True,
-                    )
-                return
-            feature[k] = banks.tile([128, 4, 128], F32, name="feature", tag=tag)
-            for t in range(4):
+            feature[k] = banks.tile([128, len(blocks), 512 // len(blocks)], F32, name="feature", tag=tag)
+            for i, t in enumerate(blocks):
                 nc.tensor.matmul_mx(
-                    out=feature[k][:, t, :],
+                    out=feature[k][:, i, :],
                     lhsT=feat_words[:, pl, 128 * t : 128 * t + 128].bitcast(FP8X4),
                     lhsT_scale=feat_scales[:, pl, 128 * t : 128 * t + 128],
-                    rhs=codes[k][0],
-                    rhs_scale=codes[k][1],
+                    rhs=moving[0],
+                    rhs_scale=moving[1],
                     start=True,
                     stop=True,
                 )
 
+        def empty(k):
+            n = jobs[k][2]
+            if k // 2 not in pair_blocks:
+                pair_blocks[k // 2] = keep.tile([128, 4, 256], F32, name="blocks%d" % (k // 2))
+                for j in range(2):
+                    part = pair_blocks[k // 2][:, :, 128 * j : 128 * j + 128]
+                    partial[n - k % 2 + j] = part.rearrange("p t n -> p n t")
+            for i in range(2):
+                t = 2 * (k % 2) + i
+                nc.scalar.activation(
+                    out=pair_blocks[k // 2][:, t, :],
+                    in_=feature[k][:, i, :],
+                    func=ACT.Copy,
+                    scale=channel_gain32[:, t : t + 1],
+                )
+
         def multiply(k):
+            if k // 2 in emptied_by_scalar:
+                return empty(k)
             step, pl, n = jobs[k]
             other = channel_gain[:].unsqueeze(1).to_broadcast([128, 128, 4]) if pl == 0 else partial[n]
-            if k // 2 in WIDE:
-                if k // 2 not in pair_blocks:
-                    pair_blocks[k // 2] = keep.tile([128, 4, 256], F32, name="blocks%d" % (k // 2))
-                    for j in range(2):
-                        part = pair_blocks[k // 2][:, :, 128 * j : 128 * j + 128]
-                        partial[n - k % 2 + j] = part.rearrange("p t n -> p n t")
-                for i in range(2):
-                    t = 2 * (k % 2) + i
-                    nc.scalar.activation(
-                        out=pair_blocks[k // 2][:, t, :],
-                        in_=feature[k][:, i, :],
-                        func=ACT.Copy,
-                        scale=channel_gain32[:, t : t + 1],
-                    )
-                return
-            if pl == 0 and k in SCALAR_GAIN:
-                blocks = work.tile([128, 4, 128], F32, name="partial", bufs=7)
-                for t in range(4):
-                    nc.scalar.activation(
-                        out=blocks[:, t, :], in_=feature[k][:, t, :], func=ACT.Copy, scale=channel_gain32[:, t : t + 1]
-                    )
-                partial[n] = blocks[:].rearrange("p t n -> p n t")
-                return
             if pl < PLANES - 1:
                 result = work.tile([128, 128, 4], F32, name="partial", bufs=7)[:]
                 partial[n] = result
@@ -431,8 +356,9 @@ def tile_kplanesgaussiananchordecoder_w4_kernel(
             nc.vector.tensor_tensor(out=result, in0=feature[k][:].rearrange("p t n -> p n t"), in1=other, op=ALU.mult)
 
         def quantise_z(n, count):
-            for j, operand in enumerate(quantise(z_pair[n // 2][:, n % 2 : n % 2 + count], count, "z")):
-                z_codes[n + j] = operand
+            words, scales = quantise(z_pair[n // 2][:, n % 2 : n % 2 + count], count, "z")
+            for j in range(count):
+                z_codes[n + j] = operand(words, scales, j, j + 1)
 
         def linear(n):
             banks, tag = (ps_o, "o") if n < TILES - 2 else (ps_f, "f")
@@ -451,47 +377,39 @@ def tile_kplanesgaussiananchordecoder_w4_kernel(
         result_sb = keep.tile([128, TILES, H], F32, name="result_sb")
         out_tiles = out.rearrange("(j p) h -> p j h", p=128)
 
-        def bias(n, lo=0, hi=H):
-            nc.vector.tensor_tensor(out=sums_b[:, n, lo:hi], in0=linear_out[n][:, lo:hi], in1=bias_row[:, lo:hi], op=ALU.add)
+        def bias(n):
+            nc.vector.tensor_tensor(out=sums_b[:, n, :], in0=linear_out[n][:], in1=bias_row[:], op=ALU.add)
 
         def cap(n, count):
-            part = slice(n, n + count)
-            if n in ABS:
-                nc.scalar.activation(out=result_sb[:, part, :], in_=sums_b[:, part, :], func=ACT.Abs)
-                return
-            (nc.gpsimd if n in POOL_CAPS else nc.vector).tensor_scalar(
-                out=result_sb[:, part, :], in0=sums_b[:, part, :], scalar1=CAP, scalar2=LOWEST, op0=ALU.min, op1=ALU.max
-            )
+            source, target = sums_b[:, n : n + count, :], result_sb[:, n : n + count, :]
+            if n == ABS_TILE:
+                nc.scalar.activation(out=target, in_=source, func=ACT.Abs)
+            else:
+                nc.vector.tensor_scalar(out=target, in0=source, scalar1=CAP, scalar2=LOWEST, op0=ALU.min, op1=ALU.max)
 
         def soft_exp(n, count):
-            part = slice(n, n + count)
-            nc.scalar.activation(
-                out=result_sb[:, part, :], in_=result_sb[:, part, :], func=ACT.Exp, scale=-1.0 if n in ABS else 1.0
-            )
+            part = result_sb[:, n : n + count, :]
+            nc.scalar.activation(out=part, in_=part, func=ACT.Exp, scale=-1.0 if n == ABS_TILE else 1.0)
 
-        def sigmoid(n, lo=0, hi=H):
-            nc.scalar.activation(out=result_sb[:, n, lo:hi], in_=sums_b[:, n, lo:hi], func=ACT.Sigmoid, scale=-1.0)
+        def sigmoid(n):
+            nc.scalar.activation(out=result_sb[:, n, :], in_=sums_b[:, n, :], func=ACT.Sigmoid, scale=-1.0)
 
         def logarithms(n, count):
             part = result_sb[:, n : n + count, :]
-            nc.scalar.activation(out=part, in_=part, func=ACT.Ln, bias=1.0 if n < HALF else TINY)
+            nc.scalar.activation(out=part, in_=part, func=ACT.Ln, bias=1.0)
 
         def logarithm(n, lo, hi):
             part = result_sb[:, n, lo:hi]
             nc.scalar.activation(out=part, in_=part, func=ACT.Ln, bias=TINY)
 
         def finish(n, lo, hi):
-            part = result_sb[:, n, lo:hi]
-            if n in ABS:
-                nc.vector.scalar_tensor_tensor(
-                    out=part, in0=sums_b[:, n, lo:hi], scalar=0.0, in1=part, op0=ALU.max, op1=ALU.add
-                )
+            part, y = result_sb[:, n, lo:hi], sums_b[:, n, lo:hi]
+            if n == ABS_TILE:
+                nc.vector.scalar_tensor_tensor(out=part, in0=y, scalar=0.0, in1=part, op0=ALU.max, op1=ALU.add)
             elif n < HALF:
-                nc.vector.tensor_tensor(out=part, in0=part, in1=sums_b[:, n, lo:hi], op=ALU.max)
+                nc.vector.tensor_tensor(out=part, in0=part, in1=y, op=ALU.max)
             else:
-                nc.vector.scalar_tensor_tensor(
-                    out=part, in0=part, scalar=-1.0, in1=sums_b[:, n, lo:hi], op0=ALU.mult, op1=ALU.max
-                )
+                nc.vector.scalar_tensor_tensor(out=part, in0=part, scalar=-1.0, in1=y, op0=ALU.mult, op1=ALU.max)
             nc.sync.dma_start(out=out_tiles[:, n, lo:hi], in_=part)
 
         def last_job(n):
@@ -503,14 +421,13 @@ def tile_kplanesgaussiananchordecoder_w4_kernel(
             if stage == interleave:
                 return [(widen, j) for j in (range(4) if i == 0 else range(4, 8))]
             if stage == subtract:
-                return [(quantise_feat, 0), (minimum, 0)]
+                return [(minimum, 0)]
             if stage == square:
-                same = [s for s in range(i // 8) if steps[s][1] == steps[i // 8][1]]
-                return [(distances, first_job[same[-3]] + steps[same[-3]][1] - 1)] if len(same) >= 3 else []
+                return [(distances, HALF * (i // 8 - 2) - 1)]
             if stage == distances:
                 return [(square, 8 * jobs[i][0] + j) for j in range(8)] + [(minimum, i - (6 if i < 8 else 2))]
             if stage == minimum:
-                return [(distances, i), (exponential, i - VALUES)]
+                return [(distances, i), (exponential, i - VALUE_BUFFERS)]
             if stage == exponential:
                 return [(minimum, i), (turn, i - EXPO_BUFFERS)]
             if stage == reciprocal:
@@ -518,7 +435,8 @@ def tile_kplanesgaussiananchordecoder_w4_kernel(
             if stage == pool_gain:
                 return [(exponential, i), (quantise_weights, i - 4)]
             if stage == normalise:
-                return [(reciprocal, i // 2)] + ([(pool_gain, i)] if by_words(i) else []) + [(quantise_weights, i - 2 if i == last - 1 and NORM_AFTER else -1)]
+                buffer = [(quantise_weights, i - 2)] if i == last - 1 else []
+                return [(reciprocal, i // 2)] + ([(pool_gain, i)] if by_words(i) else []) + buffer
             if stage == turn:
                 return [(normalise, i), (group, i - 2)]
             if stage == group:
@@ -530,23 +448,23 @@ def tile_kplanesgaussiananchordecoder_w4_kernel(
                 bank = (minimum, last) if i // 2 == pairs - 3 else (multiply, 2 * before)
                 return [(quantise_weights, i), bank, (quantise_feat, jobs[i][1])]
             if stage == multiply:
-                return [(products, i), (multiply, i - 4), (multiply, i - 4 + 1 - 2 * (i % 2))]
+                return [(products, i), (multiply, i - 4), (multiply, i - 3 - 2 * (i % 2))]
             if stage == quantise_z:
                 return [(multiply, last_job(i + j)) for j in range(rest[0])]
             if stage == linear:
-                return [(quantise_z, i), (bias, i - 2 if i < TILES - 2 else -1), (multiply, last - 2 if i >= TILES - 2 else -1)]
+                return [(quantise_z, i), (bias, i - 2) if i < TILES - 2 else (multiply, last - 2)]
             if stage == bias:
                 return [(linear, i)]
             if stage == cap:
                 return [(bias, i + j) for j in range(rest[0])]
             if stage == sigmoid:
-                return [(bias, i, *rest[:1])]
+                return [(bias, i)]
             if stage == soft_exp:
                 return [(cap, i + j) for j in range(rest[0])]
             if stage == logarithms:
                 return [(soft_exp, j) for j in range(HALF)]
             if stage == logarithm:
-                return [(sigmoid, TILES - 2)]
+                return [(sigmoid, i)]
             if stage == finish:
                 return [(logarithms, i) if i < HALF else (logarithm, i, rest[0])]
             return []
@@ -558,117 +476,88 @@ def tile_kplanesgaussiananchordecoder_w4_kernel(
                     while order and all(need in made or need[1] < 0 for need in needs(*order[0])):
                         stage, i, *rest = order.pop(0)
                         stage(i, *rest)
-                        several = stage in (quantise_weights, quantise_z, logarithms, cap, soft_exp) or (stage == quantise_feat and rest)
+                        several = stage in (quantise_weights, quantise_z, logarithms, cap, soft_exp)
                         made.update((stage, i + j) for j in range(rest[0] if several else 1))
-                        if stage in (logarithm, bias, sigmoid) and rest:
+                        if stage == logarithm:
                             made.add((stage, i, rest[0]))
                         moved = True
                 assert moved
 
-        def widen_gain(i):
-            (nc.vector if GAIN_ON == "vector" else nc.gpsimd).tensor_copy(out=channel_gain32[:], in_=channel_gain[:])
+        def each(stage, indices):
+            return [(stage, i) for i in indices]
 
         spread_points(0)
         spread_points(1)
-        vector, scalar, pool, tensor = [], [], [], []
-        squares_left = list(range(8 * len(steps)))
-
-        def more_squares(count):
-            scalar.extend((square, squares_left.pop(0)) for i in range(min(count, len(squares_left))))
+        vector = each(widen, (0, 2, 3)) + [(interleave, 0)] + each(widen, range(4, 8)) + [(quantise_feat, 0)]
+        vector += each(interleave, (1, 2)) + each(minimum, range(5))
+        vector += [(reciprocal, 0), (quantise_feat, 1), (normalise, 1), (normalise, 0), (quantise_feat, 2)]
+        vector += [(reciprocal, 1), (minimum, 5), (group, 1), (group, 0)]
+        scalar = [(widen, SCALAR_ROW)] + each(square, range(16)) + each(exponential, range(4))
+        scalar += each(square, range(16, 20)) + [(exponential, 4)] + each(square, (20, 21)) + [(exponential, 5), (square, 22)]
+        tensor = each(distances, range(6)) + [(turn, 1), (turn, 0), (distances, 6), (turn, 3), (turn, 2), (distances, 7)]
+        tensor += each(products, (0, 1))
+        pool = [(subtract, POOL_SQUARE), (square, POOL_SQUARE), (normalise, 3), (normalise, 2)]
+        squares_left = list(range(POOL_SQUARE + 1, 8 * len(steps)))
+        first_bias = 2 * 8 + 1
 
         def front(k):
             vector.append((minimum, k))
             scalar.append((exponential, k))
-            if k % 2 == 0 and k:
-                scalar.extend((normalise, j) for j in (k - 2, k - 1) if road(j) == DIAGONAL and not diagonal_on_pool(j) and j not in VECTOR_DIAG)
-            if k >= 4 and by_words(k - 4) and k - 4 not in COPY_VECTOR:
-                scalar.append((group, k - 4))
-            scalar.extend((multiply, j) for j in sorted(SCALAR_GAIN, reverse=True) if SCALAR_GAIN[j] == k)
-            more_squares(PACES.get(k, 2))
-            scalar.extend(parse(EXTRA_S.get(k, "")))
+            if k % 2 == 0:
+                scalar.extend(each(group, [j for j in (k - 4,) if by_words(j)]))
+                if k // 2 - 3 in emptied_by_scalar:
+                    scalar.extend(each(multiply, (k - 5, k - 6)))
+            scalar.extend((square, squares_left.pop(0)) for i in range(min(2, len(squares_left))))
             if k + 2 < JOBS:
                 tensor.append((distances, k + 2))
 
-        def gains(r):
-            vector.extend((group, k) for k in (2 * r + 1, 2 * r) if not by_words(k))
-
-        def multiplies(r):
-            return [(multiply, k) for k in (2 * r + 1, 2 * r) if k not in SCALAR_GAIN]
-
-        def close(n, count):
-            vector.append((quantise_z, n, count))
-
-        def biases(k):
-            if k in BIAS_AT:
-                n = BIAS_AT.index(k)
+        def next_bias(k):
+            n = k - first_bias
+            if 0 <= n < HALF:
                 vector.append((bias, n))
-                if n == 1:
-                    tensor.append((linear, 3))
-
-        names = dict(m=multiply, g=group, r=reciprocal, n=minimum, b=bias, e=exponential, d=normalise, s=sigmoid, t=turn, p=products, l=linear, x=soft_exp, c=cap, D=distances, W=widen, Q=square, G=pool_gain, w=widen_gain, S=subtract)
-
-        def parse(text):
-            out = []
-            for w in text.split():
-                i = [int(v) for v in w[1:].split(".")]
-                if w[0] == "q":
-                    out.append((quantise_weights, i[0], i[1]))
-                elif w[0] in "IU":
-                    out.append(({"I": interleave, "U": quantise_feat}[w[0]], *i))
-                elif w[0] == "z":
-                    out.append((quantise_z, i[0], i[1]))
-                elif w[0] in "cx":
-                    out.append(({"c": cap, "x": soft_exp}[w[0]], i[0], i[1]))
-                elif w[0] == "L":
-                    out.append((logarithms, i[0], i[1]))
-                elif w[0] in "fk" or len(i) > 1:
-                    lo, hi = (128 * i[1], 128 * i[2]) if len(i) > 1 else (0, H)
-                    out.append(({"f": finish, "k": logarithm, "b": bias, "s": sigmoid}[w[0]], i[0], lo, hi))
-                else:
-                    out.append((names[w[0]], i[0]))
-            return out
-
-        vector += parse(HV)
-        scalar += parse(HS)
-        tensor += parse(HT)
-        pool += parse(HG)
-        squares_left = [q for q in squares_left if (square, q) not in scalar + pool and q not in POOL_SQ]
+            if n == 1:
+                tensor.append((linear, 3))
 
         for r in range(3, pairs - 1):
             front(2 * r)
             if r == 3:
-                vector += parse(H3)
-            gains(r - 2)
+                vector += [(quantise_weights, 0, 2), (widen_gain, 0)]
+            vector += each(group, [k for k in (2 * r - 3, 2 * r - 4) if not by_words(k)])
             vector.append((reciprocal, r - 1))
-            biases(2 * r)
-            if r >= 1:
-                later = []
-                tensor += [(turn, k) for k in sorted((2 * r - 1, 2 * r - 2), key=by_words)] + later
+            next_bias(2 * r)
+            tensor += each(turn, (2 * r - 1, 2 * r - 2))
             front(2 * r + 1)
-            biases(2 * r + 1)
-            if r >= 3:
-                vector += multiplies(r - 3)[:1]
-            if 2 * r - 4 in COPY_VECTOR:
-                vector.append((group, 2 * r - 4))
-            if r >= 3:
-                vector += multiplies(r - 3)[1:]
-            if r >= 2:
-                vector.append((quantise_weights, 2 * r - 4, 2))
-                tensor += [(products, 2 * r - 4), (products, 2 * r - 3)]
-            if r >= 3 and jobs[2 * r - 6][1] == PLANES - 1:
+            next_bias(2 * r + 1)
+            if r - 3 not in emptied_by_scalar:
+                vector += each(multiply, (2 * r - 5, 2 * r - 6))
+            vector.append((quantise_weights, 2 * r - 4, 2))
+            tensor += each(products, (2 * r - 4, 2 * r - 3))
+            if jobs[2 * r - 6][1] == PLANES - 1:
                 n = jobs[2 * r - 6][2]
-                close(n, 2)
-                tensor += [(linear, n)] + ([(linear, 1)] if n == 0 else [])
-            vector += parse(EXTRA_V.get(r, ""))
+                vector.append((quantise_z, n, 2))
+                tensor += each(linear, (0, 1) if n == 0 else (n,))
+            if r == pairs - 3:
+                vector.append((cap, 1, 1))
+                scalar.append((cap, ABS_TILE, 1))
+            if r == pairs - 2:
+                vector.append((cap, 2, 2))
+                scalar += [(soft_exp, 0, 1), (soft_exp, 1, 1)]
 
-        vector += parse(DV)
-        scalar += parse(DS)
-        tensor += parse(DT)
+        e, f, c, d, a, b = range(JOBS - 6, JOBS)
+        vector += [(minimum, a), (reciprocal, pairs - 2), (group, f), (minimum, b)]
+        vector += [(multiply, e - 1), (quantise_weights, e, 2), (reciprocal, pairs - 1), (multiply, e - 2), (group, d)]
+        vector += [(multiply, f), (quantise_weights, c, 2), (multiply, e), (group, b)]
+        vector += [(multiply, c), (quantise_weights, b, 1), (multiply, d), (quantise_weights, a, 1)]
+        vector += [(quantise_z, 4, 2), (multiply, b), (multiply, a), (quantise_z, 7, 1), (bias, 4), (quantise_z, 6, 1)]
+        vector += each(bias, (5, 7, 6))
+        tensor += each(turn, (d, c)) + each(products, (e, f)) + [(turn, b)] + each(products, (c, d)) + [(turn, a)]
+        tensor += each(products, (b, a)) + each(linear, (4, 5, 7, 6))
+        parts = [(n, 0, H) for n in range(HALF, TILES - 1)] + [(TILES - 1, lo, lo + H // 2) for lo in (0, H // 2)]
+        vector += [(finish, n, 0, H) for n in range(HALF)] + [(finish, *part) for part in parts]
+        scalar += [(exponential, a), (group, e), (exponential, b), (soft_exp, 2, 2), (normalise, b), (group, c)]
+        scalar += [(logarithms, 0, 2), (group, a), (logarithms, 2, 2)]
+        scalar += each(sigmoid, (4, 5, 7, 6)) + [(logarithm, *part) for part in parts]
 
         for r in range(2, pairs):
-            both = (2 * r, 2 * r + 1)
-            pool += [(pool_gain, k) for k in both if by_words(k)]
-            pool += [(normalise, k) for k in both if diagonal_on_pool(k)]
-            pool += [(normalise, k) for k in both[::-1] if road(k) in (WORDS, POOL)]
-            pool += parse(EXTRA_G.get(r, ""))
+            pool += [(pool_gain, 2 * r)] + each(normalise, [k for k in (2 * r + 1, 2 * r) if k != last])
         issue([vector, scalar, pool, tensor])

from contextlib import ExitStack

import concourse.mybir as mybir
from concourse.masks import make_identity

F32 = mybir.dt.float32
BF16 = mybir.dt.bfloat16
U32 = mybir.dt.uint32
I32 = mybir.dt.int32
U8 = mybir.dt.uint8
FP8 = mybir.dt.float8_e4m3fn
FP8X4 = mybir.dt.float8_e4m3fn_x4
FP4X4 = mybir.dt.float4_e2m1fn_x4
ACT = mybir.ActivationFunctionType
ALU = mybir.AluOpType

N, PLANES, M, C, H = 1024, 3, 512, 512, 512
FLOPS = 2 * N * M * C * PLANES + 2 * N * C * H
WIDTH2 = 0.0018
COORDS = ((0, 1), (0, 2), (1, 2))
TILES = N // 128
JOBS = TILES * PLANES
TINY = 2.0**-60

CAP = 40.0
LOWEST = -3.0e38

HALF = TILES // 2
SCALAR_ROW = 1
POOL_SQUARE = 8 * 3 - 1
CLOCK_JOB, CLOCK_BLOCKS = 5, 3
ABS_TILE = 0
EXPO_BUFFERS = 10
VALUE_BUFFERS = 6
VECTOR, POOL, WORDS, DIAGONAL = "vector", "pool", "words", "diagonal"


def tile_kplanesgaussiananchordecoder_w4_kernel(
    tc, pts, cen, ga, feat_bytes, feat_scale, gc, w1_words, w1_scales, b1, out
):
    nc = tc.nc
    with ExitStack() as ctx:
        keep = ctx.enter_context(tc.tile_pool(name="keep", bufs=1))
        work = ctx.enter_context(tc.tile_pool(name="work", bufs=2))
        ps_d2 = ctx.enter_context(tc.psum_pool(name="ps_d2", bufs=2))
        ps_xt = ctx.enter_context(tc.psum_pool(name="ps_xt", bufs=2))
        ps_f = ctx.enter_context(tc.psum_pool(name="ps_f", bufs=2))
        ps_o = ctx.enter_context(tc.psum_pool(name="ps_o", bufs=2))
        ctx.enter_context(tc.manual_schedule())

        head_points = keep.tile([128, HALF * 3], BF16, name="head_points")
        nc.scalar.dma_start(out=head_points[:], in_=pts[0 : 128 * HALF, :].rearrange("(p j) x -> p (j x)", j=HALF))
        scale_sb = keep.tile([128, 4], F32, name="scale_sb")
        nc.sync.dma_start(out=scale_sb[:], in_=feat_scale.rearrange("o (p t) x -> p (o t x)", t=4))
        first_bytes = keep.tile([128, 4, C], U8, name="first_bytes")
        later_bytes = keep.tile([128, 4, 2, C], U8, name="later_bytes")

        def load_feat(pl, lo, hi):
            rows = feat_bytes[pl].rearrange("(p t) c -> p t c", t=4)
            target = first_bytes[:, lo:hi, :] if pl == 0 else later_bytes[:, lo:hi, pl - 1, :]
            nc.sync.dma_start(out=target, in_=rows[:, lo:hi, :])

        centre_rows = cen.rearrange("x (p t) axis -> p x (t axis)", t=4)
        first_centres = keep.tile([128, 8], BF16, name="first_centres")
        nc.scalar.dma_start(out=first_centres[:], in_=centre_rows[:, 0, :])
        load_feat(0, 0, 2)
        load_feat(0, 2, 4)
        load_feat(1, 0, 4)
        load_feat(2, 0, 4)
        half = N // 2
        points = [keep.tile([128, half, 3], BF16, name="points%d" % h) for h in range(2)]

        def load_points(h):
            nc.sync.dma_start(
                out=points[h][:].rearrange("p n x -> p (n x)"),
                in_=pts[h * half : (h + 1) * half, :].rearrange("n x -> (n x)").partition_broadcast(128),
            )

        load_points(0)
        later_centres = keep.tile([128, PLANES - 1, 8], BF16, name="later_centres")
        nc.sync.dma_start(out=later_centres[:], in_=centre_rows[:, 1:PLANES, :])
        centres = [first_centres[:]] + [later_centres[:, i, :] for i in range(PLANES - 1)]
        gain_rows = keep.tile([128, PLANES, 4], BF16, name="gain_rows")
        nc.sync.dma_start(out=gain_rows[:], in_=ga.rearrange("x (p t) -> p x t", t=4))
        gain_all = keep.tile([128, PLANES, M], BF16, name="gain_all")
        nc.sync.dma_start(
            out=gain_all[:].rearrange("n x m -> n (x m)"), in_=ga.rearrange("x m -> (x m)").partition_broadcast(128)
        )
        load_points(1)
        channel_gain = keep.tile([128, 4], BF16, name="channel_gain")
        nc.sync.dma_start(out=channel_gain[:], in_=gc.rearrange("(p t) -> p t", t=4))
        channel_gain32 = keep.tile([128, 4], F32, name="channel_gain32")
        w_words = keep.tile([128, 2 * H], U8, name="w_words", align_bytes=64)
        nc.sync.dma_start(out=w_words[:], in_=w1_words[0])
        w_scales = keep.tile([128, H], U8, name="w_scales", align_bytes=64)
        nc.vector.memset(w_scales[:].bitcast(I32), 0)
        for quad in range(4):
            rows = w1_scales[0, 4 * quad : 4 * quad + 4, :]
            nc.sync.dma_start(out=w_scales[32 * quad : 32 * quad + 4, :].bitcast(I32), in_=rows.bitcast(I32))
        bias_row = keep.tile([128, H], BF16, name="bias_row")
        nc.sync.dma_start(out=bias_row[:], in_=b1.partition_broadcast(128))

        ident_bf = keep.tile([128, 128], BF16, name="ident_bf")
        make_identity(nc, ident_bf[:])
        ident = keep.tile([128, 128], F32, name="ident")
        nc.scalar.activation(out=ident[:], in_=ident_bf[:], func=ACT.Copy)

        steps = [(first, pl) for first in (0, HALF) for pl in range(PLANES)]
        jobs = [(s, pl, first + i) for s, (first, pl) in enumerate(steps) for i in range(HALF)]

        head_coords = []

        def spread_points(x):
            bank = ps_o.tile([128, HALF, 128], BF16, name="head_bank", tag="o")
            for j in range(HALF):
                column = head_points[:, 3 * j + x : 3 * j + x + 1]
                nc.tensor.transpose(bank[:, j, :], column.to_broadcast([128, 128]), ident_bf[:])
            head_coords.append(bank[:].rearrange("p j n -> p n j"))

        feat_words = keep.tile([128, PLANES, C], U32, name="feat_words", align_bytes=64)
        feat_scales = keep.tile([128, PLANES, C], U8, name="feat_scales", align_bytes=64)

        first_wide = keep.tile([128, 4, C], BF16, name="first_wide")
        later_wide = keep.tile([128, 2, 2 * C, 2], BF16, name="later_wide")
        later_words = later_wide[:].rearrange("p u c e -> p u (c e)").bitcast(F32)
        side_by_side = keep.tile([128, PLANES, 4 * C], BF16, name="side_by_side", align_bytes=64)

        def widen(j):
            t = j % 4
            source = first_bytes[:, t, :] if j < 4 else later_bytes[:, t].rearrange("p x c -> p (x c)")
            target = first_wide[:, t, :] if j < 4 else later_wide[:, t // 2, :, t % 2]
            if j == SCALAR_ROW:
                nc.scalar.activation(out=target, in_=source.bitcast(FP8), func=ACT.Copy, scale=scale_sb[:, t : t + 1])
            else:
                nc.vector.tensor_scalar(
                    out=target, in0=source.bitcast(FP8), scalar1=scale_sb[:, t : t + 1], scalar2=None, op0=ALU.mult
                )

        def interleave(pl):
            if pl == 0:
                target = side_by_side[:, pl].rearrange("p (t m i j) -> p m j i t", t=4, i=2, j=4)
                source = first_wide[:].rearrange("p j (m i t) -> p m j i t", i=2, t=4)
            else:
                target = side_by_side[:, pl].bitcast(F32).rearrange("p (t m i u) -> p m u i t", t=4, i=2, u=2)
                source = later_words[:, :, C * (pl - 1) : C * pl].rearrange("p u (m i t) -> p m u i t", i=2, t=4)
            nc.vector.tensor_copy(out=target, in_=source)

        def quantise_feat(pl):
            nc.vector.quantize_mx(out=feat_words[:, pl].bitcast(FP8X4), scales=feat_scales[:, pl], in_=side_by_side[:, pl])

        def widen_gain(i):
            nc.vector.tensor_copy(out=channel_gain32[:], in_=channel_gain[:])

        squared, distance, scaled, expo, sums, recips, gained, weights = ({} for i in range(8))
        turned, grouped, codes, feature, partial, z_pair, z_codes, linear_out = ({} for i in range(8))
        diagonal, pair_codes, pair_blocks = {}, {}, {}
        pairs = JOBS // 2
        last = JOBS - 1
        emptied_by_scalar = (pairs // 2, pairs // 2 + 1)

        def road(k):
            if k % 2:
                return DIAGONAL
            return {0: VECTOR, 2: POOL}.get(k, WORDS)

        def by_words(k):
            return road(k) == WORDS

        def normaliser(k):
            return nc.vector if k < 2 else nc.scalar if k == last else nc.gpsimd

        def square_operands(q):
            step, within = divmod(q, 8)
            t, axis = divmod(within, 2)
            first, pl = steps[step]
            coordinate = head_coords[axis] if step == 0 else points[first // HALF][:, :, COORDS[pl][axis]]
            return step, t, axis, coordinate, centres[pl][:, 2 * t + axis : 2 * t + axis + 1]

        differences = later_words[:, 0, C : 2 * C]

        def subtract(q):
            step, t, axis, coordinate, centre = square_operands(q)
            nc.gpsimd.tensor_scalar(
                out=differences, in0=coordinate, scalar1=-1.0, scalar2=centre, op0=ALU.mult, op1=ALU.add
            )

        def square(q):
            step, t, axis, coordinate, centre = square_operands(q)
            if step not in squared:
                squared[step] = work.tile([128, 2, 4, half], F32, name="squared", bufs=3)
            target = squared[step][:, axis, t, :]
            if step == 0:
                target = target.rearrange("p (n j) -> p n j", j=HALF)
            if q == POOL_SQUARE:
                nc.gpsimd.tensor_tensor(out=target, in0=differences, in1=differences, op=ALU.mult)
            else:
                nc.scalar.activation(out=target, in_=coordinate, func=ACT.Square, scale=-1.0, bias=centre)

        def distances(k):
            step, pl, n = jobs[k]
            i = n - steps[step][0]
            banks, tag = {1: (ps_f, "f"), 2: (ps_o, "o")}.get(k // 2, (ps_d2, "d2"))
            distance[k] = banks.tile([128, 4, 128], F32, name="d2", tag=tag)
            for t in range(4):
                for axis in range(2):
                    nc.tensor.matmul(
                        out=distance[k][:, t, :],
                        lhsT=squared[step][:, axis, t, 128 * i : 128 * i + 128],
                        rhs=ident[:],
                        start=(axis == 0),
                        stop=(axis == 1),
                        is_transpose=not (axis == 0 and k == CLOCK_JOB and t < CLOCK_BLOCKS),
                    )

        def minimum(k):
            values = work.tile([128, M], F32, name="values", bufs=VALUE_BUFFERS)
            least = work.tile([128, 1], F32, name="least", bufs=VALUE_BUFFERS)
            target, source = values[:], distance[k][:].rearrange("n t p -> n (t p)")
            if by_words(k):
                target = values[:].rearrange("n (p t) -> n p t", t=4)
                source = distance[k][:].rearrange("n t p -> n p t")
            nc.vector.tensor_scalar(
                out=target, in0=source, scalar1=1.0 / WIDTH2, scalar2=None, op0=ALU.mult, op1=ALU.min, accum_out=least[:]
            )
            scaled[k] = (values, least)

        def exponential(k):
            values, least = scaled[k]
            expo[k] = work.tile([128, M], F32, name="expo", bufs=EXPO_BUFFERS)
            if k % 2 == 0:
                sums[k // 2] = work.tile([128, 2], F32, name="sums", bufs=3)
            nc.scalar.activation(
                out=expo[k][:],
                in_=values[:],
                func=ACT.Exp,
                scale=-1.0,
                bias=least[:],
                accum_out=sums[k // 2][:, k % 2 : k % 2 + 1],
            )

        def reciprocal(r):
            recips[r] = work.tile([128, 2], F32, name="recips", bufs=3)
            nc.vector.reciprocal(out=recips[r][:], in_=sums[r][:])

        def pool_gain(k):
            gained[k] = grouped[k // 2 - 2][:].rearrange("p j n t -> p (j n t)").bitcast(F32)
            nc.gpsimd.tensor_tensor(out=gained[k], in0=expo[k][:], in1=gain_all[:, jobs[k][1], :], op=ALU.mult)

        def normalise(k):
            source = target = expo[k][:]
            factor = recips[k // 2][:, k % 2 : k % 2 + 1]
            if road(k) == WORDS:
                if k == last - 1:
                    weights[k] = grouped[k // 2 - 1][:, 0].rearrange("p n t -> p (n t)")
                else:
                    weights[k] = work.tile([128, M], BF16, name="weights", bufs=4)
                source = gained[k].rearrange("n (p u e) -> n u p e", u=2, e=2)
                target = weights[k][:].rearrange("n (u p e) -> n u p e", u=2, e=2)
            if road(k) == DIAGONAL:
                diagonal[k] = work.tile([128, 128], F32, name="diagonal")
                source, target = ident[:], diagonal[k][:]
            if normaliser(k) is nc.vector:
                nc.vector.tensor_scalar(out=target, in0=source, scalar1=factor, scalar2=None, op0=ALU.mult)
            elif normaliser(k) is nc.scalar:
                nc.scalar.activation(out=target, in_=source, func=ACT.Copy, scale=factor)
            else:
                nc.gpsimd.tensor_scalar(out=target, in0=source, scalar1=factor, scalar2=1.0, op0=ALU.mult, op1=ALU.mult)

        def turn(k):
            blocks = 2 if by_words(k) else 4
            source = weights[k][:].bitcast(F32) if by_words(k) else expo[k][:]
            turned[k] = ps_xt.tile([128, blocks, 128], F32, name="turned", tag="xt")
            for t in range(blocks):
                block = source[:, 128 * t : 128 * t + 128]
                if road(k) == DIAGONAL:
                    nc.tensor.matmul(out=turned[k][:, t, :], lhsT=block, rhs=diagonal[k][:], start=True, stop=True)
                else:
                    nc.tensor.transpose(turned[k][:, t, :], block, ident[:])

        def group(k):
            if k // 2 not in grouped:
                grouped[k // 2] = work.tile([128, 2, 128, 4], BF16, name="grouped", align_bytes=64, bufs=7)
            target = grouped[k // 2][:, k % 2]
            if by_words(k):
                nc.scalar.copy(out=target.bitcast(F32), in_=turned[k][:].rearrange("p u n -> p n u"))
            else:
                nc.vector.tensor_tensor(
                    out=target,
                    in0=turned[k][:].rearrange("p t n -> p n t"),
                    in1=gain_rows[:, jobs[k][1], :].unsqueeze(1).to_broadcast([128, 128, 4]),
                    op=ALU.mult,
                )

        def quantise(source, count, name):
            words = work.tile([128, 128 * count], U32, name=name + "_words", tag=name + "_words", align_bytes=64, bufs=3)
            scales = work.tile([128, 128 * count], U8, name=name + "_scales", tag=name + "_scales", align_bytes=64, bufs=3)
            flat = source.rearrange("p j n t -> p (j n t)")
            nc.vector.quantize_mx(out=words[:].bitcast(FP8X4), scales=scales[:], in_=flat)
            return words, scales

        def operand(words, scales, lo, hi):
            return words[:, 128 * lo : 128 * hi].bitcast(FP8X4), scales[:, 128 * lo : 128 * hi]

        def quantise_weights(k, count):
            words, scales = quantise(grouped[k // 2][:, k % 2 : k % 2 + count], count, "a")
            pair_codes[k // 2] = operand(words, scales, 0, count)
            for j in range(count):
                codes[k + j] = operand(words, scales, j, j + 1)

        def products(k):
            pl = jobs[k][1]
            wide = k // 2 in emptied_by_scalar
            blocks = range(2 * (k % 2), 2 * (k % 2) + 2) if wide else range(4)
            moving = pair_codes[k // 2] if wide else codes[k]
            banks, tag = (ps_d2, "d2") if k // 2 in (pairs - 3, pairs - 1) else (ps_f, "f")
            feature[k] = banks.tile([128, len(blocks), 512 // len(blocks)], F32, name="feature", tag=tag)
            for i, t in enumerate(blocks):
                nc.tensor.matmul_mx(
                    out=feature[k][:, i, :],
                    lhsT=feat_words[:, pl, 128 * t : 128 * t + 128].bitcast(FP8X4),
                    lhsT_scale=feat_scales[:, pl, 128 * t : 128 * t + 128],
                    rhs=moving[0],
                    rhs_scale=moving[1],
                    start=True,
                    stop=True,
                )

        def empty(k):
            n = jobs[k][2]
            if k // 2 not in pair_blocks:
                pair_blocks[k // 2] = keep.tile([128, 4, 256], F32, name="blocks%d" % (k // 2))
                for j in range(2):
                    part = pair_blocks[k // 2][:, :, 128 * j : 128 * j + 128]
                    partial[n - k % 2 + j] = part.rearrange("p t n -> p n t")
            for i in range(2):
                t = 2 * (k % 2) + i
                nc.scalar.activation(
                    out=pair_blocks[k // 2][:, t, :],
                    in_=feature[k][:, i, :],
                    func=ACT.Copy,
                    scale=channel_gain32[:, t : t + 1],
                )

        def multiply(k):
            if k // 2 in emptied_by_scalar:
                return empty(k)
            step, pl, n = jobs[k]
            other = channel_gain[:].unsqueeze(1).to_broadcast([128, 128, 4]) if pl == 0 else partial[n]
            if pl < PLANES - 1:
                result = work.tile([128, 128, 4], F32, name="partial", bufs=7)[:]
                partial[n] = result
            else:
                if n // 2 not in z_pair:
                    z_pair[n // 2] = work.tile([128, 2, 128, 4], BF16, name="z_pair", align_bytes=64)
                result = z_pair[n // 2][:, n % 2]
            nc.vector.tensor_tensor(out=result, in0=feature[k][:].rearrange("p t n -> p n t"), in1=other, op=ALU.mult)

        def quantise_z(n, count):
            words, scales = quantise(z_pair[n // 2][:, n % 2 : n % 2 + count], count, "z")
            for j in range(count):
                z_codes[n + j] = operand(words, scales, j, j + 1)

        def linear(n):
            banks, tag = (ps_o, "o") if n < TILES - 2 else (ps_f, "f")
            linear_out[n] = banks.tile([128, H], F32, name="linear_out", tag=tag)
            nc.tensor.matmul_mx(
                out=linear_out[n][:],
                lhsT=z_codes[n][0],
                lhsT_scale=z_codes[n][1],
                rhs=w_words[:].bitcast(FP4X4),
                rhs_scale=w_scales[:],
                start=True,
                stop=True,
            )

        sums_b = keep.tile([128, TILES, H], F32, name="sums_b")
        result_sb = keep.tile([128, TILES, H], F32, name="result_sb")
        out_tiles = out.rearrange("(j p) h -> p j h", p=128)

        def bias(n):
            nc.vector.tensor_tensor(out=sums_b[:, n, :], in0=linear_out[n][:], in1=bias_row[:], op=ALU.add)

        def cap(n, count):
            source, target = sums_b[:, n : n + count, :], result_sb[:, n : n + count, :]
            if n == ABS_TILE:
                nc.scalar.activation(out=target, in_=source, func=ACT.Abs)
            else:
                nc.vector.tensor_scalar(out=target, in0=source, scalar1=CAP, scalar2=LOWEST, op0=ALU.min, op1=ALU.max)

        def soft_exp(n, count):
            part = result_sb[:, n : n + count, :]
            nc.scalar.activation(out=part, in_=part, func=ACT.Exp, scale=-1.0 if n == ABS_TILE else 1.0)

        def sigmoid(n):
            nc.scalar.activation(out=result_sb[:, n, :], in_=sums_b[:, n, :], func=ACT.Sigmoid, scale=-1.0)

        def logarithms(n, count):
            part = result_sb[:, n : n + count, :]
            nc.scalar.activation(out=part, in_=part, func=ACT.Ln, bias=1.0)

        def logarithm(n, lo, hi):
            part = result_sb[:, n, lo:hi]
            nc.scalar.activation(out=part, in_=part, func=ACT.Ln, bias=TINY)

        def finish(n, lo, hi):
            part, y = result_sb[:, n, lo:hi], sums_b[:, n, lo:hi]
            if n == ABS_TILE:
                nc.vector.scalar_tensor_tensor(out=part, in0=y, scalar=0.0, in1=part, op0=ALU.max, op1=ALU.add)
            elif n < HALF:
                nc.vector.tensor_tensor(out=part, in0=part, in1=y, op=ALU.max)
            else:
                nc.vector.scalar_tensor_tensor(out=part, in0=part, scalar=-1.0, in1=y, op0=ALU.mult, op1=ALU.max)
            nc.sync.dma_start(out=out_tiles[:, n, lo:hi], in_=part)

        def last_job(n):
            return [k for k in range(JOBS) if jobs[k][1:] == (PLANES - 1, n)][0]

        made = set()

        def needs(stage, i, *rest):
            if stage == interleave:
                return [(widen, j) for j in (range(4) if i == 0 else range(4, 8))]
            if stage == subtract:
                return [(minimum, 0)]
            if stage == square:
                return [(distances, HALF * (i // 8 - 2) - 1)]
            if stage == distances:
                return [(square, 8 * jobs[i][0] + j) for j in range(8)] + [(minimum, i - (6 if i < 8 else 2))]
            if stage == minimum:
                return [(distances, i), (exponential, i - VALUE_BUFFERS)]
            if stage == exponential:
                return [(minimum, i), (turn, i - EXPO_BUFFERS)]
            if stage == reciprocal:
                return [(exponential, 2 * i + 1)]
            if stage == pool_gain:
                return [(exponential, i), (quantise_weights, i - 4)]
            if stage == normalise:
                buffer = [(quantise_weights, i - 2)] if i == last - 1 else []
                return [(reciprocal, i // 2)] + ([(pool_gain, i)] if by_words(i) else []) + buffer
            if stage == turn:
                return [(normalise, i), (group, i - 2)]
            if stage == group:
                return [(turn, i)]
            if stage == quantise_weights:
                return [(group, i + j) for j in range(rest[0])]
            if stage == products:
                before = i // 2 - (2 if i // 2 >= pairs - 2 else 1)
                bank = (minimum, last) if i // 2 == pairs - 3 else (multiply, 2 * before)
                return [(quantise_weights, i), bank, (quantise_feat, jobs[i][1])]
            if stage == multiply:
                return [(products, i), (multiply, i - 4), (multiply, i - 3 - 2 * (i % 2))]
            if stage == quantise_z:
                return [(multiply, last_job(i + j)) for j in range(rest[0])]
            if stage == linear:
                return [(quantise_z, i), (bias, i - 2) if i < TILES - 2 else (multiply, last - 2)]
            if stage == bias:
                return [(linear, i)]
            if stage == cap:
                return [(bias, i + j) for j in range(rest[0])]
            if stage == sigmoid:
                return [(bias, i)]
            if stage == soft_exp:
                return [(cap, i + j) for j in range(rest[0])]
            if stage == logarithms:
                return [(soft_exp, j) for j in range(HALF)]
            if stage == logarithm:
                return [(sigmoid, i)]
            if stage == finish:
                return [(logarithms, i) if i < HALF else (logarithm, i, rest[0])]
            return []

        def issue(orders):
            while any(orders):
                moved = False
                for order in orders:
                    while order and all(need in made or need[1] < 0 for need in needs(*order[0])):
                        stage, i, *rest = order.pop(0)
                        stage(i, *rest)
                        several = stage in (quantise_weights, quantise_z, logarithms, cap, soft_exp)
                        made.update((stage, i + j) for j in range(rest[0] if several else 1))
                        if stage == logarithm:
                            made.add((stage, i, rest[0]))
                        moved = True
                assert moved

        def each(stage, indices):
            return [(stage, i) for i in indices]

        spread_points(0)
        spread_points(1)
        vector = each(widen, (0, 2, 3)) + [(interleave, 0)] + each(widen, range(4, 8)) + [(quantise_feat, 0)]
        vector += each(interleave, (1, 2)) + each(minimum, range(5))
        vector += [(reciprocal, 0), (quantise_feat, 1), (normalise, 1), (normalise, 0), (quantise_feat, 2)]
        vector += [(reciprocal, 1), (minimum, 5), (group, 1), (group, 0)]
        scalar = [(widen, SCALAR_ROW)] + each(square, range(16)) + each(exponential, range(4))
        scalar += each(square, range(16, 20)) + [(exponential, 4)] + each(square, (20, 21)) + [(exponential, 5), (square, 22)]
        tensor = each(distances, range(6)) + [(turn, 1), (turn, 0), (distances, 6), (turn, 3), (turn, 2), (distances, 7)]
        tensor += each(products, (0, 1))
        pool = [(subtract, POOL_SQUARE), (square, POOL_SQUARE), (normalise, 3), (normalise, 2)]
        squares_left = list(range(POOL_SQUARE + 1, 8 * len(steps)))
        first_bias = 2 * 8 + 1

        def front(k):
            vector.append((minimum, k))
            scalar.append((exponential, k))
            if k % 2 == 0:
                scalar.extend(each(group, [j for j in (k - 4,) if by_words(j)]))
                if k // 2 - 3 in emptied_by_scalar:
                    scalar.extend(each(multiply, (k - 5, k - 6)))
            scalar.extend((square, squares_left.pop(0)) for i in range(min(2, len(squares_left))))
            if k + 2 < JOBS:
                tensor.append((distances, k + 2))

        def next_bias(k):
            n = k - first_bias
            if 0 <= n < HALF:
                vector.append((bias, n))
            if n == 1:
                tensor.append((linear, 3))

        for r in range(3, pairs - 1):
            front(2 * r)
            if r == 3:
                vector += [(quantise_weights, 0, 2), (widen_gain, 0)]
            vector += each(group, [k for k in (2 * r - 3, 2 * r - 4) if not by_words(k)])
            vector.append((reciprocal, r - 1))
            next_bias(2 * r)
            tensor += each(turn, (2 * r - 1, 2 * r - 2))
            front(2 * r + 1)
            next_bias(2 * r + 1)
            if r - 3 not in emptied_by_scalar:
                vector += each(multiply, (2 * r - 5, 2 * r - 6))
            vector.append((quantise_weights, 2 * r - 4, 2))
            tensor += each(products, (2 * r - 4, 2 * r - 3))
            if jobs[2 * r - 6][1] == PLANES - 1:
                n = jobs[2 * r - 6][2]
                vector.append((quantise_z, n, 2))
                tensor += each(linear, (0, 1) if n == 0 else (n,))
            if r == pairs - 3:
                vector.append((cap, 1, 1))
                scalar.append((cap, ABS_TILE, 1))
            if r == pairs - 2:
                vector.append((cap, 2, 2))
                scalar += [(soft_exp, 0, 1), (soft_exp, 1, 1)]

        e, f, c, d, a, b = range(JOBS - 6, JOBS)
        vector += [(minimum, a), (reciprocal, pairs - 2), (group, f), (minimum, b)]
        vector += [(multiply, e - 1), (quantise_weights, e, 2), (reciprocal, pairs - 1), (multiply, e - 2), (group, d)]
        vector += [(multiply, f), (quantise_weights, c, 2), (multiply, e), (group, b)]
        vector += [(multiply, c), (quantise_weights, b, 1), (multiply, d), (quantise_weights, a, 1)]
        vector += [(quantise_z, 4, 2), (multiply, b), (multiply, a), (quantise_z, 7, 1), (bias, 4), (quantise_z, 6, 1)]
        vector += each(bias, (5, 7, 6))
        tensor += each(turn, (d, c)) + each(products, (e, f)) + [(turn, b)] + each(products, (c, d)) + [(turn, a)]
        tensor += each(products, (b, a)) + each(linear, (4, 5, 7, 6))
        parts = [(n, 0, H) for n in range(HALF, TILES - 1)] + [(TILES - 1, lo, lo + H // 2) for lo in (0, H // 2)]
        vector += [(finish, n, 0, H) for n in range(HALF)] + [(finish, *part) for part in parts]
        scalar += [(exponential, a), (group, e), (exponential, b), (soft_exp, 2, 2), (normalise, b), (group, c)]
        scalar += [(logarithms, 0, 2), (group, a), (logarithms, 2, 2)]
        scalar += each(sigmoid, (4, 5, 7, 6)) + [(logarithm, *part) for part in parts]

        for r in range(2, pairs):
            pool += [(pool_gain, 2 * r)] + each(normalise, [k for k in (2 * r + 1, 2 * r) if k != last])
        issue([vector, scalar, pool, tensor])
